import numpy as np, ml_dtypes
CORES = [78,86,94,102,110,118]
N = 6
BF = ml_dtypes.bfloat16
def gentries(a):
    return np.ascontiguousarray(a.reshape(8, 16, -1).transpose(0, 2, 1)).reshape(8, -1)
def gtable(e):
    e = np.asarray(e); return np.ascontiguousarray(e.reshape(8, -1, 16).transpose(0, 2, 1)).reshape(128, -1).astype(np.int32)
V, RO, VO, GS = 3072, 2, 11, 3
def mix(rng, p):
    return [p[i] for i in rng.permutation(len(p))]
def invol(rng, n):
    o = rng.permutation(V); t = np.arange(V); t[o[n::2]] = o[n + 1::2]; t[o[n + 1::2]] = o[n::2]
    return t
def sew(parts, line):
    t = np.arange(V); s = np.arange(V); at = 0
    for n, kind in parts:
        w = line[at:at + n]; at += n
        if n == 1: continue
        two = (t, s) if kind == 1 else (s, t)
        for q in (0, 1):
            e = w[q:]; m = len(e) // 2 * 2; a = e[0:m:2]; b = e[1:m:2]
            two[q][a] = b; two[q][b] = a
        if kind == 2: t[w[0]] = w[n - 1]; t[w[n - 1]] = w[0]
    return t, s
def tie(rng, s, goal, straight):
    v = np.arange(V); u = np.empty(V, np.int64); a = v[s > v]; z = v[goal > v]
    u[rng.permutation(v[s == v])] = v[goal == v]
    if straight: z = goal[z]
    else: a = rng.permutation(a); z = np.where(rng.random(len(z)) < 0.5, z, goal[z])
    u[a] = z; u[s[a]] = goal[z]
    return u
def grow(rng, parts, lines, straight=False):
    b = [sew(parts[r], lines[r]) for r in range(N)]; t = np.stack([y[0] for y in b])
    return t, np.stack([tie(rng, b[r][1], t[(r + 1) % N], straight) for r in range(N)])
def cut(rng, n, top, ring):
    out = []; left = V
    for i in range(n // 2):
        if rng.random() < 0.5: z = 2 * rng.integers(0, top // 2, 2) + 1; y = rng.integers(0, 2, 2)
        else: z = 2 * rng.integers(1, top // 2 + 1, 2); y = (0, 1)
        out += [(int(z[0]), int(y[0])), (int(z[1]), int(y[1]))]; left -= int(z[0] + z[1])
    while left > 0:
        m = min(left, 2 * int(rng.integers(1, ring + 1))); out.append((m, 2)); left -= m
    return mix(rng, out)
CUTS = ((64, 16, 10), (128, 8, 6), (16, 64, 40), (4, 256, 150))
def base(rng):
    t = np.empty((N, 8, V), np.int64); u = np.empty((N, 8, V), np.int64); o = rng.permutation(8)
    for q in range(8):
        g = o[q]
        if q < 4:
            for r in range(N):
                n = int(rng.choice(np.array([0, 2]))) if q == 0 else 2 * int(rng.choice(np.array([0, 1, V // 64, V // 32, V // 16, V // 8, V // 4])))
                t[r, g] = invol(rng, n); u[r, g] = rng.permutation(V)
        else:
            n, top, ring = CUTS[q - 4]
            t[:, g], u[:, g] = grow(rng, [cut(rng, n, top, ring) for r in range(N)], [rng.permutation(V) for r in range(N)])
    return t, u
def hang(rng):
    n = np.array([VO, VO - 1, 16, 0, VO, VO - 1, 15, VO + 1])[(np.arange(8)[None, :] + np.arange(N)[:, None] + rng.integers(0, 8)) % 8][:, :, None, None]
    ok = np.argsort(rng.random((N, 8, 16, 1)), axis=2) < n
    th = rng.choice(np.array([0, 1, 7, 100, 253, 254]), (N, 8, 16, 1)); gap = th + 1 - ok.astype(np.int64)
    low = np.floor(rng.random((N, 8, 16, 1)) * (256 - gap)).astype(np.int64); share = rng.choice(np.array([0.004, 0.03, 0.2, 0.5]), (N, 8, 1, 1))
    hi = (rng.random((N, 8, 1, V)) < share) & (rng.random((N, 8, 16, V)) < 0.75)
    return low + gap * hi, th
def pack(t, u, x, th):
    return {"t0": np.stack([gtable(a) for a in t]), "u0": np.stack([gtable(a) for a in u]),
            "x": np.ascontiguousarray(x.reshape(N, 128, V)).astype(np.float32).astype(BF), "th": np.ascontiguousarray(th.reshape(N, 128, 1)).astype(np.int32)}
def setup_inputs(rng):
    t, u = base(rng)
    th = rng.integers(8, 120, (N, 8, 16, 1)); low = np.floor(rng.random((N, 8, 16, 1)) * (256 - th)).astype(np.int64)
    x = low + np.floor(rng.random((N, 8, 16, V)) * (th + 1)).astype(np.int64)
    share = rng.choice(np.array([0.004, 0.015, 0.04, 0.12]), (N, 8, 1, 1))
    m = (rng.random((N, 8, 1, V)) < share) & (rng.random((N, 8, 16, V)) < rng.random((N, 8, 1, V)))
    return pack(t, u, np.where(m, rng.integers(0, 256, m.shape), x), th)
def setup_inputs_spread(rng):
    t, u = base(rng)
    th = np.floor(np.exp2(8 * rng.random((N, 8, 16, 1)))).astype(np.int64) - (rng.random((N, 8, 16, 1)) < 0.25)
    e = rng.choice(np.array([1.0, 3.0, 8.0]), (N, 8, 1, 1))
    x = np.floor(np.exp2(8 * rng.random((N, 8, 1, V)) ** e) * rng.random((N, 8, 16, V))).astype(np.int64)
    return pack(t, u, x, th)
def setup_inputs_ends(rng):
    zig = np.empty(V, np.int64); zig[0::2] = np.arange(V // 2); zig[1::2] = V - 1 - np.arange(V // 2)
    t = np.empty((N, 8, V), np.int64); u = np.empty((N, 8, V), np.int64)
    for g in range(8):
        if g < 3: lines = [np.roll(zig, 2 * int(rng.integers(0, V // 2))) for r in range(N)]
        elif g < 6: lines = [zig.reshape(-1, 16)[rng.permutation(V // 16)].reshape(-1) for r in range(N)]
        else: lines = [np.arange(V)[::(1, -1)[(r + g) % 2]] for r in range(N)]
        if g == 0: parts = [[(V, r % 2)] for r in range(N)]
        elif g == 1: parts = [[(V - 1, int(rng.integers(0, 2))), (1, 0)] for r in range(N)]
        elif g == 2: parts = [[(V, 2)] for r in range(N)]
        else: parts = [cut(rng, *CUTS[(2, 0, 3, 1, 0)[g - 3]]) for r in range(N)]
        t[:, g], u[:, g] = grow(rng, parts, lines, g % 2 == 1)
    n = np.stack([rng.permutation(np.array([VO, VO - 1, VO - 2, VO - 1, VO - 1, 0, 16, 15])) for r in range(N)])[:, :, None, None]
    all_ = np.argsort(rng.random((N, 8, 16, 1)), axis=2) < n; th = 255 * all_.astype(np.int64)
    e = rng.integers(0, 2, (N, 8, 16, 1)); share = rng.choice(np.array([0.003, 0.02, 0.06]), (N, 8, 1, 1))
    m = (rng.random((N, 8, 1, V)) < share) & (rng.random((N, 8, 16, V)) < rng.random((N, 8, 1, V)))
    m[:, 1::2, :, V - 1] = True; m[:, 0::2, :, 0] = True
    m = np.where(all_, rng.random(m.shape) < 0.5, m)
    return pack(t, u, 255 * (e ^ m.astype(np.int64)), th)
def setup_inputs_corners(rng):
    t = np.empty((N, 8, V), np.int64); u = np.empty((N, 8, V), np.int64); o = rng.permutation(8)
    for q in range(8):
        g = o[q]; lines = [rng.permutation(V) for r in range(N)]
        if q == 0: parts = [[(V, r % 2)] for r in range(N)]
        elif q == 1:
            parts = [[(V - 1, int(rng.integers(0, 2))), (1, 0)] for r in range(N)]; lines = [np.append(rng.permutation(V - 1), V - 1) for r in range(N)]
        elif q == 2: parts = [[(V, 2)] for r in range(N)]
        elif q == 3: parts = [[(V - 2, 2), (2, 2)] for r in range(N)]
        elif q == 4:
            m = V // 6 // 2 * 2; left = V - 4 * (V // 8) - 3 * m
            p = [(2, 0)] * (V // 8) + [(2, 1)] * (V // 8) + [(3, 0)] * (m // 2) + [(3, 1)] * (m // 2) + ([(left, 2)] if left else [])
            parts = [mix(rng, p) for r in range(N)]
        elif q == 5: parts = [mix(rng, [(4, 2), (8, 2), (4, 2)] * (V // 16)) for r in range(N)]
        elif q == 6:
            z = int(rng.integers(0, N))
            for r in range(N): t[r, g] = invol(rng, V if r == z else 2 * int(rng.choice(np.array([0, 1, V // 16, V // 4])))); u[r, g] = rng.permutation(V)
            continue
        else: parts = [cut(rng, *CUTS[0]) for r in range(N)]
        t[:, g], u[:, g] = grow(rng, parts, lines)
    x, th = hang(rng)
    return pack(t, u, x, th)
def setup_inputs_lone(rng):
    t = np.empty((N, 8, V), np.int64); u = np.empty((N, 8, V), np.int64); o = rng.permutation(8)
    pairs = [(2, 0)] * (V // 8) + [(2, 1)] * (V // 8) + [(4, 2)] * (V // 8)
    few = [(3, 0)] * (V // 128) + [(3, 1)] * (V // 128) + [(2, 0)] * (V // 64) + [(2, 1)] * (V // 64) + [(4, 2)] * (V // 128)
    m = 10 * (V // 128) + 4 * (V // 64); still = [(2, 2)] * (V // 8) + [(1, 0)] * (V - m - 2 * (V // 8))
    for q in range(8):
        g = o[q]; lines = [rng.permutation(V) for r in range(N)]
        if q < 2: parts = [[(V, r % 2)] for r in range(N)]
        elif q == 2: parts = [[(V - 16, r % 2), (16, 2)] for r in range(N)]
        elif q < 5:
            parts = [mix(rng, pairs) for r in range(N)]
            if q == 4: lines = [np.arange(V)[::(1, -1)[r % 2]] for r in range(N)]
        elif q == 5:
            parts = [still + mix(rng, few) for r in range(N)]; lines = [np.concatenate([rng.permutation(V - m), V - m + rng.permutation(m)]) for r in range(N)]
        elif q == 6:
            parts = [[(1, 0)] * (V - 2) + [(2, r % 2)] for r in range(N)]; lines = [np.append(rng.permutation(V - 2), [V - 2, V - 1]) for r in range(N)]
        else: parts = [mix(rng, still + few) for r in range(N)]
        t[:, g], u[:, g] = grow(rng, parts, lines)
    pos = np.argsort(rng.random((N, 8, 16, 1)), axis=2); th = rng.choice(np.array([0, 1, 7, 100, 253, 254]), (N, 8, 16, 1))
    low = np.floor(rng.random((N, 8, 16, 1)) * (255 - th)).astype(np.int64); step = th + (pos >= VO - 1).astype(np.int64)
    x = low + step * rng.integers(0, 2, (N, 8, 1, V))
    for r in range(N):
        for q in range(8):
            g = int(o[q]); s = np.argsort(u[r, g])[t[(r + 1) % N, g][u[r, g]]]; row, first = orbits(t[r, g][s]); size = np.diff(np.append(first, V))
            i = int(np.argmax(pos[r, g, :, 0] == VO - 1)); a = int(low[r, g, i, 0]); b = int(th[r, g, i, 0])
            if q < 3:
                k = int(np.argmax(size)); n = int(size[k]) // 2; j = n - 1 if q == 1 else int(rng.integers(V // 3, n))
                x[r, g, i] = a; x[r, g, i, int(row[int(first[k]) + j + n * int(rng.integers(0, 2))])] = a + b + (r + q) % 2
            else:
                k = int(np.flatnonzero(size % 2 == 0)[-1]); v = int(row[first[k]]); w = int(row[first[k] + 1])
                x[r, g, :, v] = low[r, g, :, 0]; x[r, g, :, w] = low[r, g, :, 0] + step[r, g, :, 0]; x[r, g, i, w] = a + b
    return pack(t, u, x, th)
def setup_inputs_votes(rng):
    t, u = base(rng); x, th = hang(rng)
    return pack(t, u, x, th)
def check_inputs(d):
    bad = []
    for k, lo, hi in (("t0", 0, V - 1), ("u0", 0, V - 1), ("x", 0, 255), ("th", 0, 255)):
        a = np.asarray(d[k]).astype(np.float64)
        if not (np.min(a) >= lo and np.max(a) <= hi): bad.append("range of " + k)
        elif np.any(a != np.floor(a)): bad.append("whole numbers in " + k)
    if not bad:
        t = np.stack([gentries(a) for a in np.asarray(d["t0"])]).astype(np.int64); u = np.stack([gentries(a) for a in np.asarray(d["u0"])]).astype(np.int64)
        if np.any(np.take_along_axis(t, t, 2) != np.arange(V)): bad.append("t0 holds involutions")
        if np.any(np.sort(u, axis=2) != np.arange(V)): bad.append("u0 holds permutations")
    return bad
def orbits(c):
    c = c.tolist(); seen = bytearray(V); row = []; first = []
    for v in range(V):
        if not seen[v]:
            first.append(len(row))
            while not seen[v]:
                seen[v] = 1; row.append(v); v = c[v]
    return np.array(row), np.array(first)
def reference(t0, u0, x, th):
    t = np.stack([gentries(a) for a in t0]).astype(np.int64); u = np.stack([gentries(a) for a in u0]).astype(np.int64)
    xs = x.astype(np.float32).reshape(N, 8, 16, V); lim = th.astype(np.float32).reshape(N, 8, 16, 1)
    for rnd in range(RO):
        tn = np.empty_like(t); un = np.empty_like(u)
        for r in range(N):
            for g in range(8):
                far = t[(r + 1) % N, g]
                s = np.argsort(u[r, g])[far[u[r, g]]]; c = t[r, g][s]
                row, first = orbits(c); size = np.diff(np.append(first, V))
                start = np.repeat(first, size); o = np.repeat(size, size)
                half = row[start + (np.arange(V) - start + o // 2) % o]
                gap = np.abs(xs[r, g][:, row] - xs[r, g][:, half])
                top = np.maximum.reduceat(gap, first, axis=1)
                votes = np.add.reduce((top <= lim[r, g]).astype(np.int64), axis=0)
                turn = np.repeat((size % 2 == 1) | (votes >= VO), size)
                k = np.empty(V, np.int64); k[row] = np.where(turn, half, row)
                h = u[r, g][k]
                tn[r, g] = np.argsort(h)[far[h]]; un[(r + 1) % N, (g + GS) % 8] = h
        t, u = tn, un
    return {"yt": np.stack([gtable(a) for a in t]).astype(np.float32), "yu": np.stack([gtable(a) for a in u]).astype(np.float32)}

@@ -1,0 +1,653 @@
+from concourse.mybir import AluOpType as A, ActivationFunctionType as F
+
+V = 3072
+M = 192
+RO = 2
+GS = 3
+HALF = V // 2
+ODD = V + HALF
+SLW = ODD + V
+PIECE = 384
+STEPS = 10
+
+
+def _sb(cols, dt):
+    return ("sbuf", [128, cols], dt)
+
+
+SCRATCH = {
+    "xs": _sb(V, "bfloat16"), "ids": _sb(V, "bfloat16"), "WU": _sb(V, "bfloat16"), "WM": _sb(V, "bfloat16"),
+    "P0": _sb(V, "bfloat16"), "P1": _sb(V, "bfloat16"), "OB": _sb(V, "bfloat16"), "OC": _sb(V, "bfloat16"),
+    "K0": _sb(V, "float32"), "K1": _sb(V, "float32"), "D0": _sb(V, "float32"), "D1": _sb(V, "float32"),
+    "SL": _sb(SLW, "bfloat16"),
+    "xa": _sb(HALF, "bfloat16"), "xd": _sb(HALF, "bfloat16"), "xm": _sb(HALF, "bfloat16"), "dec": _sb(HALF, "bfloat16"),
+    "CN": _sb(64 * STEPS, "float32"),
+    "LL": _sb(M * (STEPS + 1), "uint16"),
+    "tin": _sb(M, "int32"), "uin": _sb(M, "int32"), "thi": _sb(8, "int32"), "thf": _sb(8, "float32"),
+    "TP0": _sb(2 * M, "bfloat16"), "TP1": _sb(2 * M, "bfloat16"), "UP": _sb(2 * M, "bfloat16"), "HP": _sb(2 * M, "bfloat16"),
+    "landF0": _sb(2 * M, "bfloat16"), "landF1": _sb(2 * M, "bfloat16"), "landU": _sb(2 * M, "bfloat16"),
+    "landY": _sb(M, "float32"), "hout": _sb(M, "float32"), "tout": _sb(M, "float32"),
+    "idp": _sb(4 * M, "bfloat16"), "vp": _sb(2 * M, "bfloat16"), "ia": _sb(M, "float32"), "wid": _sb(M, "float32"),
+    "sp": _sb(4 * M, "bfloat16"), "rh": _sb(2 * M, "bfloat16"), "rl": _sb(2 * M, "bfloat16"),
+    "Zb": _sb(200, "float32"), "zer": _sb(256, "float32"), "zb": _sb(ODD // 16, "bfloat16"),
+    "ci": _sb(8, "int32"), "cf": _sb(24, "float32"), "wt": _sb(8, "float32"), "i8": _sb(8, "float32"),
+    "cc": _sb(144, "float32"), "EB": _sb(144, "float32"), "gg": _sb(128, "float32"), "t128": _sb(128, "float32"),
+    "BO": _sb(128, "bfloat16"), "FB": _sb(128, "bfloat16"), "SH": _sb(128, "bfloat16"), "TR": _sb(128, "float32"),
+}
+for _n in ("E01", "E23", "E45", "Eus", "EC", "Eo", "Ev", "Eh"):
+    SCRATCH[_n] = _sb(144, "bfloat16")
+for _n in ("ul", "uI", "fI", "sI", "lab16", "sl16", "hs16", "es16", "row16", "wid16", "sv16"):
+    SCRATCH[_n] = _sb(M, "uint16")
+for _n in ("i1", "i2", "i3", "di"):
+    SCRATCH[_n] = _sb(M, "int32")
+for _n in ("tf", "uf", "sf", "kt", "KL", "AL", "BL", "f1", "f2", "f3", "f4", "f5", "w1", "il", "pre", "ge", "odd", "ev",
+           "bt", "ds", "tn"):
+    SCRATCH[_n] = _sb(M, "float32")
+for _b in range(8):
+    SCRATCH["ps%d" % _b] = ("psum", [128, 512], "float32")
+
+_PER_ROUND = ["clr", "upk", "upt", "upu", "upf", "sdn", "srow", "kdn", "adn", "bdn", "rec", "rs_t", "rs_h", "ar_t", "ar_h"]
+SEMAPHORES = (["qv", "qs", "qt", "qg", "ldt", "ldu", "ldx", "ldth", "ldsl", "upid", "outt", "outu"]
+              + ["acc%d" % i for i in range(6)] + ["pre%d" % i for i in range(6)]
+              + [n + str(r) for r in range(RO) for n in _PER_ROUND])
+
+
+def rank_program(g, core, T, topo):
+    rank = T.rank_of(core)
+    if rank is None:
+        return
+    n_ranks = len(T.cores)
+    nxt = T.cores[(rank + 1) % n_ranks]
+    prv = T.cores[(rank - 1) % n_ranks]
+
+    Q = {"v": g.vector, "s": g.scalar, "t": g.tensor, "y": g.sync, "g": g}
+    total = {}
+    seen = {q: {} for q in Q}
+    writer = {}
+    readers = {}
+    bank = {}
+
+    def need(q, tok):
+        sem, val = tok
+        if val is None:
+            val = total[sem]
+        if seen[q].get(sem, 0) < val:
+            Q[q].wait_ge(T.sem[sem], val)
+            seen[q][sem] = val
+
+    def before(q, rd, wr):
+        toks = []
+        for k in rd:
+            if k in writer:
+                toks.append(writer[k])
+        for k in wr:
+            if k in writer:
+                toks.append(writer[k])
+            toks.extend(readers.get(k, []))
+        for k in rd + wr:
+            if k[0] == "ps" and k[1] in bank and bank[k[1]][0] != q:
+                toks.append(bank[k[1]][1])
+        top = {}
+        for sem, val in toks:
+            if q == "t" and sem == "qt":
+                continue
+            top[sem] = max(top.get(sem, 0), total[sem] if val is None else val)
+        for sem in top:
+            need(q, (sem, top[sem]))
+
+    def after(q, tok, rd, wr):
+        for k in rd:
+            readers.setdefault(k, []).append(tok)
+        for k in wr:
+            writer[k] = tok
+            readers[k] = []
+        for k in rd + wr:
+            if k[0] == "ps":
+                bank[k[1]] = (q, tok)
+
+    def op(q, fn, rd, wr):
+        before(q, rd, wr)
+        sem = "q" + q
+        fn().then_inc(T.sem[sem], 1)
+        total[sem] = total.get(sem, 0) + 1
+        after(q, (sem, total[sem]), rd, wr)
+
+    def dma(q, out, in_, sem, rd, wr, **kw):
+        before(q, rd, wr)
+        Q[q].dma_start(out, in_, **kw).then_inc(T.sem[sem], 16)
+        total[sem] = total.get(sem, 0) + 16
+        after(q, (sem, None), rd, wr)
+
+    def send(src, dst, to, sem_l, sem_r, rd):
+        before("g", rd, [])
+        rid, pid, _ = topo.addr(to)
+        g.remote_dma(T[dst][:], T[src][:], T.sem[sem_r], T.sem[sem_l], pid, rid, topo.mask(core, to))
+        total[sem_l] = len(topo.engines(core, to))
+        after("g", (sem_l, None), rd, [])
+
+    def arrive(buf, frm, sem_r):
+        total[sem_r] = len(topo.engines(frm, core))
+        writer[(buf,)] = (sem_r, None)
+
+    def K(name, *parts):
+        return [(name, x) for x in parts] if parts else [(name,)]
+
+    def K3(name):
+        return K(name, 0, 1, 2)
+
+    def whole(name):
+        return [k for k in writer if k[0] == name]
+
+    def claim(name, queues):
+        keys = whole(name)
+        for q in queues:
+            before(q, [], keys)
+        for k in keys:
+            del writer[k]
+            readers.pop(k, None)
+
+    def chunks(name, a, b, tag=None):
+        return [(name, c if tag is None else (tag, c)) for c in range(a // 64, (b - 1) // 64 + 1)]
+
+    def p(b, s):
+        return ("ps", b, s)
+
+    def ap(x):
+        if isinstance(x, tuple):
+            return T["ps%d" % x[1]][:, 256 * x[2]:256 * x[2] + M]
+        return T[x][:, 0:M]
+
+    def ky(x):
+        return [x] if isinstance(x, tuple) else [(x,)]
+
+    def tt(out, a, b, o):
+        op("v", lambda: g.vector.tensor_tensor(ap(out), ap(a), ap(b), o), ky(a) + ky(b), ky(out))
+
+    def ts(out, a, s1, o1, s2=None, o2=None):
+        if o2 is None:
+            op("v", lambda: g.vector.tensor_scalar(ap(out), ap(a), s1, None, o1), ky(a), ky(out))
+        else:
+            op("v", lambda: g.vector.tensor_scalar(ap(out), ap(a), s1, s2, o1, o2), ky(a), ky(out))
+
+    def cp(out, a):
+        op("v", lambda: g.vector.tensor_copy(ap(out), ap(a)), ky(a), ky(out))
+
+    def vop(fn, rd, wr):
+        op("v", fn, rd, wr)
+
+    def matmuls(calls, rd, wr):
+        before("t", rd, wr)
+        ins = None
+        for k, (out, lhsT, rhs) in enumerate(calls):
+            ins = g.tensor.matmul(out, lhsT, rhs, k == 0, k == len(calls) - 1)
+        ins.then_inc(T.sem.qt, 1)
+        total["qt"] = total.get("qt", 0) + 1
+        after("t", ("qt", total["qt"]), rd, wr)
+
+    def pk(b):
+        return [p(b, 0), p(b, 1)]
+
+    def conv(E, srcs, n, b, col, rd):
+        matmuls([(T["ps%d" % b][:, col:col + n], T[E][:, 15 - i:143 - i], T[s][:, c0 + i:c0 + 16 * n:16])
+                 for (s, c0) in srcs for i in range(16)], rd + K(E), [p(b, 0)])
+
+    def gather(q, out, win, wcols, lst, l0, a, b, rd, wr, bias=None):
+        src = T[win][:, 0:wcols].indirect(T[lst][:, l0 + a:l0 + b])
+        dst = T[out][:, 16 * a:16 * b]
+        if q == "s":
+            if bias is None:
+                op("s", lambda: g.scalar.activation(dst, src, F.Copy), rd, wr)
+            else:
+                op("s", lambda: g.scalar.activation(dst, src, F.Identity, bias=bias), rd, wr)
+        elif bias is None:
+            op("v", lambda: g.vector.tensor_copy(dst, src), rd, wr)
+        else:
+            op("v", lambda: g.vector.tensor_scalar(dst, src, bias, None, A.add), rd, wr)
+
+    def to16(lst, a, b, bk, col, wr):
+        vop(lambda: g.vector.tensor_copy(T[lst][:, a:b], T["ps%d" % bk][:, col:col + b - a]), [p(bk, 0)], wr)
+
+    def row(buf, r):
+        return T[buf][r::16, 0:V]
+
+    def col(out, src, s1, o1, s2=None, o2=None):
+        a = T[src[0]][:, src[1]:src[1] + 1]
+        rd = K("wt") if src[0] == "wt" else K(src[0], src[1])
+        if o2 is None:
+            vop(lambda: g.vector.tensor_scalar(T.cf[:, out:out + 1], a, s1, None, o1), rd, K("cf", out))
+        else:
+            vop(lambda: g.vector.tensor_scalar(T.cf[:, out:out + 1], a, s1, s2, o1, o2), rd, K("cf", out))
+
+    def cf(i):
+        return T.cf[:, i:i + 1]
+
+    def wt(i):
+        return T.wt[:, i:i + 1]
+
+    def act(out, in_, rd, wr, func=F.Identity, **kw):
+        op("s", lambda: g.scalar.activation(out, in_, func, **kw), rd, wr)
+
+    def make_e(name, weights, key):
+        act(T[name][:], T.EB[:], K("EB") + key, K(name), scale=weights)
+
+    WMK = K("WM", "f0", "f1", "t0", "t1", "u0", "u1", "u2", "u3", "s0", "s1", "v0", "v1")
+    IDK = K("ids", 0, 1, 2, 3)
+    sh = 16 * GS
+
+    dma("y", T.uin[:], T.u0[:], "ldu", [], K("uin"))
+    dma("s", T.tin[:], T.t0[:], "ldt", [], K("tin"))
+    fl = {"allow_small_or_imprecise_dtypes": True}
+    op("g", lambda: g.iota(T.ci[:, 0:1], [[0, 1]], 0, 1), [], K("ci", 0))
+    op("g", lambda: g.iota(T.ia[:], [[1, 12], [0, 16]], 0, 0, **fl), [], K("ia"))
+    op("g", lambda: g.iota(T.idp[:, 0:M], [[0, 12], [M, 16]], 0, 0, **fl), [], K("idp", 0))
+    op("g", lambda: g.iota(T.idp[:, 3 * M:4 * M], [[0, 12], [1, 16]], 0, 0, **fl), [], K("idp", 3))
+    op("g", lambda: g.iota(T.cc[:], [[1, 144]], 0, -1, **fl), [], K("cc"))
+    op("g", lambda: g.iota(T.i8[:], [[1, 8]], 0, 0, **fl), [], K("i8"))
+    vop(lambda: g.vector.memset(T.zer[:], 0.0), [], K("zer"))
+    vop(lambda: g.vector.memset(T.ids[:], 1.0), [], IDK)
+    for c in range(V // 256):
+        op("s", lambda: g.scalar.activation(T.WM[:, 256 * c:256 * c + 256], T.zer[:], F.Copy), K("zer"), K("WM", "z%d" % c))
+    for k in WMK:
+        writer[k] = writer[("WM", "z%d" % (V // 256 - 1))]
+    vop(lambda: g.vector.tensor_scalar(T.ci[:, 1:2], T.ci[:, 0:1], 15, None, A.bitwise_and), K("ci", 0), K("ci", 1))
+    col(0, ("ci", 1), 12.0, A.mult)
+    vop(lambda: g.vector.tensor_scalar(T.idp[:, M:2 * M], T.ia[:], cf(0), None, A.add), K("ia") + K("cf", 0), K("idp", 1))
+    vop(lambda: g.vector.tensor_scalar(T.idp[:, 2 * M:3 * M], T.ia[:], cf(0), 16.0, A.add, A.mult),
+        K("ia") + K("cf", 0), K("idp", 2))
+    for r in (0, 3, 1, 2):
+        dma("y", row("ids", r), T.idp[:, r * M:(r + 1) * M], "upid", K("idp", r), K("ids", r))
+
+    def pieces_in(src, pc):
+        ts("i1", src, 15, A.bitwise_and)
+        ts("i2", src, 4, A.arith_shift_right)
+        vop(lambda: g.vector.tensor_scalar(T[pc][:, 0:M], T.i1[:], float(M), None, A.mult), K("i1"), K(pc, 0))
+        vop(lambda: g.vector.tensor_scalar(T[pc][:, M:2 * M], T.i2[:], 1.0, None, A.mult), K("i2"), K(pc, 1))
+
+    pieces_in("tin", "TP0")
+    send("TP0", "landF0", prv, "rs_t0", "ar_t0", K("TP0", 0, 1))
+    pieces_in("uin", "UP")
+    vop(lambda: g.vector.tensor_tensor(T.uf[:], T.UP[:, 0:M], T.UP[:, M:2 * M], A.add), K("UP", 0, 1), K("uf"))
+    cp("ul", "uf")
+
+    def constants_head():
+        col(1, ("ci", 1), -1.0, A.mult, 15.0, A.add)
+        vop(lambda: g.vector.tensor_scalar(T.ci[:, 2:3], T.ci[:, 1:2], 1, None, A.arith_shift_right), K("ci", 1), K("ci", 2))
+        col(2, ("ci", 2), 1.0, A.mult)
+        vop(lambda: g.vector.tensor_scalar(T.EB[:], T.cc[:], cf(1), None, A.is_equal), K("cc") + K("cf", 1), K("EB"))
+        vop(lambda: g.vector.tensor_scalar(T.wt[:], T.i8[:], cf(2), None, A.is_equal), K("i8") + K("cf", 2), K("wt"))
+        make_e("E45", wt(2), K("wt"))
+        make_e("E01", wt(0), K("wt"))
+        make_e("E23", wt(1), K("wt"))
+
+    dma("g", T.thi[:, 0:1], T.th[:], "ldth", [], K("thi"), allow_slow_non_contiguous=True)
+
+    def step_constant(j):
+        op("g", lambda: g.iota(T.CN[:, 64 * j:64 * j + 64], [[0, 64]], -2 ** j, 0, **fl), [], K("CN", j))
+
+    op("g", lambda: g.iota(T.wid[:], [[1, M]], 0, 0, **fl), [], K("wid"))
+    step_constant(0)
+    step_constant(1)
+    op("g", lambda: g.iota(T.D0[:], [[0, V]], 0, 0, **fl), [], K3("D0"))
+    op("g", lambda: g.iota(T.D1[:], [[0, V]], 0, 0, **fl), [], K3("D1"))
+
+    loads = ([(T.SL[:, c:c + PIECE], T.x[:, c % V:c % V + PIECE], "ldsl", ("SL", "p%d" % c)) for c in range(0, SLW, PIECE)]
+             + [(T.xs[:, c:c + PIECE], T.x[:, c:c + PIECE], "ldx", ("xs", "p%d" % c)) for c in range(0, V, PIECE)])
+    SLK = [x[3] for x in loads if x[3][0] == "SL"] + K("SL", 0, 12, 13)
+    XK = [x[3] for x in loads if x[3][0] == "xs"]
+
+    def constants_doubling():
+        act(cf(12), cf(1), K("cf", 1), K("cf", 12), scale=-1.0, bias=15.0)
+        act(cf(6), cf(1), K("cf", 1), K("cf", 6), scale=-float(M), bias=15.0 * M)
+        act(T.zb[:, 0:256], T.zer[:], K("zer"), K("zb", 0))
+        act(T.zb[:, 256:ODD // 16], T.zer[:, 0:ODD // 16 - 256], K("zer"), K("zb", 1))
+        act(cf(10), cf(12), K("cf", 12), K("cf", 10), func=F.Sign)
+        act(T.wid[:], T.wid[:], K("wid") + K("cf", 6), K("wid"), bias=cf(6))
+        act(T.vp[:, M:2 * M], T.zer[:, 0:M], K("zer") + K("cf", 12), K("vp", 1), bias=cf(12))
+        act(cf(11), cf(10), K("cf", 10), K("cf", 11), scale=-1.0, bias=1.0)
+
+    def constants_leaders():
+        vop(lambda: g.vector.tensor_scalar(T.ci[:, 3:4], T.ci[:, 0:1], 4, None, A.arith_shift_right), K("ci", 0), K("ci", 3))
+        vop(lambda: g.vector.tensor_copy(T.thf[:, 0:1], T.thi[:, 0:1]), K("thi"), K("thf"))
+        col(3, ("ci", 3), 1.0, A.mult)
+        vop(lambda: g.vector.tensor_scalar(T.gg[:], T.gg[:], cf(3), None, A.is_equal), K("gg") + K("cf", 3), K("gg"))
+        op("g", lambda: g.affine_select(T.TR[:], T.gg[:], [[1, 128]], A.is_gt, 0.0, 0, -1), K("gg"), K("TR"))
+        op("g", lambda: g.iota(T.Zb[:, 0:1], [[0, 1]], 0, 0, **fl), [], K("Zb", 0))
+        op("g", lambda: g.affine_select(T.t128[:], T.zer[:, 0:128], [[1, 128]], A.not_equal, 1.0, -sh, -1), K("zer"), K("t128"))
+        op("g", lambda: g.affine_select(T.t128[:], T.t128[:], [[1, 128]], A.not_equal, 1.0, 128 - sh, -1), K("t128"), K("t128"))
+
+    def constants_votes():
+        act(cf(8), wt(4), K("wt"), K("cf", 8), bias=wt(5))
+        act(cf(13), wt(5), K("wt"), K("cf", 13), scale=0.5)
+        act(cf(7), wt(3), K("wt"), K("cf", 7), scale=4096.0, bias=wt(2))
+        act(cf(9), wt(0), K("wt"), K("cf", 9), scale=0.5)
+        act(cf(5), cf(12), K("wt") + K("cf", 12), K("cf", 5), scale=wt(0), bias=-1.0)
+        make_e("Eo", cf(13), K("cf", 13))
+        make_e("EC", cf(8), K("cf", 8))
+        make_e("Ev", wt(6), K("wt"))
+        make_e("Eus", cf(7), K("cf", 7))
+        make_e("Eh", cf(9), K("cf", 9))
+        act(T.BO[:], T.gg[:], K("gg"), K("BO"))
+        act(T.FB[:], T.gg[:], K("gg") + K("cf", 11), K("FB"), scale=cf(11))
+        act(T.SH[:], T.t128[:], K("t128"), K("SH"))
+
+    def unlabel(out, src):
+        ts("f2", src, -95.5, A.add, 1.0 / M, A.mult)
+        ts("f1", src, 16.0, A.mult)
+        cp("i1", "f2")
+        ts(p(4, 1), "i1", -float(V - 1), A.mult)
+        tt(out, "f1", p(4, 1), A.add)
+
+    def split(dst, src):
+        vop(lambda: g.vector.tensor_copy(T[dst][:, 0:M], ap(src)), ky(src), K(dst, 0))
+        vop(lambda: g.vector.tensor_tensor(T[dst][:, M:2 * M], ap(src), T[dst][:, 0:M], A.subtract),
+            ky(src) + K(dst, 0), K(dst, 1))
+
+    CH = [(0, 64), (64, 128), (128, 192)]
+    HV = [(0, 96), (96, 192)]
+    QUARTERS = [("v", 0, 48), ("s", 48, 96), ("v", 96, 144), ("s", 144, 192)]
+
+    for rnd in range(RO):
+        R = str(rnd)
+        last = rnd + 1 == RO
+        TP = "TP" + R
+        landF = "landF" + R
+        if rnd == 0:
+            dma("y", row("WM", 4), T.UP[:, 0:M], "upu0", K("UP", 0), K("WM", "u0", "u2"))
+            dma("s", row("WM", 5), T.UP[:, M:2 * M], "upu0", K("UP", 1), K("WM", "u1", "u3"))
+        else:
+            arrive("landU", prv, "ar_h0")
+            matmuls([(T.ps0[:, 0:M], T.SH[:], T.landU[:, 0:M]), (T.ps0[:, 0:M], T.SH[:], T.landU[:, M:2 * M])],
+                    K("landU") + K("SH"), [p(0, 0)])
+            cp("ul", p(0, 0))
+            for x in range(2):
+                q = "y" if x == 0 else "s"
+                dma(q, T.WM[sh + 4 + x::16, 0:V], T.landU[0:128 - sh, x * M:(x + 1) * M], "upu1", K("landU"), K("WM", "u%d" % x))
+                dma(q, T.WM[4 + x:sh:16, 0:V], T.landU[128 - sh:128, x * M:(x + 1) * M], "upu1", K("landU"), K("WM", "u%d" % (x + 2)))
+
+        def scatter_u(a, b):
+            vop(lambda: g.vector.tensor_copy(T.WU[:, 0:V].indirect(T.ul[:, a:b]), T.ids[:, 16 * a:16 * b]),
+                K("ul") + IDK, K("WU"))
+
+        if rnd == 0:
+            scatter_u(0, 24)
+            constants_head()
+            scatter_u(24, 64)
+        else:
+            scatter_u(0, 64)
+        if rnd == 0:
+            vop(lambda: g.vector.tensor_tensor(T.tf[:], T.TP0[:, 0:M], T.TP0[:, M:2 * M], A.add), K("TP0", 0, 1), K("tf"))
+            ts("kt", "tf", 4096.0, A.mult, 1024.0, A.add)
+        else:
+            cp("uf", p(0, 0))
+            claim("K1", "y")
+            dma("y", row("K1", 0), T.kt[:], "upk" + R, K("kt"), K3("K1"))
+        conv("E45", [("WM", 0)], M, 1, 0, WMK)
+        to16("uI", 0, M, 1, 0, K("uI"))
+        dma("y", row("WM", 2), T[TP][:, 0:M], "upt" + R, K(TP, 0), K("WM", "t0"))
+        dma("y", row("WM", 3), T[TP][:, M:2 * M], "upt" + R, K(TP, 1), K("WM", "t1"))
+        arrive(landF, nxt, "ar_t" + R)
+        dma("y", row("WM", 0), T[landF][:, 0:M], "upf" + R, K(landF), K("WM", "f0"))
+        dma("y", row("WM", 1), T[landF][:, M:2 * M], "upf" + R, K(landF), K("WM", "f1"))
+        if rnd == 0:
+            op("s", lambda: g.scalar.activation(T.K1[:], T.ids[:], F.Copy), IDK, K3("K1"))
+            dma("y", row("K1", 0), T.kt[:], "upk" + R, K("kt"), K3("K1"))
+            constants_doubling()
+        scatter_u(64, M)
+        claim("OB", "s")
+        for c, (a, b) in enumerate(CH):
+            gather("s", "OB", "WM", V, "uI", 0, a, b, WMK + K("uI"), K("OB", c))
+            conv("E01", [("OB", 16 * a)], 64, c, 0, K("OB", c))
+        for c, (a, b) in enumerate(CH):
+            to16("fI", a, b, c, 0, K("fI", c))
+        claim("OC", "vs")
+        for q, a, b in QUARTERS:
+            gather(q, "OC", "WU", V, "fI", 0, a, b, K("WU") + chunks("fI", a, b), K("OC", a))
+            if q == "s":
+                conv("E01", [("OC", 16 * (b - 96))], 96, b // 96 - 1, 0, K("OC", b - 96, a))
+        to16("sI", 0, 96, 0, 0, K("sI", 0))
+
+        def prefill(j, c):
+            D = "D%d" % (j % 2)
+            dma("y", T[D][0::16, 1024 * c:1024 * c + 1024], T.CN[:, 64 * j:64 * j + 64], "pre%d" % (3 * (j % 2) + c),
+                K("CN", j), K(D, c))
+
+        def accumulate(j, c):
+            D, Kj = "D%d" % (j % 2), "K%d" % (j % 2)
+            dma("g", T[D][0::16, 1024 * c:1024 * c + 1024], T[Kj][0::16, 1024 * c:1024 * c + 1024],
+                "acc%d" % (3 * (j % 2) + c), K(Kj, c), K(D, c), accum_op=A.add)
+
+        claim("D0", "y")
+        for j in range(2):
+            for c in range(3):
+                prefill(j, c)
+        SK = [K("sI", 0), K("sI", 0, 1), K("sI", 1)]
+        pend = []
+
+        def flush():
+            while pend:
+                j1, c1 = pend.pop(0)
+                to16("LL", M * j1 + 64 * c1, M * j1 + 64 * c1 + 64, c1, 0, K("LL", (j1, c1)))
+
+        claim("P0", "s")
+        for c, (a, b) in enumerate(CH):
+            gather("s", "P0", "WM", V, "sI", 0, a, b, WMK + SK[c], K("P0", c))
+            gather("v", "K0", "K1", V, "sI", 0, a, b, K3("K1") + SK[c], K("K0", c))
+            if c == 0:
+                to16("sI", 96, M, 1, 0, K("sI", 1))
+            conv("E23", [("P0", 16 * a)], 64, c, 0, K("P0", c))
+            accumulate(0, c)
+            flush()
+            pend.append((0, c))
+        for r in range(2 if last else 0, 4):
+            dma("y", T.sp[:, r * M:(r + 1) * M], row("OC", r), "sdn" + R, whole("OC"), K("sp", r))
+        if rnd == 0:
+            cp("wid16", "wid")
+            op("g", lambda: g.iota(T.vp[:, 0:M], [[16, M]], 0, 0, **fl), [], K("vp", 0))
+            op("g", lambda: g.iota(T.gg[:], [[1, 8], [0, 16]], 0, 0, **fl), [], K("gg"))
+        for r in range(2):
+            dma("y", row("WM", 6 + r), row("OC", r + (2 if last else 0)), "srow" + R, whole("OC"), K("WM", "s%d" % r))
+            if rnd == 0:
+                dma("y", row("WM", 12 + r), T.vp[:, r * M:(r + 1) * M], "srow" + R, K("vp", r), K("WM", "v%d" % r))
+
+        for j in range(STEPS):
+            Pa, Pb = "P%d" % (j % 2), "P%d" % ((j + 1) % 2)
+            Ka, Kb, D = "K%d" % (j % 2), "K%d" % ((j + 1) % 2), "D%d" % (j % 2)
+            for c, (a, b) in enumerate(CH):
+                lk = K("LL", (j, c))
+                src = T[Ka][:, 0:V].indirect(T.LL[:, M * j + a:M * j + b])
+                vop(lambda: g.vector.tensor_tensor(T[Kb][:, 16 * a:16 * b], src, T[D][:, 16 * a:16 * b], A.min),
+                    K3(Ka) + lk + K(D, c), K(Kb, c))
+                if j + 1 < STEPS:
+                    accumulate(j + 1, c)
+                if j + 2 < STEPS:
+                    if rnd == 0 and c == 0:
+                        step_constant(j + 2)
+                    prefill(j + 2, c)
+                if loads:
+                    out, in_, sem, key = loads.pop(0)
+                    before("y", K(Kb, c), [])
+                    dma("y", out, in_, sem, [], [key])
+                if (j, c) == (STEPS - 2, 0):
+                    before("y", [], SLK)
+                    for r in (0, 12, 13):
+                        dma("y", T.SL[r::16, 0:ODD], T.zb[:], "clr" + R, K("zb", 0, 1), K("SL", r))
+                flush()
+                gather("s", Pb, Pa, V, "LL", M * j, a, b, K3(Pa) + lk, K(Pb, c))
+                conv("E23", [(Pb, 16 * a)], 64, c, 0, K(Pb, c))
+                pend.append((j + 1, c))
+        dma("y", T.KL[:], row("K0", 0), "kdn" + R, K3("K0"), K("KL"))
+        for (dst, win, sem, lst, parts) in (
+                ("K1", "K0", "adn", "AL", [("v", 0, 64), ("s", 64, 128), ("v", 128, 160), ("s", 160, M)]),
+                ("D0", "K1", "bdn", "BL", [("v", 0, 96), ("s", 96, M)])):
+            claim(dst, "vs")
+            for q, a, b in parts:
+                gather(q, dst, win, V, "LL", M * STEPS, a, b, whole(win) + chunks("LL", a, b, STEPS), K(dst, "at%d" % a),
+                       bias=1024.0)
+                flush()
+            dma("y", T[lst][:], row(dst, 0), sem + R, whole(dst), K(lst))
+        op("s", lambda: g.scalar.activation(T.P1[:], T.WM[:, 0:V].indirect(T.wid16[:]), F.Identity, bias=cf(11), scale=cf(10)),
+           WMK + K("wid16") + K("cf", 10, 11), K3("P1"))
+
+        if rnd == 0:
+            constants_leaders()
+        sv = "sf" if last else "f1"
+        vop(lambda: g.vector.tensor_tensor(T[sv][:], T.sp[:, 2 * M:3 * M], T.sp[:, 3 * M:4 * M], A.add), K("sp", 2, 3), K(sv))
+        tt(p(6, 0), "KL", "AL", A.min)
+        cp("sv16", sv)
+        if last:
+            unlabel("tf", "tf")
+        else:
+            vop(lambda: g.vector.tensor_tensor(T.sf[:], T.sp[:, 0:M], T.sp[:, M:2 * M], A.add), K("sp", 0, 1), K("sf"))
+        tt("i1", "BL", p(6, 0), A.min)
+        ts("i2", "i1", 12, A.arith_shift_right)
+        ts("di", "i1", 4095, A.bitwise_and)
+        tt(p(7, 1), "i2", "wid", A.is_equal)
+        vop(lambda: g.vector.tensor_tensor(T.ps5[:, M:2 * M], T.di[:], ap(p(7, 1)), A.mult), K("di") + [p(7, 1)], [p(5, 1)])
+        vop(lambda: g.vector.tensor_tensor_scan(T.Zb[:, 1:M + 1], T.ps5[:, M:2 * M], T.zer[:, 0:M], 0.0, A.add, A.add),
+            [p(5, 1)] + K("zer"), K("Zb", 1))
+        matmuls([(T.ps3[:, 0:2], T.TR[:], T.Zb[:, M - 1:M + 1])], K("TR") + K("Zb", 1), [p(3, 0)])
+        ts("i3", "di", 1, A.bitwise_and)
+        cp("lab16", "i2")
+        ts(p(6, 1), "i3", float(2 * ODD - 1), A.mult, -float(ODD), A.add)
+        vop(lambda: g.vector.tensor_scalar(T.i1[:], T.Zb[:, 0:M], T.ps3[:, 1:2], 1.0, A.add, A.add),
+            K("Zb", 0, 1) + [p(3, 0)], K("i1"))
+        ts("i3", "i1", 1, A.arith_shift_right)
+        tt(p(6, 0), "i1", p(6, 1), A.add)
+        tt(p(5, 0), "i3", p(6, 0), A.max)
+        vop(lambda: g.vector.tensor_copy(T.rh[:], T.ps5[:, 0:2 * M]), pk(5), K("rh"))
+        before("y", [], K3("P0"))
+        dma("y", row("P0", 8), T.rh[:, 0:M], "rec" + R, K("rh"), K("P0", "r0"))
+        dma("y", row("P0", 10), T.rh[:, M:2 * M], "rec" + R, K("rh"), K("P0", "r2"))
+        vop(lambda: g.vector.tensor_tensor(T.rl[:], T.ps5[:, 0:2 * M], T.rh[:], A.subtract), pk(5) + K("rh"), K("rl"))
+        dma("y", row("P0", 9), T.rl[:, 0:M], "rec" + R, K("rl"), K("P0", "r1"))
+        dma("y", row("P0", 11), T.rl[:, M:2 * M], "rec" + R, K("rl"), K("P0", "r3"))
+        ts("f1", p(6, 1), 0.0, A.is_lt, float(V), A.mult)
+        tt("bt", "tf", "sf", A.subtract)
+        tt("il", "f1", p(7, 1), A.mult)
+        tt("pre", "il", "di", A.subtract)
+        if rnd == 0:
+            constants_votes()
+        if last:
+            unlabel("uf", "uf")
+        claim("OB", "vs")
+        for q, a, b in QUARTERS:
+            gather(q, "OB", "P0", V, "lab16", 0, a, b, whole("P0") + K("lab16"), K("OB", a))
+            if q == "s":
+                conv("Eo", [("OB", 16 * (b - 96))], 96, 6, b - 96, K("OB", b - 96, a))
+                conv("EC", [("OB", 16 * (b - 96))], 96, 7, b - 96, K("OB", b - 96, a))
+
+        mh, ce = p(6, 0), p(7, 0)
+        tt(p(5, 0), mh, "di", A.is_ge)
+        ts("w1", mh, -1.0, A.mult, float(HALF), A.add)
+        ts("ev", ce, float(ODD), A.is_lt)
+        tt(p(5, 1), "pre", ce, A.add)
+        tt("f4", "w1", "ev", A.mult)
+        tt("f1", "f4", p(5, 0), A.mult)
+        tt("f3", "f1", p(5, 1), A.add)
+        cp("sl16", "f3")
+        vop(lambda: g.vector.tensor_copy(T.SL[:, 0:SLW].indirect(T.sl16[:]), T.P1[:]), K("sl16") + K3("P1"), SLK)
+        ts(p(6, 1), p(5, 0), -2.0, A.mult, 1.0, A.add)
+
+        conv("Ev", [("SL", HALF)], 96, 1, 0, SLK)
+        conv("Ev", [("SL", 0), ("SL", V)], 96, 0, 0, SLK)
+        for c in range(3):
+            matmuls([(T["ps%d" % (3 + c)][:], T.FB[:], T.SL[:, 512 * c:512 * c + 512])], K("FB") + SLK, pk(3 + c))
+        tt("f2", "f4", mh, A.add)
+        tt(p(7, 1), "di", mh, A.is_equal)
+        tt("f1", "f2", p(6, 1), A.mult)
+        to16("row16", 96, M, 1, 0, K("row16", 1))
+        for c in range(3):
+            src = T.xs[:, 0:V].indirect(T.row16[:, 96 + 32 * c:128 + 32 * c])
+            op("s", lambda: g.scalar.activation(T.xa[:, 512 * c:512 * c + 512], src, F.Copy),
+               XK + K("row16", 1), K("xa", c))
+        ts(p(6, 1), p(7, 1), float(V), A.mult, -0.25, A.add)
+        tt(p(7, 1), "f3", "il", A.subtract)
+        tt("f2", "f1", p(6, 1), A.add)
+        tt("f5", "f2", p(7, 1), A.add)
+        ts("odd", ce, float(ODD), A.is_ge)
+        cp("i1", "f5")
+        tt("f1", "w1", ce, A.add)
+        cp("hs16", "i1")
+        ts("es16", "f1", -float(HALF + 1), A.add, float(HALF - 1), A.min)
+        to16("row16", 0, 96, 0, 0, K("row16", 0))
+
+        def half(q, c):
+            a, b = CH[c]
+            gather(q, "OC", "SL", SLW, "hs16", 0, a, b, SLK + K("hs16"), K("OC", "c%d" % c))
+
+        def half_list(c):
+            conv("Eus", [("OC", 16 * CH[c][0])], 64, 6, CH[c][0], K("OC", "c%d" % c))
+
+        claim("OC", "vs")
+        half("s", 0)
+        half_list(0)
+        for c in range(3):
+            s_ = slice(512 * c, 512 * c + 512)
+            src = T.xs[:, 0:V].indirect(T.row16[:, 32 * c:32 * c + 32])
+            vop(lambda: g.vector.tensor_tensor(T.xd[:, s_], src, T.xa[:, s_], A.subtract),
+                XK + K("row16", 0) + K("xa", c), K("xd", c))
+            op("s", lambda: g.scalar.activation(T.xa[:, s_], T.xd[:, s_], F.Abs), K("xd", c), K("xa", c))
+        half("s", 1)
+        for c in range(3):
+            s_ = slice(512 * c, 512 * c + 512)
+            init = 0.0 if c == 0 else T.xm[:, 512 * c - 1:512 * c]
+            vop(lambda: g.vector.tensor_tensor_scan(T.xm[:, s_], T["ps%d" % (3 + c)][:], T.xa[:, s_], init, A.mult, A.max),
+                pk(3 + c) + K("xa", c) + (K("xm", c - 1) if c else []), K("xm", c))
+            vop(lambda: g.vector.tensor_scalar(T.xd[:, s_], T.xm[:, s_], T.thf[:, 0:1], None, A.is_gt),
+                K("xm", c) + K("thf"), K("xd", c))
+            matmuls([(T["ps%d" % c][:], T.BO[:], T.xd[:, s_])], K("BO") + K("xd", c), pk(c))
+            op("s", lambda: g.scalar.activation(T.dec[:, s_], T["ps%d" % c][:], F.Sign, bias=5.5, scale=cf(5)),
+               pk(c) + K("cf", 5), K("dec", c))
+        half("v", 2)
+        half_list(1)
+        half_list(2)
+        claim("OB", "vs")
+        cut = 128 if last else 112
+        for q, a, b in (("s", 0, 64), ("v", cut, M), ("s", 64, cut)):
+            gather(q, "OB", "dec", HALF, "es16", 0, a, b, K3("dec") + K("es16"), K("OB", a))
+            conv("Eh", [("OB", 16 * a)], b - a, 3, a, K("OB", a))
+        claim("OC", "vs")
+        cut = 144 if last else 152
+        for a, b in ((0, 88), (88, cut)):
+            gather("s", "OC", "OB", V, "sv16", 0, a, b, whole("OB") + K("sv16"), K("OC", a))
+        conv("Eh", [("OC", 0)], 88, 2, 0, K("OC", 0))
+        cp("i1", p(6, 0))
+        ts("i2", "i1", 4095, A.bitwise_and)
+        ts("i3", "i1", 12, A.arith_shift_right)
+        if last:
+            unlabel("f3", "i2")
+        tt(p(7, 0), "f3" if last else "i2", "uf", A.subtract)
+        tt("tn", "odd", p(3, 0), A.max)
+        tt(p(7, 1), "tn", p(7, 0), A.mult)
+        if not last:
+            tt(p(5, 0), "uf", p(7, 1), A.add)
+            split("HP", p(5, 0))
+            send("HP", "landU", nxt, "rs_h" + R, "ar_h" + R, K("HP", 0, 1))
+        else:
+            tt("hout", "uf", p(7, 1), A.add)
+            send("hout", "landY", nxt, "rs_h" + R, "ar_h" + R, K("hout"))
+        gather("v", "OC", "OB", V, "sv16", 0, cut, M, whole("OB") + K("sv16"), K("OC", cut))
+        conv("Eh", [("OC", 16 * cut)], M - cut, 2, cut, K("OC", cut))
+        conv("Eh", [("OC", 16 * 88)], cut - 88, 2, 88, K("OC", 88))
+        tt(p(7, 0), "i3", "sf", A.subtract)
+        tt(p(7, 1), "bt", "odd", A.mult)
+        tt("ds", "ev", p(7, 0), A.mult)
+        tt("bt", "sf", p(7, 1), A.add)
+        tt(p(7, 1), "tn", p(2, 0), A.not_equal)
+        tt(p(7, 0), "ds", p(7, 1), A.mult)
+        if not last:
+            tt(p(7, 1), "bt", p(7, 0), A.add)
+            nx = str(rnd + 1)
+            split("TP" + nx, p(7, 1))
+            send("TP" + nx, "landF" + nx, prv, "rs_t" + nx, "ar_t" + nx, K("TP" + nx, 0, 1))
+            cp("tf", p(7, 1))
+            ts("kt", p(7, 1), 4096.0, A.mult, 1024.0, A.add)
+        else:
+            tt("tout", "bt", p(7, 0), A.add)
+            arrive("landY", prv, "ar_h" + R)
+            dma("s", T.yt[:], T.tout[:], "outt", K("tout"), K("yt"))
+            dma("y", T.yu[sh:128, :], T.landY[0:128 - sh, :], "outu", K("landY"), K("yu", 0))
+            dma("y", T.yu[0:sh, :], T.landY[128 - sh:128, :], "outu", K("landY"), K("yu", 1))
+
+    for sem in total:
+        need("g", (sem, None))

@@ -1,3 +1,4 @@
+import math
 from concourse.mybir import AluOpType as A, ActivationFunctionType as F
 
 V = 3072
@@ -5,10 +6,10 @@ M = 192
 RO = 2
 GS = 3
 HALF = V // 2
-ODD = V + HALF
+ODD = V
 SLW = ODD + V
-PIECE = 384
 STEPS = 10
+PIECE = 768
 
 
 def _sb(cols, dt):
@@ -20,34 +21,43 @@ SCRATCH = {
     "P0": _sb(V, "bfloat16"), "P1": _sb(V, "bfloat16"), "OB": _sb(V, "bfloat16"), "OC": _sb(V, "bfloat16"),
     "K0": _sb(V, "float32"), "K1": _sb(V, "float32"), "D0": _sb(V, "float32"), "D1": _sb(V, "float32"),
     "SL": _sb(SLW, "bfloat16"),
-    "xa": _sb(HALF, "bfloat16"), "xd": _sb(HALF, "bfloat16"), "xm": _sb(HALF, "bfloat16"), "dec": _sb(HALF, "bfloat16"),
-    "CN": _sb(64 * STEPS, "float32"),
+    "xa": _sb(HALF, "bfloat16"), "xd": _sb(HALF, "bfloat16"), "xm": _sb(HALF, "bfloat16"), "dec": _sb(HALF + 16, "bfloat16"),
+    "CN": _sb(1024, "float32"), "cb": _sb(8, "bfloat16"),
     "LL": _sb(M * (STEPS + 1), "uint16"),
     "tin": _sb(M, "int32"), "uin": _sb(M, "int32"), "thi": _sb(8, "int32"), "thf": _sb(8, "float32"),
-    "TP0": _sb(2 * M, "bfloat16"), "TP1": _sb(2 * M, "bfloat16"), "UP": _sb(2 * M, "bfloat16"), "HP": _sb(2 * M, "bfloat16"),
-    "landF0": _sb(2 * M, "bfloat16"), "landF1": _sb(2 * M, "bfloat16"), "landU": _sb(2 * M, "bfloat16"),
+    "TP": _sb(2 * M, "bfloat16"), "UP": _sb(2 * M, "bfloat16"), "HP": _sb(2 * M, "bfloat16"),
+    "landF": _sb(2 * M, "bfloat16"), "landU": _sb(2 * M, "bfloat16"), "landW": _sb(2 * M, "bfloat16"),
+    "wp": _sb(2 * M, "bfloat16"), "TF": _sb(2 * M, "float32"), "vf": _sb(2 * M, "float32"),
+    "QW": _sb(V, "float32"),
     "landY": _sb(M, "float32"), "hout": _sb(M, "float32"), "tout": _sb(M, "float32"),
     "idp": _sb(4 * M, "bfloat16"), "vp": _sb(2 * M, "bfloat16"), "ia": _sb(M, "float32"), "wid": _sb(M, "float32"),
-    "sp": _sb(4 * M, "bfloat16"), "rh": _sb(2 * M, "bfloat16"), "rl": _sb(2 * M, "bfloat16"),
-    "Zb": _sb(200, "float32"), "zer": _sb(256, "float32"), "zb": _sb(ODD // 16, "bfloat16"),
+    "sp": _sb(4 * M, "bfloat16"), "r1": _sb(2 * M, "bfloat16"), "r2": _sb(2 * M, "bfloat16"), "uv": _sb(2 * M, "bfloat16"),
+    "sg": _sb(M, "bfloat16"), "fg": _sb(M, "bfloat16"),
+    "Ip": _sb(128, "float32"), "In": _sb(128, "float32"), "I16": _sb(128, "float32"),
+    "Zb": _sb(M, "float32"), "zer": _sb(256, "float32"), "zb": _sb(M, "bfloat16"),
     "ci": _sb(8, "int32"), "cf": _sb(24, "float32"), "wt": _sb(8, "float32"), "i8": _sb(8, "float32"),
     "cc": _sb(144, "float32"), "EB": _sb(144, "float32"), "gg": _sb(128, "float32"), "t128": _sb(128, "float32"),
-    "BO": _sb(128, "bfloat16"), "FB": _sb(128, "bfloat16"), "SH": _sb(128, "bfloat16"), "TR": _sb(128, "float32"),
+    "BO": _sb(128, "bfloat16"), "FB": _sb(128, "bfloat16"), "TR": _sb(128, "float32"),
 }
-for _n in ("E01", "E23", "E45", "Eus", "EC", "Eo", "Ev", "Eh"):
+for _n in ("E01", "E23", "E45", "E67", "E89", "Ecw", "EA", "EBh", "Ev", "Eh"):
     SCRATCH[_n] = _sb(144, "bfloat16")
-for _n in ("ul", "uI", "fI", "sI", "lab16", "sl16", "hs16", "es16", "row16", "wid16", "sv16"):
+for _n in ("Iq", "It", "Ib", "Im"):
+    SCRATCH[_n] = _sb(128, "bfloat16")
+for _n in ("ul", "uI", "fI", "sI", "lab16", "sl16", "hs16", "es16", "row16", "wid16", "sv16",
+           "landK", "landT"):
     SCRATCH[_n] = _sb(M, "uint16")
 for _n in ("i1", "i2", "i3", "di"):
     SCRATCH[_n] = _sb(M, "int32")
-for _n in ("tf", "uf", "sf", "kt", "KL", "AL", "BL", "f1", "f2", "f3", "f4", "f5", "w1", "il", "pre", "ge", "odd", "ev",
-           "bt", "ds", "tn"):
+for _n in ("tf", "uf", "du", "mh", "t0s", "KL", "AL", "BL", "f1", "f2", "f3", "f4", "w4k", "za", "zo", "hd", "up", "Bs",
+           "zz", "st", "od", "mm", "tm", "tn"):
     SCRATCH[_n] = _sb(M, "float32")
 for _b in range(8):
     SCRATCH["ps%d" % _b] = ("psum", [128, 512], "float32")
 
-_PER_ROUND = ["clr", "upk", "upt", "upu", "upf", "sdn", "srow", "kdn", "adn", "bdn", "rec", "rs_t", "rs_h", "ar_t", "ar_h"]
-SEMAPHORES = (["qv", "qs", "qt", "qg", "ldt", "ldu", "ldx", "ldth", "ldsl", "upid", "outt", "outu"]
+_PER_ROUND = ["clr", "upk", "upu", "sdn", "srow", "crow", "kdn", "adn", "bdn", "rec", "flg",
+              "rs_t", "rs_h", "ar_t", "ar_h"]
+SEMAPHORES = (["qv", "qs", "qt", "qg", "ldt", "ldu", "ldx", "ldth", "ldsl", "upid", "upt", "upf", "uvd", "vup", "wdn", "wup",
+               "rs_w", "ar_w", "rs_k", "ar_k", "outt", "outu"]
               + ["acc%d" % i for i in range(6)] + ["pre%d" % i for i in range(6)]
               + [n + str(r) for r in range(RO) for n in _PER_ROUND])
 
@@ -127,9 +137,12 @@ def rank_program(g, core, T, topo):
 
     def arrive(buf, frm, sem_r):
         total[sem_r] = len(topo.engines(frm, core))
-        writer[(buf,)] = (sem_r, None)
+        for k in K(buf):
+            writer[k] = (sem_r, None)
 
     def K(name, *parts):
+        if not parts and SCRATCH[name][1][1] == M:
+            parts = (0, 1, 2)
         return [(name, x) for x in parts] if parts else [(name,)]
 
     def K3(name):
@@ -152,25 +165,30 @@ def rank_program(g, core, T, topo):
     def p(b, s):
         return ("ps", b, s)
 
-    def ap(x):
+    def ap(x, a=0, b=M):
         if isinstance(x, tuple):
-            return T["ps%d" % x[1]][:, 256 * x[2]:256 * x[2] + M]
-        return T[x][:, 0:M]
+            return T["ps%d" % x[1]][:, 256 * x[2] + a:256 * x[2] + b]
+        return T[x][:, a:b]
 
-    def ky(x):
-        return [x] if isinstance(x, tuple) else [(x,)]
+    def ky(x, cols=(0, M)):
+        return [x] if isinstance(x, tuple) else chunks(x, *cols)
 
-    def tt(out, a, b, o):
-        op("v", lambda: g.vector.tensor_tensor(ap(out), ap(a), ap(b), o), ky(a) + ky(b), ky(out))
+    def tt(out, a, b, o, cols=(0, M)):
+        op("v", lambda: g.vector.tensor_tensor(ap(out, *cols), ap(a, *cols), ap(b, *cols), o),
+           ky(a, cols) + ky(b, cols), ky(out, cols))
 
-    def ts(out, a, s1, o1, s2=None, o2=None):
+    def ts(out, a, s1, o1, s2=None, o2=None, cols=(0, M), rd=()):
+        rd = ky(a, cols) + list(rd)
         if o2 is None:
-            op("v", lambda: g.vector.tensor_scalar(ap(out), ap(a), s1, None, o1), ky(a), ky(out))
+            op("v", lambda: g.vector.tensor_scalar(ap(out, *cols), ap(a, *cols), s1, None, o1), rd, ky(out, cols))
         else:
-            op("v", lambda: g.vector.tensor_scalar(ap(out), ap(a), s1, s2, o1, o2), ky(a), ky(out))
+            op("v", lambda: g.vector.tensor_scalar(ap(out, *cols), ap(a, *cols), s1, s2, o1, o2), rd, ky(out, cols))
 
     def cp(out, a):
         op("v", lambda: g.vector.tensor_copy(ap(out), ap(a)), ky(a), ky(out))
+
+    def sa(out, a, func, scale=1.0, bias=0.0):
+        op("s", lambda: g.scalar.activation(ap(out), ap(a), func, bias=bias, scale=scale), ky(a), ky(out))
 
     def vop(fn, rd, wr):
         op("v", fn, rd, wr)
@@ -187,9 +205,21 @@ def rank_program(g, core, T, topo):
     def pk(b):
         return [p(b, 0), p(b, 1)]
 
-    def conv(E, srcs, n, b, col, rd):
-        matmuls([(T["ps%d" % b][:, col:col + n], T[E][:, 15 - i:143 - i], T[s][:, c0 + i:c0 + 16 * n:16])
-                 for (s, c0) in srcs for i in range(16)], rd + K(E), [p(b, 0)])
+    def conv(E, srcs, n, b, col, rd, plus=()):
+        out = T["ps%d" % b][:, col:col + n]
+        a = col % 256
+        matmuls([(out, T[I][:], T[x][:, c0 + a:c0 + a + n]) for (I, x, c0, _) in plus]
+                + [(out, T[E][:, 15 - i:143 - i], T[s][:, c0 + i:c0 + 16 * n:16]) for (s, c0) in srcs for i in range(16)],
+                rd + K(E) + [k for x in plus for k in x[3]], [p(b, col // 256)])
+
+    def term(I, x):
+        return [(I, x, 0, K(I) + K(x))]
+
+    def pieces(I, buf, c):
+        return [(I, buf, x * M, K(I) + K(buf, x)) for x in (c, c + 1)]
+
+    def lin(out, terms):
+        matmuls([(ap(out), T[I][:], T[x][:, c0:c0 + M]) for (I, x, c0, _) in terms], [k for x in terms for k in x[3]], [out])
 
     def gather(q, out, win, wcols, lst, l0, a, b, rd, wr, bias=None):
         src = T[win][:, 0:wcols].indirect(T[lst][:, l0 + a:l0 + b])
@@ -230,7 +260,11 @@ def rank_program(g, core, T, topo):
     def make_e(name, weights, key):
         act(T[name][:], T.EB[:], K("EB") + key, K(name), scale=weights)
 
-    WMK = K("WM", "f0", "f1", "t0", "t1", "u0", "u1", "u2", "u3", "s0", "s1", "v0", "v1")
+    def pair_sum(out, buf, c, rd):
+        vop(lambda: g.vector.tensor_tensor(T[out][:], T[buf][:, c * M:(c + 1) * M], T[buf][:, (c + 1) * M:(c + 2) * M], A.add),
+            rd, K(out))
+
+    WMK = K("WM", *[x + r for x in "ftuswcv" for r in "01"]) + K("WM", "g")
     IDK = K("ids", 0, 1, 2, 3)
     sh = 16 * GS
 
@@ -245,65 +279,75 @@ def rank_program(g, core, T, topo):
     op("g", lambda: g.iota(T.i8[:], [[1, 8]], 0, 0, **fl), [], K("i8"))
     vop(lambda: g.vector.memset(T.zer[:], 0.0), [], K("zer"))
     vop(lambda: g.vector.memset(T.ids[:], 1.0), [], IDK)
-    for c in range(V // 256):
-        op("s", lambda: g.scalar.activation(T.WM[:, 256 * c:256 * c + 256], T.zer[:], F.Copy), K("zer"), K("WM", "z%d" % c))
-    for k in WMK:
-        writer[k] = writer[("WM", "z%d" % (V // 256 - 1))]
+    vop(lambda: g.vector.memset(T.dec[:, HALF:HALF + 16], 1.0), [], K("dec", "one"))
+
+    def fill(buf, a, b, keys):
+        for c in range(a, b):
+            act(T[buf][:, 256 * c:256 * c + 256], T.zer[:], K("zer"), K(buf, "z%d" % c), func=F.Copy)
+        for k in keys:
+            writer[k] = writer[(buf, "z%d" % (b - 1))]
+
+    fill("WM", 0, 12, WMK)
     vop(lambda: g.vector.tensor_scalar(T.ci[:, 1:2], T.ci[:, 0:1], 15, None, A.bitwise_and), K("ci", 0), K("ci", 1))
     col(0, ("ci", 1), 12.0, A.mult)
+    col(12, ("ci", 1), 1.0, A.mult)
+    act(T.cb[:, 0:1], cf(12), K("cf", 12), K("cb"), func=F.Exp, scale=math.log(2.0))
     vop(lambda: g.vector.tensor_scalar(T.idp[:, M:2 * M], T.ia[:], cf(0), None, A.add), K("ia") + K("cf", 0), K("idp", 1))
     vop(lambda: g.vector.tensor_scalar(T.idp[:, 2 * M:3 * M], T.ia[:], cf(0), 16.0, A.add, A.mult),
         K("ia") + K("cf", 0), K("idp", 2))
     for r in (0, 3, 1, 2):
         dma("y", row("ids", r), T.idp[:, r * M:(r + 1) * M], "upid", K("idp", r), K("ids", r))
 
-    def pieces_in(src, pc):
-        ts("i1", src, 15, A.bitwise_and)
-        ts("i2", src, 4, A.arith_shift_right)
-        vop(lambda: g.vector.tensor_scalar(T[pc][:, 0:M], T.i1[:], float(M), None, A.mult), K("i1"), K(pc, 0))
-        vop(lambda: g.vector.tensor_scalar(T[pc][:, M:2 * M], T.i2[:], 1.0, None, A.mult), K("i2"), K(pc, 1))
+    def pieces_in(pc, lo, hi):
+        vop(lambda: g.vector.tensor_scalar(T[pc][:, 0:M], T[lo][:], float(M), None, A.mult), K(lo), K(pc, 0))
+        vop(lambda: g.vector.tensor_scalar(T[pc][:, M:2 * M], T[hi][:], 1.0, None, A.mult), K(hi), K(pc, 1))
 
-    pieces_in("tin", "TP0")
-    send("TP0", "landF0", prv, "rs_t0", "ar_t0", K("TP0", 0, 1))
-    pieces_in("uin", "UP")
-    vop(lambda: g.vector.tensor_tensor(T.uf[:], T.UP[:, 0:M], T.UP[:, M:2 * M], A.add), K("UP", 0, 1), K("uf"))
+    ts("i1", "tin", 15, A.bitwise_and)
+    ts("i2", "tin", 4, A.arith_shift_right)
+    ts("i3", "uin", 15, A.bitwise_and)
+    pieces_in("TP", "i1", "i2")
+    send("TP", "landF", prv, "rs_t0", "ar_t0", K("TP", 0, 1))
+    for r in range(2):
+        dma("y", row("WM", 2 + r), T.TP[:, r * M:(r + 1) * M], "upt", K("TP", r), K("WM", "t%d" % r))
+    ts("di", "uin", 4, A.arith_shift_right)
+    col(1, ("ci", 1), -1.0, A.mult, 15.0, A.add)
+    vop(lambda: g.vector.tensor_scalar(T.ci[:, 2:3], T.ci[:, 1:2], 1, None, A.arith_shift_right), K("ci", 1), K("ci", 2))
+    pieces_in("UP", "i3", "di")
+    col(2, ("ci", 2), 1.0, A.mult)
+    vop(lambda: g.vector.tensor_scalar(T.EB[:], T.cc[:], cf(1), None, A.is_equal), K("cc") + K("cf", 1), K("EB"))
+    pair_sum("uf", "UP", 0, K("UP", 0, 1))
+    vop(lambda: g.vector.tensor_scalar(T.wt[:], T.i8[:], cf(2), None, A.is_equal), K("i8") + K("cf", 2), K("wt"))
+    pair_sum("tf", "TP", 0, K("TP", 0, 1))
     cp("ul", "uf")
-
-    def constants_head():
-        col(1, ("ci", 1), -1.0, A.mult, 15.0, A.add)
-        vop(lambda: g.vector.tensor_scalar(T.ci[:, 2:3], T.ci[:, 1:2], 1, None, A.arith_shift_right), K("ci", 1), K("ci", 2))
-        col(2, ("ci", 2), 1.0, A.mult)
-        vop(lambda: g.vector.tensor_scalar(T.EB[:], T.cc[:], cf(1), None, A.is_equal), K("cc") + K("cf", 1), K("EB"))
-        vop(lambda: g.vector.tensor_scalar(T.wt[:], T.i8[:], cf(2), None, A.is_equal), K("i8") + K("cf", 2), K("wt"))
-        make_e("E45", wt(2), K("wt"))
-        make_e("E01", wt(0), K("wt"))
-        make_e("E23", wt(1), K("wt"))
-
-    dma("g", T.thi[:, 0:1], T.th[:], "ldth", [], K("thi"), allow_slow_non_contiguous=True)
-
-    def step_constant(j):
-        op("g", lambda: g.iota(T.CN[:, 64 * j:64 * j + 64], [[0, 64]], -2 ** j, 0, **fl), [], K("CN", j))
+    dma("y", row("WM", 4), T.UP[:, 0:M], "upu0", K("UP", 0), K("WM", "u0"))
+    dma("y", row("WM", 5), T.UP[:, M:2 * M], "upu0", K("UP", 1), K("WM", "u1"))
+    make_e("E45", wt(2), K("wt"))
+    make_e("E01", wt(0), K("wt"))
+    make_e("E23", wt(1), K("wt"))
 
     op("g", lambda: g.iota(T.wid[:], [[1, M]], 0, 0, **fl), [], K("wid"))
-    step_constant(0)
-    step_constant(1)
     op("g", lambda: g.iota(T.D0[:], [[0, V]], 0, 0, **fl), [], K3("D0"))
+    dma("g", T.thi[:, 0:1], T.th[:], "ldth", [], K("thi"), allow_slow_non_contiguous=True)
     op("g", lambda: g.iota(T.D1[:], [[0, V]], 0, 0, **fl), [], K3("D1"))
-
-    loads = ([(T.SL[:, c:c + PIECE], T.x[:, c % V:c % V + PIECE], "ldsl", ("SL", "p%d" % c)) for c in range(0, SLW, PIECE)]
-             + [(T.xs[:, c:c + PIECE], T.x[:, c:c + PIECE], "ldx", ("xs", "p%d" % c)) for c in range(0, V, PIECE)])
-    SLK = [x[3] for x in loads if x[3][0] == "SL"] + K("SL", 0, 12, 13)
-    XK = [x[3] for x in loads if x[3][0] == "xs"]
+    loads = ([(T.SL[:, c:c + PIECE], T.x[:, c % V:c % V + PIECE], "ldsl", [], K("SL", "p%d" % c)) for c in range(0, SLW, PIECE)]
+             + [(T.xs[:, c:c + PIECE], T.x[:, c:c + PIECE], "ldx", [], K("xs", c)) for c in range(0, V, PIECE)])
+    SLK = [x[4][0] for x in loads if x[2] == "ldsl"] + K("SL", 12, 13, 14)
+    XK = [x[4][0] for x in loads if x[2] == "ldx"]
 
     def constants_doubling():
-        act(cf(12), cf(1), K("cf", 1), K("cf", 12), scale=-1.0, bias=15.0)
-        act(cf(6), cf(1), K("cf", 1), K("cf", 6), scale=-float(M), bias=15.0 * M)
-        act(T.zb[:, 0:256], T.zer[:], K("zer"), K("zb", 0))
-        act(T.zb[:, 256:ODD // 16], T.zer[:, 0:ODD // 16 - 256], K("zer"), K("zb", 1))
-        act(cf(10), cf(12), K("cf", 12), K("cf", 10), func=F.Sign)
+        act(cf(14), T.cb[:, 0:1], K("cb"), K("cf", 14), scale=-1.0)
+        act(cf(6), cf(12), K("cf", 12), K("cf", 6), scale=float(M))
+        for c in range(4):
+            act(T.CN[:, 256 * c:256 * c + 256], T.zer[:], K("zer") + K("cf", 14), K("CN", c), bias=cf(14))
+        fill("K1", 0, 12, K3("K1"))
+        act(T.zb[:], T.zer[:, 0:M], K("zer"), K("zb"))
+        act(T.wp[:, M:2 * M], T.wid[:], K("wid"), K("wp", 1), func=F.Copy)
+        act(T.wp[:, 0:M], T.zer[:, 0:M], K("zer") + K("cf", 6), K("wp", 0), bias=cf(6))
+        act(T.uv[:, 0:M], T.UP[:, M:2 * M], K("UP", 1), K("uv", 0), scale=16.0)
+        act(T.uv[:, M:2 * M], T.UP[:, 0:M], K("UP", 0), K("uv", 1), scale=1.0 / M)
         act(T.wid[:], T.wid[:], K("wid") + K("cf", 6), K("wid"), bias=cf(6))
         act(T.vp[:, M:2 * M], T.zer[:, 0:M], K("zer") + K("cf", 12), K("vp", 1), bias=cf(12))
-        act(cf(11), cf(10), K("cf", 10), K("cf", 11), scale=-1.0, bias=1.0)
+        act(T.w4k[:], T.wid[:], K("wid"), K("w4k"), scale=4096.0)
 
     def constants_leaders():
         vop(lambda: g.vector.tensor_scalar(T.ci[:, 3:4], T.ci[:, 0:1], 4, None, A.arith_shift_right), K("ci", 0), K("ci", 3))
@@ -311,116 +355,118 @@ def rank_program(g, core, T, topo):
         col(3, ("ci", 3), 1.0, A.mult)
         vop(lambda: g.vector.tensor_scalar(T.gg[:], T.gg[:], cf(3), None, A.is_equal), K("gg") + K("cf", 3), K("gg"))
         op("g", lambda: g.affine_select(T.TR[:], T.gg[:], [[1, 128]], A.is_gt, 0.0, 0, -1), K("gg"), K("TR"))
-        op("g", lambda: g.iota(T.Zb[:, 0:1], [[0, 1]], 0, 0, **fl), [], K("Zb", 0))
         op("g", lambda: g.affine_select(T.t128[:], T.zer[:, 0:128], [[1, 128]], A.not_equal, 1.0, -sh, -1), K("zer"), K("t128"))
         op("g", lambda: g.affine_select(T.t128[:], T.t128[:], [[1, 128]], A.not_equal, 1.0, 128 - sh, -1), K("t128"), K("t128"))
 
-    def constants_votes():
-        act(cf(8), wt(4), K("wt"), K("cf", 8), bias=wt(5))
+    def constants_sums():
+        act(T.vf[:], T.vp[:], K("vp", 0, 1), K("vf"), func=F.Copy)
+        act(T.In[:], T.cc[:, 0:128], K("cc"), K("In"), func=F.Abs)
+        act(cf(8), wt(4), K("wt"), K("cf", 8), scale=0.5)
+        act(T.Ip[:], T.In[:], K("In"), K("Ip"), func=F.Relu, scale=-1.0, bias=1.0)
         act(cf(13), wt(5), K("wt"), K("cf", 13), scale=0.5)
-        act(cf(7), wt(3), K("wt"), K("cf", 7), scale=4096.0, bias=wt(2))
+        for name, scale in (("Ib", 1.0), ("Im", -1.0), ("In", -1.0), ("It", -1280.0), ("Iq", -0.25), ("I16", 16.0)):
+            act(T[name][:], T.Ip[:], K("Ip"), K(name), scale=scale)
+        make_e("EBh", cf(13), K("cf", 13))
+        make_e("EA", cf(8), K("cf", 8))
+
+    def constants_votes():
         act(cf(9), wt(0), K("wt"), K("cf", 9), scale=0.5)
+        act(cf(10), cf(12), K("cf", 12), K("cf", 10), func=F.Abs, bias=-14.0)
         act(cf(5), cf(12), K("wt") + K("cf", 12), K("cf", 5), scale=wt(0), bias=-1.0)
-        make_e("Eo", cf(13), K("cf", 13))
-        make_e("EC", cf(8), K("cf", 8))
+        act(cf(11), cf(10), K("cf", 10), K("cf", 11), func=F.Relu, scale=-1.0, bias=1.0)
         make_e("Ev", wt(6), K("wt"))
-        make_e("Eus", cf(7), K("cf", 7))
+        make_e("E67", wt(3), K("wt"))
         make_e("Eh", cf(9), K("cf", 9))
         act(T.BO[:], T.gg[:], K("gg"), K("BO"))
         act(T.FB[:], T.gg[:], K("gg") + K("cf", 11), K("FB"), scale=cf(11))
-        act(T.SH[:], T.t128[:], K("t128"), K("SH"))
+        act(cf(7), wt(4), K("wt"), K("cf", 7), scale=-1.0, bias=wt(5))
+        make_e("E89", wt(4), K("wt"))
+        make_e("Ecw", cf(7), K("cf", 7))
 
-    def unlabel(out, src):
-        ts("f2", src, -95.5, A.add, 1.0 / M, A.mult)
-        ts("f1", src, 16.0, A.mult)
-        cp("i1", "f2")
-        ts(p(4, 1), "i1", -float(V - 1), A.mult)
-        tt(out, "f1", p(4, 1), A.add)
+    def high(dst, a, b, o):
+        vop(lambda: g.vector.tensor_tensor(T[dst][:, 0:M], ap(a), ap(b), o), ky(a) + ky(b), K(dst, 0))
 
-    def split(dst, src):
-        vop(lambda: g.vector.tensor_copy(T[dst][:, 0:M], ap(src)), ky(src), K(dst, 0))
+    def low(dst, src):
         vop(lambda: g.vector.tensor_tensor(T[dst][:, M:2 * M], ap(src), T[dst][:, 0:M], A.subtract),
             ky(src) + K(dst, 0), K(dst, 1))
 
     CH = [(0, 64), (64, 128), (128, 192)]
-    HV = [(0, 96), (96, 192)]
-    QUARTERS = [("v", 0, 48), ("s", 48, 96), ("v", 96, 144), ("s", 144, 192)]
 
     for rnd in range(RO):
         R = str(rnd)
         last = rnd + 1 == RO
-        TP = "TP" + R
-        landF = "landF" + R
-        if rnd == 0:
-            dma("y", row("WM", 4), T.UP[:, 0:M], "upu0", K("UP", 0), K("WM", "u0", "u2"))
-            dma("s", row("WM", 5), T.UP[:, M:2 * M], "upu0", K("UP", 1), K("WM", "u1", "u3"))
-        else:
-            arrive("landU", prv, "ar_h0")
-            matmuls([(T.ps0[:, 0:M], T.SH[:], T.landU[:, 0:M]), (T.ps0[:, 0:M], T.SH[:], T.landU[:, M:2 * M])],
-                    K("landU") + K("SH"), [p(0, 0)])
-            cp("ul", p(0, 0))
-            for x in range(2):
-                q = "y" if x == 0 else "s"
-                dma(q, T.WM[sh + 4 + x::16, 0:V], T.landU[0:128 - sh, x * M:(x + 1) * M], "upu1", K("landU"), K("WM", "u%d" % x))
-                dma(q, T.WM[4 + x:sh:16, 0:V], T.landU[128 - sh:128, x * M:(x + 1) * M], "upu1", K("landU"), K("WM", "u%d" % (x + 2)))
+        def rows_up(q, buf, r, land, x, sem):
+            dma(q, T[buf][sh + r::16, 0:V], T[land][0:128 - sh, x * M:(x + 1) * M], sem, K(land), K(buf, "a%d" % r))
+            dma(q, T[buf][r:sh:16, 0:V], T[land][128 - sh:128, x * M:(x + 1) * M], sem, K(land), K(buf, "b%d" % r))
 
         def scatter_u(a, b):
             vop(lambda: g.vector.tensor_copy(T.WU[:, 0:V].indirect(T.ul[:, a:b]), T.ids[:, 16 * a:16 * b]),
                 K("ul") + IDK, K("WU"))
 
-        if rnd == 0:
-            scatter_u(0, 24)
-            constants_head()
-            scatter_u(24, 64)
-        else:
-            scatter_u(0, 64)
-        if rnd == 0:
-            vop(lambda: g.vector.tensor_tensor(T.tf[:], T.TP0[:, 0:M], T.TP0[:, M:2 * M], A.add), K("TP0", 0, 1), K("tf"))
-            ts("kt", "tf", 4096.0, A.mult, 1024.0, A.add)
-        else:
-            cp("uf", p(0, 0))
-            claim("K1", "y")
-            dma("y", row("K1", 0), T.kt[:], "upk" + R, K("kt"), K3("K1"))
-        conv("E45", [("WM", 0)], M, 1, 0, WMK)
-        to16("uI", 0, M, 1, 0, K("uI"))
-        dma("y", row("WM", 2), T[TP][:, 0:M], "upt" + R, K(TP, 0), K("WM", "t0"))
-        dma("y", row("WM", 3), T[TP][:, M:2 * M], "upt" + R, K(TP, 1), K("WM", "t1"))
-        arrive(landF, nxt, "ar_t" + R)
-        dma("y", row("WM", 0), T[landF][:, 0:M], "upf" + R, K(landF), K("WM", "f0"))
-        dma("y", row("WM", 1), T[landF][:, M:2 * M], "upf" + R, K(landF), K("WM", "f1"))
-        if rnd == 0:
-            op("s", lambda: g.scalar.activation(T.K1[:], T.ids[:], F.Copy), IDK, K3("K1"))
-            dma("y", row("K1", 0), T.kt[:], "upk" + R, K("kt"), K3("K1"))
-            constants_doubling()
-        scatter_u(64, M)
-        claim("OB", "s")
-        for c, (a, b) in enumerate(CH):
-            gather("s", "OB", "WM", V, "uI", 0, a, b, WMK + K("uI"), K("OB", c))
-            conv("E01", [("OB", 16 * a)], 64, c, 0, K("OB", c))
-        for c, (a, b) in enumerate(CH):
-            to16("fI", a, b, c, 0, K("fI", c))
-        claim("OC", "vs")
-        for q, a, b in QUARTERS:
-            gather(q, "OC", "WU", V, "fI", 0, a, b, K("WU") + chunks("fI", a, b), K("OC", a))
-            if q == "s":
-                conv("E01", [("OC", 16 * (b - 96))], 96, b // 96 - 1, 0, K("OC", b - 96, a))
-        to16("sI", 0, 96, 0, 0, K("sI", 0))
-
         def prefill(j, c):
             D = "D%d" % (j % 2)
-            dma("y", T[D][0::16, 1024 * c:1024 * c + 1024], T.CN[:, 64 * j:64 * j + 64], "pre%d" % (3 * (j % 2) + c),
-                K("CN", j), K(D, c))
+            dma("y", T[D][0::16, 1024 * c:1024 * c + 1024], T.CN[j::16, :], "pre%d" % (3 * (j % 2) + c),
+                K("CN", 0, 1, 2, 3), K(D, c))
 
         def accumulate(j, c):
             D, Kj = "D%d" % (j % 2), "K%d" % (j % 2)
             dma("g", T[D][0::16, 1024 * c:1024 * c + 1024], T[Kj][0::16, 1024 * c:1024 * c + 1024],
                 "acc%d" % (3 * (j % 2) + c), K(Kj, c), K(D, c), accum_op=A.add)
 
-        claim("D0", "y")
-        for j in range(2):
-            for c in range(3):
-                prefill(j, c)
-        SK = [K("sI", 0), K("sI", 0, 1), K("sI", 1)]
+        def prefill_first():
+            claim("D0", "y")
+            for j in range(2):
+                for c in range(3):
+                    prefill(j, c)
+
+        if rnd == 0:
+            constants_doubling()
+            scatter_u(0, 72)
+            conv("E45", [("WM", 0)], M, 1, 0, WMK)
+            to16("uI", 0, M, 1, 0, K("uI"))
+            arrive("landF", nxt, "ar_t0")
+            for r in range(2):
+                dma("y", row("WM", r), T.landF[:, r * M:(r + 1) * M], "upf", K("landF"), K("WM", "f%d" % r))
+            dma("y", row("K1", 0), T.tf[:], "upk" + R, K("tf"), K3("K1"))
+            prefill_first()
+            scatter_u(72, M)
+            for c, (a, b) in enumerate(CH):
+                gather("s", "OB", "WM", V, "uI", 0, a, b, WMK + K("uI"), K("OB", c))
+                conv("E01", [("OB", 16 * a)], 64, c, 0, K("OB", c))
+            for c in range(2):
+                to16("fI", 64 * c, 64 * c + 64, c, 0, K("fI", c))
+            for c, (a, b) in enumerate(CH):
+                for q, a1 in (("v", a), ("s", a + 32)):
+                    gather(q, "OC", "WU", V, "fI", 0, a1, a1 + 32, K("WU") + K("fI", c), K("OC", a1))
+                if c == 0:
+                    to16("fI", 128, M, 2, 0, K("fI", 2))
+                conv("E01", [("OC", 16 * a)], 64, 3 + c, 0, K("OC", a, a + 32))
+            keys, keyk, tabs, tabk = "K1", K3("K1"), "WM", WMK
+        else:
+            arrive("landU", prv, "ar_h0")
+            dma("y", row("K1", 0), T.tf[:], "upk1", K("tf"), K("K1", "k"))
+            for r in range(2):
+                dma("y", row("K1", 2 + r), T.TF[:, r * M:(r + 1) * M], "upk1", K("TF", r), K("K1", "t%d" % r))
+            claim("OC", "y")
+            for r in range(2):
+                rows_up("y", "OC", 4 + r, "landU", r, "upu1")
+            prefill_first()
+            conv("E45", [("OC", 0)], M, 1, 0, whole("OC"))
+            arrive("landK", prv, "ar_k")
+            arrive("landT", nxt, "ar_t1")
+            claim("OB", "vs")
+            for q, a, b in (("v", 0, 96), ("s", 96, M)):
+                gather(q, "OB", "WU", V, "landT", 0, a, b, whole("WU") + K("landT"), K("OB", a))
+            for q, a, b in (("v", 0, 64), ("s", 88, M), ("v", 64, 88)):
+                gather(q, "QW", "K1", V, "landK", 0, a, b, whole("K1") + K("landK"), K("QW", a))
+                if a == 0:
+                    to16("uI", 0, M, 1, 0, K("uI"))
+            claim("P1", "vs")
+            for c, (a, b) in enumerate(CH):
+                for q, a1 in (("v", a), ("s", a + 32)):
+                    gather(q, "P1", "OB", V, "uI", 0, a1, a1 + 32, whole("OB") + K("uI"), K("P1", "y%d" % a1))
+                conv("E23", [("P1", 16 * a)], 64, 3 + c, 0, K("P1", "y%d" % a, "y%d" % (a + 32)))
+            keys, keyk, tabs, tabk = "QW", whole("QW"), "QW", whole("QW")
         pend = []
 
         def flush():
@@ -428,26 +474,53 @@ def rank_program(g, core, T, topo):
                 j1, c1 = pend.pop(0)
                 to16("LL", M * j1 + 64 * c1, M * j1 + 64 * c1 + 64, c1, 0, K("LL", (j1, c1)))
 
+        def first_keys(a, b, c, tag):
+            vop(lambda: g.vector.tensor_scalar(T.K0[:, 16 * a:16 * b], T[keys][:, 0:V].indirect(T.sI[:, a:b]),
+                                               4096.0, 1024.0, A.mult, A.add), keyk + K("sI", c), K("K0", tag))
+
         claim("P0", "s")
         for c, (a, b) in enumerate(CH):
-            gather("s", "P0", "WM", V, "sI", 0, a, b, WMK + SK[c], K("P0", c))
-            gather("v", "K0", "K1", V, "sI", 0, a, b, K3("K1") + SK[c], K("K0", c))
             if c == 0:
-                to16("sI", 96, M, 1, 0, K("sI", 1))
+                to16("sI", 0, 64, 3, 0, K("sI", 0))
+                if rnd == 0:
+                    cp("wid16", "wid")
+                first_keys(0, 32, 0, "a")
+                to16("sI", 64, 128, 4, 0, K("sI", 1))
+                first_keys(32, 64, 0, 0)
+                to16("sI", 128, M, 5, 0, K("sI", 2))
+            else:
+                first_keys(a, b, c, c)
+            gather("s", "P0", tabs, V, "sI", 0, a, b, tabk + K("sI", c), K("P0", c))
             conv("E23", [("P0", 16 * a)], 64, c, 0, K("P0", c))
             accumulate(0, c)
             flush()
             pend.append((0, c))
-        for r in range(2 if last else 0, 4):
-            dma("y", T.sp[:, r * M:(r + 1) * M], row("OC", r), "sdn" + R, whole("OC"), K("sp", r))
         if rnd == 0:
-            cp("wid16", "wid")
             op("g", lambda: g.iota(T.vp[:, 0:M], [[16, M]], 0, 0, **fl), [], K("vp", 0))
             op("g", lambda: g.iota(T.gg[:], [[1, 8], [0, 16]], 0, 0, **fl), [], K("gg"))
-        for r in range(2):
-            dma("y", row("WM", 6 + r), row("OC", r + (2 if last else 0)), "srow" + R, whole("OC"), K("WM", "s%d" % r))
-            if rnd == 0:
-                dma("y", row("WM", 12 + r), T.vp[:, r * M:(r + 1) * M], "srow" + R, K("vp", r), K("WM", "v%d" % r))
+
+        side = []
+        if rnd == 0:
+            for r in range(2):
+                dma("y", row("WM", 10 + r), row("P0", 2 + r), "crow0", K3("P0"), K("WM", "c%d" % r))
+            for r in range(2):
+                side.append((T.HP[:, r * M:(r + 1) * M], row("WU", 2 + r), "wdn", K("WU"), K("HP", r)))
+            for r in range(4):
+                side.append((T.sp[:, r * M:(r + 1) * M], row("OC", r), "sdn" + R, whole("OC"), K("sp", r)))
+            for r in range(2):
+                side.append((row("WM", 6 + r), row("OC", r), "srow" + R, whole("OC"), K("WM", "s%d" % r)))
+                for x, at in (("uv", 4), ("wp", 8), ("vp", 12)):
+                    side.append((row("WM", at + r), T[x][:, r * M:(r + 1) * M], "srow" + R, K(x, r), K("WM", x[0] + str(r))))
+            side += loads
+        else:
+            claim("K1", "v")
+            claim("P1", "s")
+            for r in range(2):
+                dma("y", row("WM", 6 + r), row("P0", 6 + r), "crow1", K3("P0"), K("WM", "s%d" % r))
+            for r in range(2):
+                side.append((T.sp[:, (2 + r) * M:(3 + r) * M], row("WM", 6 + r), "sdn" + R, K("WM", "s%d" % r), K("sp", 2 + r)))
+                side.append((row("WM", 4 + r), row("OC", 4 + r), "srow" + R, whole("OC"), K("WM", "u%d" % r)))
+                side.append((T.uv[:, r * M:(r + 1) * M], row("OC", 4 + r), "uvd", whole("OC"), K("uv", r)))
 
         for j in range(STEPS):
             Pa, Pb = "P%d" % (j % 2), "P%d" % ((j + 1) % 2)
@@ -460,17 +533,20 @@ def rank_program(g, core, T, topo):
                 if j + 1 < STEPS:
                     accumulate(j + 1, c)
                 if j + 2 < STEPS:
-                    if rnd == 0 and c == 0:
-                        step_constant(j + 2)
                     prefill(j + 2, c)
-                if loads:
-                    out, in_, sem, key = loads.pop(0)
-                    before("y", K(Kb, c), [])
-                    dma("y", out, in_, sem, [], [key])
-                if (j, c) == (STEPS - 2, 0):
+                if side:
+                    dma("y", *side.pop(0))
+                if (rnd, j, c) == (0, 2, 0):
+                    send("HP", "landW", nxt, "rs_w", "ar_w", K("HP", 0, 1))
+                if (rnd, j, c) == (0, STEPS - 1, 0):
+                    arrive("landW", prv, "ar_w")
+                    before("y", [], K("WU"))
+                    for r in range(2):
+                        rows_up("y", "WU", 2 + r, "landW", r, "wup")
+                if (j, c) == (STEPS - 2, 1):
                     before("y", [], SLK)
-                    for r in (0, 12, 13):
-                        dma("y", T.SL[r::16, 0:ODD], T.zb[:], "clr" + R, K("zb", 0, 1), K("SL", r))
+                    for r in (12, 13, 14):
+                        dma("y", row("SL", r), T.zb[:], "clr" + R, K("zb"), K("SL", r))
                 flush()
                 gather("s", Pb, Pa, V, "LL", M * j, a, b, K3(Pa) + lk, K(Pb, c))
                 conv("E23", [(Pb, 16 * a)], 64, c, 0, K(Pb, c))
@@ -485,167 +561,253 @@ def rank_program(g, core, T, topo):
                        bias=1024.0)
                 flush()
             dma("y", T[lst][:], row(dst, 0), sem + R, whole(dst), K(lst))
-        op("s", lambda: g.scalar.activation(T.P1[:], T.WM[:, 0:V].indirect(T.wid16[:]), F.Identity, bias=cf(11), scale=cf(10)),
-           WMK + K("wid16") + K("cf", 10, 11), K3("P1"))
 
         if rnd == 0:
             constants_leaders()
-        sv = "sf" if last else "f1"
-        vop(lambda: g.vector.tensor_tensor(T[sv][:], T.sp[:, 2 * M:3 * M], T.sp[:, 3 * M:4 * M], A.add), K("sp", 2, 3), K(sv))
+            constants_sums()
+        sc = 2 if last else 0
+        lin(p(4, 1), pieces("Ib", "sp", 2))
         tt(p(6, 0), "KL", "AL", A.min)
-        cp("sv16", sv)
+        lin(p(4, 0), pieces("Ib", "uv", 0))
+        sa("uf", p(4, 0), F.Copy)
+        t_terms = term("Ip", "tf")
         if last:
-            unlabel("tf", "tf")
+            sa("f2", "tf", F.Identity, scale=1.0 / M, bias=-95.5 / M)
+            cp("i2", "f2")
         else:
-            vop(lambda: g.vector.tensor_tensor(T.sf[:], T.sp[:, 0:M], T.sp[:, M:2 * M], A.add), K("sp", 0, 1), K("sf"))
-        tt("i1", "BL", p(6, 0), A.min)
-        ts("i2", "i1", 12, A.arith_shift_right)
-        ts("di", "i1", 4095, A.bitwise_and)
-        tt(p(7, 1), "i2", "wid", A.is_equal)
-        vop(lambda: g.vector.tensor_tensor(T.ps5[:, M:2 * M], T.di[:], ap(p(7, 1)), A.mult), K("di") + [p(7, 1)], [p(5, 1)])
-        vop(lambda: g.vector.tensor_tensor_scan(T.Zb[:, 1:M + 1], T.ps5[:, M:2 * M], T.zer[:, 0:M], 0.0, A.add, A.add),
-            [p(5, 1)] + K("zer"), K("Zb", 1))
-        matmuls([(T.ps3[:, 0:2], T.TR[:], T.Zb[:, M - 1:M + 1])], K("TR") + K("Zb", 1), [p(3, 0)])
-        ts("i3", "di", 1, A.bitwise_and)
-        cp("lab16", "i2")
-        ts(p(6, 1), "i3", float(2 * ODD - 1), A.mult, -float(ODD), A.add)
-        vop(lambda: g.vector.tensor_scalar(T.i1[:], T.Zb[:, 0:M], T.ps3[:, 1:2], 1.0, A.add, A.add),
-            K("Zb", 0, 1) + [p(3, 0)], K("i1"))
-        ts("i3", "i1", 1, A.arith_shift_right)
-        tt(p(6, 0), "i1", p(6, 1), A.add)
-        tt(p(5, 0), "i3", p(6, 0), A.max)
-        vop(lambda: g.vector.tensor_copy(T.rh[:], T.ps5[:, 0:2 * M]), pk(5), K("rh"))
-        before("y", [], K3("P0"))
-        dma("y", row("P0", 8), T.rh[:, 0:M], "rec" + R, K("rh"), K("P0", "r0"))
-        dma("y", row("P0", 10), T.rh[:, M:2 * M], "rec" + R, K("rh"), K("P0", "r2"))
-        vop(lambda: g.vector.tensor_tensor(T.rl[:], T.ps5[:, 0:2 * M], T.rh[:], A.subtract), pk(5) + K("rh"), K("rl"))
-        dma("y", row("P0", 9), T.rl[:, 0:M], "rec" + R, K("rl"), K("P0", "r1"))
-        dma("y", row("P0", 11), T.rl[:, M:2 * M], "rec" + R, K("rl"), K("P0", "r3"))
-        ts("f1", p(6, 1), 0.0, A.is_lt, float(V), A.mult)
-        tt("bt", "tf", "sf", A.subtract)
-        tt("il", "f1", p(7, 1), A.mult)
-        tt("pre", "il", "di", A.subtract)
+            claim("K1", "y")
+            for r in range(2):
+                dma("y", row("K1", 6 + r), T.vf[:, r * M:(r + 1) * M], "vup", K("vf"), K("K1", "v%d" % r))
         if rnd == 0:
             constants_votes()
+        key, own = p(5, 1), p(5, 0)
+        off = T.ps3[:, 1:2]
+        tt(key, "BL", p(6, 0), A.min)
+        tt("i1", "BL", p(6, 0), A.min)
         if last:
-            unlabel("uf", "uf")
-        claim("OB", "vs")
-        for q, a, b in QUARTERS:
-            gather(q, "OB", "P0", V, "lab16", 0, a, b, whole("P0") + K("lab16"), K("OB", a))
-            if q == "s":
-                conv("Eo", [("OB", 16 * (b - 96))], 96, 6, b - 96, K("OB", b - 96, a))
-                conv("EC", [("OB", 16 * (b - 96))], 96, 7, b - 96, K("OB", b - 96, a))
+            ts("f4", "i2", -float(V - 1), A.mult)
+            t_terms = term("I16", "tf") + term("Ip", "f4")
+        tt(own, "w4k", key, A.max)
+        ts("i3", "i1", 1, A.bitwise_and)
+        vop(lambda: g.vector.tensor_tensor_scan(T.Zb[:], ap(own), T.w4k[:], 0.0, A.add, A.subtract),
+            [own] + K("w4k"), K("Zb"))
+        matmuls([(T.ps3[:, 0:2], T.TR[:], T.Zb[:, M - 2:M])], K("TR") + K("Zb"), [p(3, 0)])
+        lin(p(1, 1), t_terms + pieces("Im", "sp", sc))
+        tt("f1", own, "w4k", A.subtract)
+        ts(p(7, 0), "i3", 5120.0, A.mult, float(V), A.add)
+        ts(p(6, 1), "i3", float(ODD + HALF), A.mult, -float(HALF), A.add)
+        tt(p(7, 1), p(7, 0), "f1", A.subtract)
+        tt("zo", "Zb", "f1", A.add)
+        ts("fg", p(7, 1), float(V), A.is_ge)
+        dma("y", row("WM", 14), T.fg[:], "flg" + R, K("fg"), K("WM", "g"))
+        tt("za", "Zb", p(6, 1), A.add)
+        high("r2", p(7, 0), "f1", A.subtract)
+        before("y", [], K3("P0"))
+        dma("y", row("P0", 10), T.r2[:, 0:M], "rec" + R, K("r2", 0), K("P0", "r2"))
+        ts(p(6, 0), "zo", off, A.add, rd=[p(3, 0)])
+        ts("f3", "za", off, A.add, 2.0, A.mult, rd=[p(3, 0)])
+        low("r2", p(7, 1))
+        dma("y", row("P0", 11), T.r2[:, M:2 * M], "rec" + R, K("r2", 1), K("P0", "r3"))
+        ts("i2", "i1", 12, A.arith_shift_right)
+        high("r1", "f3", p(6, 0), A.max)
+        dma("y", row("P0", 8), T.r1[:, 0:M], "rec" + R, K("r1", 0), K("P0", "r0"))
+        tt(p(6, 1), "f3", p(6, 0), A.max)
+        ts("di", "i1", 4095, A.bitwise_and)
+        cp("lab16", "i2")
+        low("r1", p(6, 1))
+        dma("y", row("P0", 9), T.r1[:, M:2 * M], "rec" + R, K("r1", 1), K("P0", "r1"))
+        ts("hd", "di", -1.0, A.mult, float(HALF), A.add)
+        cp("sv16", p(4, 1))
 
-        mh, ce = p(6, 0), p(7, 0)
-        tt(p(5, 0), mh, "di", A.is_ge)
-        ts("w1", mh, -1.0, A.mult, float(HALF), A.add)
-        ts("ev", ce, float(ODD), A.is_lt)
-        tt(p(5, 1), "pre", ce, A.add)
-        tt("f4", "w1", "ev", A.mult)
-        tt("f1", "f4", p(5, 0), A.mult)
-        tt("f3", "f1", p(5, 1), A.add)
-        cp("sl16", "f3")
-        vop(lambda: g.vector.tensor_copy(T.SL[:, 0:SLW].indirect(T.sl16[:]), T.P1[:]), K("sl16") + K3("P1"), SLK)
-        ts(p(6, 1), p(5, 0), -2.0, A.mult, 1.0, A.add)
+        def load_rows(a, b):
+            gather("s", "P1", "WM", V, "wid16", 0, a, b, WMK + K("wid16"), K("P1", "r%d" % a))
+
+        claim("P1", "s")
+        load_rows(0, 64)
+        load_rows(64, 96)
+
+        rb, ra = p(6, 0), p(7, 0)
+
+        def records(c, parts):
+            a, b = CH[c]
+            for q, a1, b1 in parts:
+                gather(q, "OB", "P0", V, "lab16", 0, a1, b1, whole("P0") + K("lab16"), K("OB", a1))
+            rd = K("OB", *[x[1] for x in parts])
+            conv("EBh", [("OB", 16 * a)], b - a, 6, a, rd)
+            conv("EA", [("OB", 16 * a)], b - a, 7, a, rd, plus=term("Ip", "hd"))
+
+        def slot_calls(cols):
+            return [lambda: tt("f2", rb, "hd", A.is_le, cols), lambda: tt("up", rb, "f2", A.mult, cols),
+                    lambda: tt("f3", ra, "up", A.add, cols), lambda: ts("sl16", "f3", 0.25 - HALF, A.add, cols=cols)]
+
+        def sort(a, b, rows):
+            vop(lambda: g.vector.tensor_copy(T.SL[:, 0:SLW].indirect(T.sl16[:, a:b]), T.P1[:, 16 * a:16 * b]),
+                chunks("sl16", a, b) + K("P1", *["r%d" % x for x in rows]), SLK)
+
+        claim("OB", "vs")
+        records(0, [("v", 0, 32), ("s", 32, 64)])
+        for call in slot_calls(CH[0]):
+            call()
+        records(1, [("s", 64, 128)])
+        records(2, [("s", 128, M)])
+        load_rows(96, 128)
+        sa("Bs", rb, F.Copy)
+        sa("sg", "Bs", F.Sign, bias=-2048.0)
+        sa("zz", "Bs", F.Relu, bias=-2560.0)
+        lin(p(0, 1), term("Ip", "Bs") + term("In", "hd") + term("It", "sg"))
+        sa("od", "sg", F.Identity, scale=0.5, bias=0.5)
+        sa("mh", "zz", F.Identity, scale=-1.0, bias=float(HALF))
+        sa("st", p(0, 1), F.Sign, bias=-1280.25)
+        sa("t0s", p(0, 1), F.Copy)
+        load_rows(128, M)
+        rest = slot_calls((64, M))
+        sort(0, 40, [0])
+        rest[0]()
+        sort(40, 64, [0])
+        rest[1]()
+        tt("tm", "od", p(1, 1), A.mult)
+        rest[2]()
+        tt("mm", "mh", "st", A.mult)
+        rest[3]()
+        lin(p(2, 0), term("Ip", "f3") + term("Ip", "mm") + term("Iq", "sg"))
+        tt("f1", "t0s", ra, A.add)
+        lin(p(7, 1), term("Ip", "tm") + pieces("Ib", "sp", sc))
+        sort(64, 128, [64, 96])
+        ts("hs16", p(2, 0), -float(HALF), A.add)
+        ts("es16", "f1", 0.25 - 1280 - HALF - 1, A.add, float(HALF), A.min)
+        sort(128, M, [128])
 
         conv("Ev", [("SL", HALF)], 96, 1, 0, SLK)
-        conv("Ev", [("SL", 0), ("SL", V)], 96, 0, 0, SLK)
+        conv("Ev", [("SL", 0)], 96, 0, 0, SLK)
         for c in range(3):
             matmuls([(T["ps%d" % (3 + c)][:], T.FB[:], T.SL[:, 512 * c:512 * c + 512])], K("FB") + SLK, pk(3 + c))
-        tt("f2", "f4", mh, A.add)
-        tt(p(7, 1), "di", mh, A.is_equal)
-        tt("f1", "f2", p(6, 1), A.mult)
-        to16("row16", 96, M, 1, 0, K("row16", 1))
-        for c in range(3):
-            src = T.xs[:, 0:V].indirect(T.row16[:, 96 + 32 * c:128 + 32 * c])
-            op("s", lambda: g.scalar.activation(T.xa[:, 512 * c:512 * c + 512], src, F.Copy),
-               XK + K("row16", 1), K("xa", c))
-        ts(p(6, 1), p(7, 1), float(V), A.mult, -0.25, A.add)
-        tt(p(7, 1), "f3", "il", A.subtract)
-        tt("f2", "f1", p(6, 1), A.add)
-        tt("f5", "f2", p(7, 1), A.add)
-        ts("odd", ce, float(ODD), A.is_ge)
-        cp("i1", "f5")
-        tt("f1", "w1", ce, A.add)
-        cp("hs16", "i1")
-        ts("es16", "f1", -float(HALF + 1), A.add, float(HALF - 1), A.min)
-        to16("row16", 0, 96, 0, 0, K("row16", 0))
 
-        def half(q, c):
-            a, b = CH[c]
-            gather(q, "OC", "SL", SLW, "hs16", 0, a, b, SLK + K("hs16"), K("OC", "c%d" % c))
+        def half(q, a, b):
+            gather(q, "OC", "SL", SLW, "hs16", 0, a, b, SLK + K("hs16"), K("OC", "c%d" % a))
 
-        def half_list(c):
-            conv("Eus", [("OC", 16 * CH[c][0])], 64, 6, CH[c][0], K("OC", "c%d" % c))
+        def half_list(E, out, own, a, b, parts):
+            conv(E, [("OC", 16 * a)], b - a, out[1], 256 * out[2] + a, K("OC", *["c%d" % x for x in parts]), plus=own)
 
-        claim("OC", "vs")
-        half("s", 0)
-        half_list(0)
-        for c in range(3):
-            s_ = slice(512 * c, 512 * c + 512)
+        def cols(c):
+            return slice(512 * c, 512 * c + 512)
+
+        def gap(c):
             src = T.xs[:, 0:V].indirect(T.row16[:, 32 * c:32 * c + 32])
-            vop(lambda: g.vector.tensor_tensor(T.xd[:, s_], src, T.xa[:, s_], A.subtract),
+            vop(lambda: g.vector.tensor_tensor(T.xd[:, cols(c)], src, T.xa[:, cols(c)], A.subtract),
                 XK + K("row16", 0) + K("xa", c), K("xd", c))
-            op("s", lambda: g.scalar.activation(T.xa[:, s_], T.xd[:, s_], F.Abs), K("xd", c), K("xa", c))
-        half("s", 1)
-        for c in range(3):
-            s_ = slice(512 * c, 512 * c + 512)
+            act(T.xa[:, cols(c)], T.xd[:, cols(c)], K("xd", c), K("xa", c), func=F.Abs)
+
+        def widest(c):
             init = 0.0 if c == 0 else T.xm[:, 512 * c - 1:512 * c]
-            vop(lambda: g.vector.tensor_tensor_scan(T.xm[:, s_], T["ps%d" % (3 + c)][:], T.xa[:, s_], init, A.mult, A.max),
+            vop(lambda: g.vector.tensor_tensor_scan(T.xm[:, cols(c)], T["ps%d" % (3 + c)][:], T.xa[:, cols(c)], init,
+                                                    A.mult, A.max),
                 pk(3 + c) + K("xa", c) + (K("xm", c - 1) if c else []), K("xm", c))
-            vop(lambda: g.vector.tensor_scalar(T.xd[:, s_], T.xm[:, s_], T.thf[:, 0:1], None, A.is_gt),
+
+        def vote(c):
+            vop(lambda: g.vector.tensor_scalar(T.xd[:, cols(c)], T.xm[:, cols(c)], T.thf[:, 0:1], None, A.is_gt),
                 K("xm", c) + K("thf"), K("xd", c))
-            matmuls([(T["ps%d" % c][:], T.BO[:], T.xd[:, s_])], K("BO") + K("xd", c), pk(c))
-            op("s", lambda: g.scalar.activation(T.dec[:, s_], T["ps%d" % c][:], F.Sign, bias=5.5, scale=cf(5)),
-               pk(c) + K("cf", 5), K("dec", c))
-        half("v", 2)
-        half_list(1)
-        half_list(2)
-        claim("OB", "vs")
-        cut = 128 if last else 112
-        for q, a, b in (("s", 0, 64), ("v", cut, M), ("s", 64, cut)):
-            gather(q, "OB", "dec", HALF, "es16", 0, a, b, K3("dec") + K("es16"), K("OB", a))
-            conv("Eh", [("OB", 16 * a)], b - a, 3, a, K("OB", a))
+            matmuls([(T["ps%d" % c][:], T.BO[:], T.xd[:, cols(c)])], K("BO") + K("xd", c), pk(c))
+
+        def verdict(c):
+            act(T.dec[:, cols(c)], T["ps%d" % c][:], pk(c) + K("cf", 5), K("dec", c), func=F.Sign, bias=5.5, scale=cf(5))
+
+        own_u, own_s = pieces("Im", "uv", 0), pieces("Im", "sp", sc)
         claim("OC", "vs")
-        cut = 144 if last else 152
-        for a, b in ((0, 88), (88, cut)):
-            gather("s", "OC", "OB", V, "sv16", 0, a, b, whole("OB") + K("sv16"), K("OC", a))
-        conv("Eh", [("OC", 0)], 88, 2, 0, K("OC", 0))
-        cp("i1", p(6, 0))
-        ts("i2", "i1", 4095, A.bitwise_and)
-        ts("i3", "i1", 12, A.arith_shift_right)
-        if last:
-            unlabel("f3", "i2")
-        tt(p(7, 0), "f3" if last else "i2", "uf", A.subtract)
-        tt("tn", "odd", p(3, 0), A.max)
-        tt(p(7, 1), "tn", p(7, 0), A.mult)
+        half("s", 0, 48)
+        half("v", 48, 80)
+        to16("row16", 96, M, 1, 0, K("row16", 1))
+        half("v", 80, 104)
+        for c in range(3):
+            act(T.xa[:, cols(c)], T.xs[:, 0:V].indirect(T.row16[:, 96 + 32 * c:128 + 32 * c]), XK + K("row16", 1), K("xa", c),
+                func=F.Copy)
+        to16("row16", 0, 96, 0, 0, K("row16", 0))
+        half("v", 104, 128)
+        early, late = (0, 128, [0, 48, 80, 104]), (128, M, [128, 138])
+        own_w = pieces("Im", "wp", 0)
+        half_list("E45", p(6, 0), own_u, *early)
+        half_list("E67", p(6, 1), own_s, *early)
         if not last:
-            tt(p(5, 0), "uf", p(7, 1), A.add)
-            split("HP", p(5, 0))
+            half_list("E89", p(7, 0), own_w, *early)
+        gap(0)
+        gap(1)
+        gap(2)
+        widest(0)
+        half("v", 128, 138)
+        widest(1)
+        vote(0)
+        widest(2)
+        vote(1)
+        vote(2)
+        half("v", 138, M)
+        for c in range(3):
+            verdict(c)
+        if not last:
+            half_list("Ecw", p(4, 0), [], *early)
+        half_list("E45", p(6, 0), own_u, *late)
+        if not last:
+            half_list("E89", p(7, 0), own_w, *late)
+            half_list("Ecw", p(4, 0), [], *late)
+        claim("OB", "vs")
+        for a, b in CH:
+            for q, a1 in (("v", a), ("s", a + 32)):
+                gather(q, "OB", "dec", HALF + 16, "es16", 0, a1, a1 + 32, K3("dec") + K("dec", "one") + K("es16"), K("OB", a1))
+            conv("Eh", [("OB", 16 * a)], 64, 3, a, K("OB", a, a + 32))
+        if not last:
+            tt("mm", "od", p(4, 0), A.mult)
+        cp("du", p(6, 0))
+        half_list("E67", p(6, 1), own_s, *late)
+        claim("P0", "vs")
+
+        def mirror(q, a, b):
+            gather(q, "P0", "OB", V, "sv16", 0, a, b, whole("OB") + K("sv16"), K("P0", a))
+
+        def mirror_list(a, parts):
+            conv("Eh", [("P0", 16 * a)], 64, 2, a, K("P0", *parts))
+
+        mirror("s", 0, 64)
+        if not last:
+            mirror("v", 64, 128)
+            mirror("s", 128, 164)
+            mirror("v", 164, M)
+            for a, parts in ((0, [0]), (64, [64]), (128, [128, 164])):
+                mirror_list(a, parts)
+            tt(p(5, 0), "du", p(3, 0), A.mult)
+            tt("mh", "mm", p(7, 0), A.add)
+            cp("tn", p(3, 0))
+            tt(p(5, 1), "uf", p(5, 0), A.add)
+            high("HP", "uf", p(5, 0), A.add)
+            tt("zz", "mh", p(3, 0), A.mult)
+            tt("f1", "tn", p(2, 0), A.not_equal)
+            low("HP", p(5, 1))
             send("HP", "landU", nxt, "rs_h" + R, "ar_h" + R, K("HP", 0, 1))
+            lin(p(1, 0), term("t128", "wid") + term("t128", "zz"))
+            tt("f2", "f1", p(6, 1), A.mult)
+            tt("tf", "f2", p(7, 1), A.add)
+            high("TP", "f2", p(7, 1), A.add)
+            cp("ul", "tf")
+            send("ul", "landT", prv, "rs_t1", "ar_t1", K("ul"))
+            vop(lambda: g.vector.tensor_tensor(T.TF[:, M:2 * M], T.tf[:], T.TP[:, 0:M], A.subtract),
+                K("tf") + K("TP", 0), K("TF", 1))
+            act(T.TF[:, 0:M], T.TP[:, 0:M], K("TP", 0), K("TF", 0), func=F.Copy)
+            cp("fI", p(1, 0))
+            send("fI", "landK", nxt, "rs_k", "ar_k", K("fI"))
         else:
-            tt("hout", "uf", p(7, 1), A.add)
+            mirror("v", 64, 88)
+            mirror_list(0, [0])
+            tt(p(5, 0), "du", p(3, 0), A.mult)
+            mirror("s", 128, 176)
+            cp("tn", p(3, 0))
+            tt("hout", "uf", p(5, 0), A.add)
             send("hout", "landY", nxt, "rs_h" + R, "ar_h" + R, K("hout"))
-        gather("v", "OC", "OB", V, "sv16", 0, cut, M, whole("OB") + K("sv16"), K("OC", cut))
-        conv("Eh", [("OC", 16 * cut)], M - cut, 2, cut, K("OC", cut))
-        conv("Eh", [("OC", 16 * 88)], cut - 88, 2, 88, K("OC", 88))
-        tt(p(7, 0), "i3", "sf", A.subtract)
-        tt(p(7, 1), "bt", "odd", A.mult)
-        tt("ds", "ev", p(7, 0), A.mult)
-        tt("bt", "sf", p(7, 1), A.add)
-        tt(p(7, 1), "tn", p(2, 0), A.not_equal)
-        tt(p(7, 0), "ds", p(7, 1), A.mult)
-        if not last:
-            tt(p(7, 1), "bt", p(7, 0), A.add)
-            nx = str(rnd + 1)
-            split("TP" + nx, p(7, 1))
-            send("TP" + nx, "landF" + nx, prv, "rs_t" + nx, "ar_t" + nx, K("TP" + nx, 0, 1))
-            cp("tf", p(7, 1))
-            ts("kt", p(7, 1), 4096.0, A.mult, 1024.0, A.add)
-        else:
-            tt("tout", "bt", p(7, 0), A.add)
+            mirror("v", 88, 128)
+            mirror_list(64, [64, 88])
+            mirror("v", 176, M)
+            mirror_list(128, [128, 176])
+            tt("f1", "tn", p(2, 0), A.not_equal)
+            tt("f2", "f1", p(6, 1), A.mult)
+            tt("tout", "f2", p(7, 1), A.add)
             arrive("landY", prv, "ar_h" + R)
-            dma("s", T.yt[:], T.tout[:], "outt", K("tout"), K("yt"))
+            dma("s", T.yt[:], T.tout[:], "outt", K("tout"), K("yt", 0))
             dma("y", T.yu[sh:128, :], T.landY[0:128 - sh, :], "outu", K("landY"), K("yu", 0))
             dma("y", T.yu[0:sh, :], T.landY[128 - sh:128, :], "outu", K("landY"), K("yu", 1))
 

@@ -1,5 +1,4 @@
-import math
-from concourse.mybir import AluOpType as A, ActivationFunctionType as F
+from concourse.mybir import AluOpType as A, ActivationFunctionType as F, AxisListType as X
 
 V = 3072
 M = 192
@@ -8,8 +7,14 @@ GS = 3
 HALF = V // 2
 ODD = V
 SLW = ODD + V
-STEPS = 10
+STEPS = 9
+HOP = 1 << STEPS
+KR = 15
+LAB = 2048
+LVL = 1 << 23
 PIECE = 768
+LIMIT = 16 - 11 + 0.5
+STEEP = 64.0
 
 
 def _sb(cols, dt):
@@ -17,47 +22,47 @@ def _sb(cols, dt):
 
 
 SCRATCH = {
-    "xs": _sb(V, "bfloat16"), "ids": _sb(V, "bfloat16"), "WU": _sb(V, "bfloat16"), "WM": _sb(V, "bfloat16"),
+    "xs": _sb(V, "bfloat16"), "WM": _sb(V, "bfloat16"),
     "P0": _sb(V, "bfloat16"), "P1": _sb(V, "bfloat16"), "OB": _sb(V, "bfloat16"), "OC": _sb(V, "bfloat16"),
     "K0": _sb(V, "float32"), "K1": _sb(V, "float32"), "D0": _sb(V, "float32"), "D1": _sb(V, "float32"),
     "SL": _sb(SLW, "bfloat16"),
-    "xa": _sb(HALF, "bfloat16"), "xd": _sb(HALF, "bfloat16"), "xm": _sb(HALF, "bfloat16"), "dec": _sb(HALF + 16, "bfloat16"),
-    "CN": _sb(1024, "float32"), "cb": _sb(8, "bfloat16"),
+    "xa": _sb(HALF, "bfloat16"), "xd": _sb(HALF, "bfloat16"), "xm": _sb(HALF + 16, "bfloat16"),
+    "CN": _sb(1024, "float32"),
     "LL": _sb(M * (STEPS + 1), "uint16"),
     "tin": _sb(M, "int32"), "uin": _sb(M, "int32"), "thi": _sb(8, "int32"), "thf": _sb(8, "float32"),
     "TP": _sb(2 * M, "bfloat16"), "UP": _sb(2 * M, "bfloat16"), "HP": _sb(2 * M, "bfloat16"),
-    "landF": _sb(2 * M, "bfloat16"), "landU": _sb(2 * M, "bfloat16"), "landW": _sb(2 * M, "bfloat16"),
-    "wp": _sb(2 * M, "bfloat16"), "TF": _sb(2 * M, "float32"), "vf": _sb(2 * M, "float32"),
-    "QW": _sb(V, "float32"),
-    "landY": _sb(M, "float32"), "hout": _sb(M, "float32"), "tout": _sb(M, "float32"),
-    "idp": _sb(4 * M, "bfloat16"), "vp": _sb(2 * M, "bfloat16"), "ia": _sb(M, "float32"), "wid": _sb(M, "float32"),
-    "sp": _sb(4 * M, "bfloat16"), "r1": _sb(2 * M, "bfloat16"), "r2": _sb(2 * M, "bfloat16"), "uv": _sb(2 * M, "bfloat16"),
-    "sg": _sb(M, "bfloat16"), "fg": _sb(M, "bfloat16"),
+    "TV": _sb(3 * M, "bfloat16"), "landF": _sb(3 * M, "bfloat16"), "landU": _sb(2 * M, "bfloat16"), "landW": _sb(2 * M, "bfloat16"),
+    "landY": _sb(M, "float32"), "wp": _sb(2 * M, "bfloat16"), "TF": _sb(2 * M, "float32"), "vf": _sb(2 * M, "float32"),
+    "QW": _sb(V, "float32"), "t128": _sb(128, "float32"),
+    "idp": _sb(2 * M, "bfloat16"), "vp": _sb(2 * M, "bfloat16"), "ia": _sb(M, "float32"), "wid": _sb(M, "float32"),
+    "sp": _sb(4 * M, "bfloat16"), "uv": _sb(2 * M, "bfloat16"),
+    "r1": _sb(2 * M, "bfloat16"), "r2": _sb(2 * M, "bfloat16"), "r3": _sb(2 * M, "bfloat16"),
     "Ip": _sb(128, "float32"), "In": _sb(128, "float32"), "I16": _sb(128, "float32"),
-    "Zb": _sb(M, "float32"), "zer": _sb(256, "float32"), "zb": _sb(M, "bfloat16"),
-    "ci": _sb(8, "int32"), "cf": _sb(24, "float32"), "wt": _sb(8, "float32"), "i8": _sb(8, "float32"),
-    "cc": _sb(144, "float32"), "EB": _sb(144, "float32"), "gg": _sb(128, "float32"), "t128": _sb(128, "float32"),
-    "BO": _sb(128, "bfloat16"), "FB": _sb(128, "bfloat16"), "TR": _sb(128, "float32"),
+    "Zb": _sb(M + 8, "float32"), "zer": _sb(256, "float32"),
+    "ci": _sb(8, "int32"), "cf": _sb(32, "float32"), "wt": _sb(8, "float32"), "i8": _sb(32, "float32"),
+    "cc": _sb(144, "float32"), "EB": _sb(144, "float32"), "gg": _sb(128, "float32"),
+    "FB": _sb(128, "bfloat16"), "TR": _sb(128, "float32"),
 }
-for _n in ("E01", "E23", "E45", "E67", "E89", "Ecw", "EA", "EBh", "Ev", "Eh"):
+for _n in ("E0", "E1", "E01", "E23", "E45", "E67", "E89", "Ecw", "Era", "Erb", "Eq", "Ev", "Eh"):
     SCRATCH[_n] = _sb(144, "bfloat16")
-for _n in ("Iq", "It", "Ib", "Im"):
+for _n in ("Iq", "It", "Ib", "Im", "I2k"):
     SCRATCH[_n] = _sb(128, "bfloat16")
-for _n in ("ul", "uI", "fI", "sI", "lab16", "sl16", "hs16", "es16", "row16", "wid16", "sv16",
-           "landK", "landT"):
+for _n in ("sg", "fg", "zb", "tfx", "fgR", "landG", "pb"):
+    SCRATCH[_n] = _sb(M, "bfloat16")
+for _n in ("ul", "uI", "fI", "sI", "sl16", "hs16", "es16", "row16", "wid16", "sv16", "landT", "landK"):
     SCRATCH[_n] = _sb(M, "uint16")
 for _n in ("i1", "i2", "i3", "di"):
     SCRATCH[_n] = _sb(M, "int32")
-for _n in ("tf", "uf", "du", "mh", "t0s", "KL", "AL", "BL", "f1", "f2", "f3", "f4", "w4k", "za", "zo", "hd", "up", "Bs",
-           "zz", "st", "od", "mm", "tm", "tn"):
+for _n in ("tf", "uf", "mh", "KL", "AL", "BL", "f1", "f2", "f3", "f4", "za", "zo", "hd", "up",
+           "zz", "st", "od", "mm", "tm"):
     SCRATCH[_n] = _sb(M, "float32")
 for _b in range(8):
     SCRATCH["ps%d" % _b] = ("psum", [128, 512], "float32")
 
 _PER_ROUND = ["clr", "upk", "upu", "sdn", "srow", "crow", "kdn", "adn", "bdn", "rec", "flg",
               "rs_t", "rs_h", "ar_t", "ar_h"]
-SEMAPHORES = (["qv", "qs", "qt", "qg", "ldt", "ldu", "ldx", "ldth", "ldsl", "upid", "upt", "upf", "uvd", "vup", "wdn", "wup",
-               "rs_w", "ar_w", "rs_k", "ar_k", "outt", "outu"]
+SEMAPHORES = (["qv", "qs", "qt", "qg", "ldt", "ldu", "ldx", "ldth", "upid", "upt", "upf", "uvd", "vup", "wup",
+               "rs_w", "ar_w", "rs_g", "ar_g", "gup", "rs_k", "ar_k", "outt", "outu"]
               + ["acc%d" % i for i in range(6)] + ["pre%d" % i for i in range(6)]
               + [n + str(r) for r in range(RO) for n in _PER_ROUND])
 
@@ -128,16 +133,17 @@ def rank_program(g, core, T, topo):
         total[sem] = total.get(sem, 0) + 16
         after(q, (sem, None), rd, wr)
 
-    def send(src, dst, to, sem_l, sem_r, rd):
+    def send(src, dst, to, sem_l, sem_r, rd, cols=None):
         before("g", rd, [])
         rid, pid, _ = topo.addr(to)
-        g.remote_dma(T[dst][:], T[src][:], T.sem[sem_r], T.sem[sem_l], pid, rid, topo.mask(core, to))
+        a, b = cols or (0, SCRATCH[src][1][1])
+        g.remote_dma(T[dst][:, a:b], T[src][:, a:b], T.sem[sem_r], T.sem[sem_l], pid, rid, topo.mask(core, to))
         total[sem_l] = len(topo.engines(core, to))
         after("g", (sem_l, None), rd, [])
 
-    def arrive(buf, frm, sem_r):
+    def arrive(buf, frm, sem_r, *parts):
         total[sem_r] = len(topo.engines(frm, core))
-        for k in K(buf):
+        for k in K(buf, *parts):
             writer[k] = (sem_r, None)
 
     def K(name, *parts):
@@ -162,8 +168,8 @@ def rank_program(g, core, T, topo):
     def chunks(name, a, b, tag=None):
         return [(name, c if tag is None else (tag, c)) for c in range(a // 64, (b - 1) // 64 + 1)]
 
-    def p(b, s):
-        return ("ps", b, s)
+    def p(b, s, *part):
+        return ("ps", b, s) + part
 
     def ap(x, a=0, b=M):
         if isinstance(x, tuple):
@@ -205,11 +211,17 @@ def rank_program(g, core, T, topo):
     def pk(b):
         return [p(b, 0), p(b, 1)]
 
+    PART = {"ids": ("SL", 0), "WU": ("SL", V)}
+
+    def W(name, a, b, step=1, rows=slice(0, 128)):
+        name, at = PART.get(name, (name, 0))
+        return T[name][rows, at + a:at + b:step]
+
     def conv(E, srcs, n, b, col, rd, plus=()):
         out = T["ps%d" % b][:, col:col + n]
         a = col % 256
         matmuls([(out, T[I][:], T[x][:, c0 + a:c0 + a + n]) for (I, x, c0, _) in plus]
-                + [(out, T[E][:, 15 - i:143 - i], T[s][:, c0 + i:c0 + 16 * n:16]) for (s, c0) in srcs for i in range(16)],
+                + [(out, T[E][:, 15 - i:143 - i], W(s, c0 + i, c0 + 16 * n, 16)) for (s, c0) in srcs for i in range(16)],
                 rd + K(E) + [k for x in plus for k in x[3]], [p(b, col // 256)])
 
     def term(I, x):
@@ -221,32 +233,27 @@ def rank_program(g, core, T, topo):
     def lin(out, terms):
         matmuls([(ap(out), T[I][:], T[x][:, c0:c0 + M]) for (I, x, c0, _) in terms], [k for x in terms for k in x[3]], [out])
 
-    def gather(q, out, win, wcols, lst, l0, a, b, rd, wr, bias=None):
-        src = T[win][:, 0:wcols].indirect(T[lst][:, l0 + a:l0 + b])
-        dst = T[out][:, 16 * a:16 * b]
+    def gather(q, out, win, wcols, lst, l0, a, b, rd, wr, bias=None, scale=1.0):
+        src = W(win, 0, wcols).indirect(T[lst][:, l0 + a:l0 + b])
+        dst = W(out, 16 * a, 16 * b)
         if q == "s":
             if bias is None:
                 op("s", lambda: g.scalar.activation(dst, src, F.Copy), rd, wr)
             else:
-                op("s", lambda: g.scalar.activation(dst, src, F.Identity, bias=bias), rd, wr)
+                op("s", lambda: g.scalar.activation(dst, src, F.Identity, bias=bias, scale=scale), rd, wr)
         elif bias is None:
             op("v", lambda: g.vector.tensor_copy(dst, src), rd, wr)
         else:
-            op("v", lambda: g.vector.tensor_scalar(dst, src, bias, None, A.add), rd, wr)
+            op("v", lambda: g.vector.tensor_scalar(dst, src, scale, bias, A.mult, A.add), rd, wr)
 
     def to16(lst, a, b, bk, col, wr):
         vop(lambda: g.vector.tensor_copy(T[lst][:, a:b], T["ps%d" % bk][:, col:col + b - a]), [p(bk, 0)], wr)
 
     def row(buf, r):
-        return T[buf][r::16, 0:V]
+        return W(buf, 0, V, rows=slice(r, 128, 16))
 
-    def col(out, src, s1, o1, s2=None, o2=None):
-        a = T[src[0]][:, src[1]:src[1] + 1]
-        rd = K("wt") if src[0] == "wt" else K(src[0], src[1])
-        if o2 is None:
-            vop(lambda: g.vector.tensor_scalar(T.cf[:, out:out + 1], a, s1, None, o1), rd, K("cf", out))
-        else:
-            vop(lambda: g.vector.tensor_scalar(T.cf[:, out:out + 1], a, s1, s2, o1, o2), rd, K("cf", out))
+    def col(out, src):
+        vop(lambda: g.vector.tensor_copy(T.cf[:, out:out + 1], T.ci[:, src:src + 1]), K("ci", src), K("cf", out))
 
     def cf(i):
         return T.cf[:, i:i + 1]
@@ -264,22 +271,18 @@ def rank_program(g, core, T, topo):
         vop(lambda: g.vector.tensor_tensor(T[out][:], T[buf][:, c * M:(c + 1) * M], T[buf][:, (c + 1) * M:(c + 2) * M], A.add),
             rd, K(out))
 
-    WMK = K("WM", *[x + r for x in "ftuswcv" for r in "01"]) + K("WM", "g")
+    WMK = K("WM", *[x + r for x in "ftuswcv" for r in "01"]) + K("WM", "g", "h")
     IDK = K("ids", 0, 1, 2, 3)
     sh = 16 * GS
 
-    dma("y", T.uin[:], T.u0[:], "ldu", [], K("uin"))
-    dma("s", T.tin[:], T.t0[:], "ldt", [], K("tin"))
-    fl = {"allow_small_or_imprecise_dtypes": True}
-    op("g", lambda: g.iota(T.ci[:, 0:1], [[0, 1]], 0, 1), [], K("ci", 0))
-    op("g", lambda: g.iota(T.ia[:], [[1, 12], [0, 16]], 0, 0, **fl), [], K("ia"))
-    op("g", lambda: g.iota(T.idp[:, 0:M], [[0, 12], [M, 16]], 0, 0, **fl), [], K("idp", 0))
-    op("g", lambda: g.iota(T.idp[:, 3 * M:4 * M], [[0, 12], [1, 16]], 0, 0, **fl), [], K("idp", 3))
-    op("g", lambda: g.iota(T.cc[:], [[1, 144]], 0, -1, **fl), [], K("cc"))
-    op("g", lambda: g.iota(T.i8[:], [[1, 8]], 0, 0, **fl), [], K("i8"))
-    vop(lambda: g.vector.memset(T.zer[:], 0.0), [], K("zer"))
-    vop(lambda: g.vector.memset(T.ids[:], 1.0), [], IDK)
-    vop(lambda: g.vector.memset(T.dec[:, HALF:HALF + 16], 1.0), [], K("dec", "one"))
+    def cs(out, src, scale=1.0, bias=0.0, func=F.Identity):
+        if isinstance(src, tuple):
+            src, rd = wt(src[0]), K("wt")
+        else:
+            src, rd = cf(src), K("cf", src)
+        if isinstance(bias, int):
+            bias, rd = cf(bias), rd + K("cf", bias)
+        act(cf(out), src, rd, K("cf", out), func=func, scale=scale, bias=bias)
 
     def fill(buf, a, b, keys):
         for c in range(a, b):
@@ -287,101 +290,139 @@ def rank_program(g, core, T, topo):
         for k in keys:
             writer[k] = writer[(buf, "z%d" % (b - 1))]
 
-    fill("WM", 0, 12, WMK)
-    vop(lambda: g.vector.tensor_scalar(T.ci[:, 1:2], T.ci[:, 0:1], 15, None, A.bitwise_and), K("ci", 0), K("ci", 1))
-    col(0, ("ci", 1), 12.0, A.mult)
-    col(12, ("ci", 1), 1.0, A.mult)
-    act(T.cb[:, 0:1], cf(12), K("cf", 12), K("cb"), func=F.Exp, scale=math.log(2.0))
-    vop(lambda: g.vector.tensor_scalar(T.idp[:, M:2 * M], T.ia[:], cf(0), None, A.add), K("ia") + K("cf", 0), K("idp", 1))
-    vop(lambda: g.vector.tensor_scalar(T.idp[:, 2 * M:3 * M], T.ia[:], cf(0), 16.0, A.add, A.mult),
-        K("ia") + K("cf", 0), K("idp", 2))
-    for r in (0, 3, 1, 2):
-        dma("y", row("ids", r), T.idp[:, r * M:(r + 1) * M], "upid", K("idp", r), K("ids", r))
+    def pieces_in(pc, lo, hi, a, b):
+        vop(lambda: g.vector.tensor_scalar(T[pc][:, 0:M], T[lo][:], a, None, A.mult), K(lo), K(pc, 0))
+        vop(lambda: g.vector.tensor_scalar(T[pc][:, M:2 * M], T[hi][:], b, None, A.mult), K(hi), K(pc, 1))
 
-    def pieces_in(pc, lo, hi):
-        vop(lambda: g.vector.tensor_scalar(T[pc][:, 0:M], T[lo][:], float(M), None, A.mult), K(lo), K(pc, 0))
-        vop(lambda: g.vector.tensor_scalar(T[pc][:, M:2 * M], T[hi][:], 1.0, None, A.mult), K(hi), K(pc, 1))
+    dma("y", T.tin[:], T.t0[:], "ldt", [], K("tin"))
+    dma("y", T.uin[:], T.u0[:], "ldu", [], K("uin"))
+    fl = {"allow_small_or_imprecise_dtypes": True}
+    op("g", lambda: g.iota(T.ci[:, 0:1], [[0, 1]], 0, 1), [], K("ci", 0))
+    op("g", lambda: g.iota(T.ia[:], [[1, 12], [0, 16]], 0, 0, **fl), [], K("ia"))
+    op("g", lambda: g.iota(T.wid[:], [[1, M]], 0, 0, **fl), [], K("wid"))
+    op("g", lambda: g.iota(T.idp[:, 0:M], [[0, 12], [M, 16]], 0, 0, **fl), [], K("idp", 0))
+    op("g", lambda: g.iota(T.i8[:, 0:16], [[1, 16]], 0, 0, **fl), [], K("i8"))
+    op("g", lambda: g.iota(T.cc[:], [[1, 144]], 0, -1, **fl), [], K("cc"))
+    vop(lambda: g.vector.memset(T.zer[:], 0.0), [], K("zer"))
+    vop(lambda: g.vector.memset(W("ids", 0, 1024), 1.0), [], K("ids", "a"))
+    vop(lambda: g.vector.tensor_scalar(T.ci[:, 1:2], T.ci[:, 0:1], 15, None, A.bitwise_and), K("ci", 0), K("ci", 1))
+    vop(lambda: g.vector.memset(W("ids", 1024, 2048), 1.0), [], K("ids", "b"))
+    col(12, 1)
+    vop(lambda: g.vector.tensor_scalar(cf(0), T.ci[:, 1:2], 12.0, None, A.mult), K("ci", 1), K("cf", 0))
+    vop(lambda: g.vector.memset(W("ids", 2048, V), 1.0), [], IDK)
+    vop(lambda: g.vector.tensor_scalar(T.idp[:, M:2 * M], T.ia[:], cf(0), None, A.add), K("ia") + K("cf", 0), K("idp", 1))
+    fill("WM", 0, 4, [])
+    act(T.f1[:], T.wid[:], K("wid") + K("cf", 12), K("f1"), bias=cf(12), scale=16.0)
+    cs(1, 12, 1.0, -15.0)
+    cs(2, 12, -1.0, 0.5)
+    cs(6, 12, float(M))
+    cs(15, 12, 1.0, -14.0, F.Relu)
+    fill("WM", 4, 12, WMK)
+    for r in (1, 0):
+        dma("y", row("ids", r), T.idp[:, r * M:(r + 1) * M], "upid", K("idp", r), K("ids", r))
 
     ts("i1", "tin", 15, A.bitwise_and)
     ts("i2", "tin", 4, A.arith_shift_right)
+    vop(lambda: g.vector.tensor_tensor(T.TV[:, 2 * M:3 * M], T.tin[:], T.f1[:], A.is_equal), K("tin") + K("f1"), K("TV", 2))
+    pieces_in("TV", "i1", "i2", 1.0, 16.0)
+    send("TV", "landF", prv, "rs_t0", "ar_t0", K("TV", 0, 1, 2))
+    cp("ul", "uin")
     ts("i3", "uin", 15, A.bitwise_and)
-    pieces_in("TP", "i1", "i2")
-    send("TP", "landF", prv, "rs_t0", "ar_t0", K("TP", 0, 1))
-    for r in range(2):
-        dma("y", row("WM", 2 + r), T.TP[:, r * M:(r + 1) * M], "upt", K("TP", r), K("WM", "t%d" % r))
     ts("di", "uin", 4, A.arith_shift_right)
-    col(1, ("ci", 1), -1.0, A.mult, 15.0, A.add)
-    vop(lambda: g.vector.tensor_scalar(T.ci[:, 2:3], T.ci[:, 1:2], 1, None, A.arith_shift_right), K("ci", 1), K("ci", 2))
-    pieces_in("UP", "i3", "di")
-    col(2, ("ci", 2), 1.0, A.mult)
-    vop(lambda: g.vector.tensor_scalar(T.EB[:], T.cc[:], cf(1), None, A.is_equal), K("cc") + K("cf", 1), K("EB"))
-    pair_sum("uf", "UP", 0, K("UP", 0, 1))
-    vop(lambda: g.vector.tensor_scalar(T.wt[:], T.i8[:], cf(2), None, A.is_equal), K("i8") + K("cf", 2), K("wt"))
-    pair_sum("tf", "TP", 0, K("TP", 0, 1))
-    cp("ul", "uf")
-    dma("y", row("WM", 4), T.UP[:, 0:M], "upu0", K("UP", 0), K("WM", "u0"))
-    dma("y", row("WM", 5), T.UP[:, M:2 * M], "upu0", K("UP", 1), K("WM", "u1"))
+    vop(lambda: g.vector.tensor_scalar(T.i8[:, 16:32], T.i8[:, 0:16], cf(12), 1.0, A.is_lt, A.add),
+        K("i8") + K("cf", 12), K("i8", 1))
+    vop(lambda: g.vector.memset(T.xm[:, HALF:HALF + 16], -1.0), [], K("xm", "turn"))
+    vop(lambda: g.vector.memset(T.Zb[:, 0:8], 0.0), [], K("Zb", 0))
+    pieces_in("UP", "i3", "di", float(M), 1.0)
+    vop(lambda: g.vector.tensor_reduce(cf(14), T.i8[:, 16:32], X.X, A.mult, negate=True), K("i8", 1), K("cf", 14))
+    for r in range(2):
+        dma("y", row("WM", 4 + r), T.UP[:, r * M:(r + 1) * M], "upu0", K("UP", r), K("WM", "u%d" % r))
+    act(T.EB[:], T.cc[:], K("cc") + K("cf", 1), K("EB"), func=F.Abs, bias=cf(1))
+    act(T.wt[:], T.i8[:, 0:8], K("i8") + K("cf", 2), K("wt"), func=F.Abs, bias=cf(2), scale=2.0)
+    act(T.In[:], T.cc[:, 0:128], K("cc"), K("In"), func=F.Abs)
+    act(T.TP[:, 0:M], T.TV[:, 0:M], K("TV", 0), K("TP", 0), scale=float(M))
+    act(T.EB[:], T.EB[:], K("EB"), K("EB"), func=F.Relu, bias=1.0, scale=-1.0)
+    act(T.wt[:], T.wt[:], K("wt"), K("wt"), func=F.Relu, bias=1.5, scale=-1.0)
+    act(T.Ip[:], T.In[:], K("In"), K("Ip"), func=F.Relu, scale=-1.0, bias=1.0)
+    act(T.TP[:, M:2 * M], T.TV[:, M:2 * M], K("TV", 1), K("TP", 1), scale=1.0 / 16)
+    act(T.fgR[:], T.TV[:, 2 * M:3 * M], K("TV", 2), K("fgR"), scale=-float(LVL))
     make_e("E45", wt(2), K("wt"))
     make_e("E01", wt(0), K("wt"))
     make_e("E23", wt(1), K("wt"))
 
-    op("g", lambda: g.iota(T.wid[:], [[1, M]], 0, 0, **fl), [], K("wid"))
-    op("g", lambda: g.iota(T.D0[:], [[0, V]], 0, 0, **fl), [], K3("D0"))
-    dma("g", T.thi[:, 0:1], T.th[:], "ldth", [], K("thi"), allow_slow_non_contiguous=True)
     op("g", lambda: g.iota(T.D1[:], [[0, V]], 0, 0, **fl), [], K3("D1"))
-    loads = ([(T.SL[:, c:c + PIECE], T.x[:, c % V:c % V + PIECE], "ldsl", [], K("SL", "p%d" % c)) for c in range(0, SLW, PIECE)]
-             + [(T.xs[:, c:c + PIECE], T.x[:, c:c + PIECE], "ldx", [], K("xs", c)) for c in range(0, V, PIECE)])
-    SLK = [x[4][0] for x in loads if x[2] == "ldsl"] + K("SL", 12, 13, 14)
-    XK = [x[4][0] for x in loads if x[2] == "ldx"]
+    dma("g", T.thi[:, 0:1], T.th[:], "ldth", [], K("thi"), allow_slow_non_contiguous=True)
+    for c in range(2):
+        op("g", lambda: g.iota(T.D0[:, 1024 * c:1024 * c + 1024], [[0, 1024]], 0, 0, **fl), [], K("D0", c))
+    SLK = K("SL", 12, 13, 14)
+    XK = K("xs", *range(0, V, PIECE))
 
     def constants_doubling():
-        act(cf(14), T.cb[:, 0:1], K("cb"), K("cf", 14), scale=-1.0)
-        act(cf(6), cf(12), K("cf", 12), K("cf", 6), scale=float(M))
+        for name, scale in (("Ib", 1.0), ("I2k", float(LAB)), ("Im", -1.0)):
+            act(T[name][:], T.Ip[:], K("Ip"), K(name), scale=scale)
+        lin(p(6, 0), pieces("I2k", "TP", 0) + 2 * term("Ib", "fgR"))
+        lin(p(7, 0), pieces("Ib", "TP", 0))
+        cs(16, 15, -float(LVL + 1), 1.0)
+        cs(26, 12, -1.0, 1.0, F.Relu)
+        cs(27, 12, 1.0, -1.0, F.Abs)
         for c in range(4):
             act(T.CN[:, 256 * c:256 * c + 256], T.zer[:], K("zer") + K("cf", 14), K("CN", c), bias=cf(14))
-        fill("K1", 0, 12, K3("K1"))
-        act(T.zb[:], T.zer[:, 0:M], K("zer"), K("zb"))
+        act(T.tfx[:], T.TV[:, 2 * M:3 * M], K("TV", 2), K("tfx"), func=F.Copy)
         act(T.wp[:, M:2 * M], T.wid[:], K("wid"), K("wp", 1), func=F.Copy)
         act(T.wp[:, 0:M], T.zer[:, 0:M], K("zer") + K("cf", 6), K("wp", 0), bias=cf(6))
+        act(T.vp[:, 0:M], T.wid[:], K("wid"), K("vp", 0), scale=16.0)
+        act(T.vp[:, M:2 * M], T.zer[:, 0:M], K("zer") + K("cf", 12), K("vp", 1), bias=cf(12))
+        act(T.zb[:], T.zer[:, 0:M], K("zer"), K("zb"))
         act(T.uv[:, 0:M], T.UP[:, M:2 * M], K("UP", 1), K("uv", 0), scale=16.0)
         act(T.uv[:, M:2 * M], T.UP[:, 0:M], K("UP", 0), K("uv", 1), scale=1.0 / M)
         act(T.wid[:], T.wid[:], K("wid") + K("cf", 6), K("wid"), bias=cf(6))
-        act(T.vp[:, M:2 * M], T.zer[:, 0:M], K("zer") + K("cf", 12), K("vp", 1), bias=cf(12))
-        act(T.w4k[:], T.wid[:], K("wid"), K("w4k"), scale=4096.0)
+        cs(28, 27, -1.0, 1.0, F.Relu)
+        make_e("E0", cf(26), K("cf", 26))
+        sa("f2", p(6, 0), F.Identity, bias=float(LVL + HOP))
+        sa("tf", p(7, 0), F.Copy)
+        make_e("E1", cf(28), K("cf", 28))
+        fill("D0", 8, 12, K("D0", 2))
 
     def constants_leaders():
         vop(lambda: g.vector.tensor_scalar(T.ci[:, 3:4], T.ci[:, 0:1], 4, None, A.arith_shift_right), K("ci", 0), K("ci", 3))
         vop(lambda: g.vector.tensor_copy(T.thf[:, 0:1], T.thi[:, 0:1]), K("thi"), K("thf"))
-        col(3, ("ci", 3), 1.0, A.mult)
+        col(3, 3)
         vop(lambda: g.vector.tensor_scalar(T.gg[:], T.gg[:], cf(3), None, A.is_equal), K("gg") + K("cf", 3), K("gg"))
-        op("g", lambda: g.affine_select(T.TR[:], T.gg[:], [[1, 128]], A.is_gt, 0.0, 0, -1), K("gg"), K("TR"))
+        op("g", lambda: g.affine_select(T.TR[:], T.gg[:], [[-1, 128]], A.is_ge, 0.0, 0, 1), K("gg"), K("TR"))
+
         op("g", lambda: g.affine_select(T.t128[:], T.zer[:, 0:128], [[1, 128]], A.not_equal, 1.0, -sh, -1), K("zer"), K("t128"))
         op("g", lambda: g.affine_select(T.t128[:], T.t128[:], [[1, 128]], A.not_equal, 1.0, 128 - sh, -1), K("t128"), K("t128"))
 
     def constants_sums():
         act(T.vf[:], T.vp[:], K("vp", 0, 1), K("vf"), func=F.Copy)
-        act(T.In[:], T.cc[:, 0:128], K("cc"), K("In"), func=F.Abs)
-        act(cf(8), wt(4), K("wt"), K("cf", 8), scale=0.5)
-        act(T.Ip[:], T.In[:], K("In"), K("Ip"), func=F.Relu, scale=-1.0, bias=1.0)
-        act(cf(13), wt(5), K("wt"), K("cf", 13), scale=0.5)
-        for name, scale in (("Ib", 1.0), ("Im", -1.0), ("In", -1.0), ("It", -1280.0), ("Iq", -0.25), ("I16", 16.0)):
+        for name, scale in (("In", -1.0), ("It", 768.0), ("Iq", -0.25), ("I16", 16.0)):
             act(T[name][:], T.Ip[:], K("Ip"), K(name), scale=scale)
-        make_e("EBh", cf(13), K("cf", 13))
-        make_e("EA", cf(8), K("cf", 8))
+        cs(10, 12, 1.0, -14.0, F.Abs)
+        cs(20, (6,), -1.0)
+        cs(13, (5,), 0.5)
+        cs(11, 10, -1.0, 1.0, F.Relu)
+        cs(19, (5,), -1.0, 20)
+        cs(22, (5,), -0.5, 20)
+        cs(21, 11, float(HALF), 13)
+        cs(8, (4,), 0.5, 19)
+        cs(23, 11, -float(HALF), 22)
+        make_e("Erb", cf(21), K("cf", 21))
+        cs(24, 11, float(ODD), 8)
+        make_e("Eq", cf(23), K("cf", 23))
+        make_e("Era", cf(24), K("cf", 24))
 
     def constants_votes():
-        act(cf(9), wt(0), K("wt"), K("cf", 9), scale=0.5)
-        act(cf(10), cf(12), K("cf", 12), K("cf", 10), func=F.Abs, bias=-14.0)
-        act(cf(5), cf(12), K("wt") + K("cf", 12), K("cf", 5), scale=wt(0), bias=-1.0)
-        act(cf(11), cf(10), K("cf", 10), K("cf", 11), func=F.Relu, scale=-1.0, bias=1.0)
+        act(cf(5), T.thf[:, 0:1], K("thf"), K("cf", 5), scale=-STEEP, bias=-0.5 * STEEP)
+        cs(25, (4,), -1.0)
         make_e("Ev", wt(6), K("wt"))
         make_e("E67", wt(3), K("wt"))
-        make_e("Eh", cf(9), K("cf", 9))
-        act(T.BO[:], T.gg[:], K("gg"), K("BO"))
+        make_e("Eh", 1.0, [])
+        cs(7, (5,), 1.0, 25)
         act(T.FB[:], T.gg[:], K("gg") + K("cf", 11), K("FB"), scale=cf(11))
-        act(cf(7), wt(4), K("wt"), K("cf", 7), scale=-1.0, bias=wt(5))
         make_e("E89", wt(4), K("wt"))
         make_e("Ecw", cf(7), K("cf", 7))
+        cs(17, 15, float(LAB - 1), 1.0)
+        cs(18, 15, float(LVL + HOP))
 
     def high(dst, a, b, o):
         vop(lambda: g.vector.tensor_tensor(T[dst][:, 0:M], ap(a), ap(b), o), ky(a) + ky(b), K(dst, 0))
@@ -400,73 +441,94 @@ def rank_program(g, core, T, topo):
             dma(q, T[buf][r:sh:16, 0:V], T[land][128 - sh:128, x * M:(x + 1) * M], sem, K(land), K(buf, "b%d" % r))
 
         def scatter_u(a, b):
-            vop(lambda: g.vector.tensor_copy(T.WU[:, 0:V].indirect(T.ul[:, a:b]), T.ids[:, 16 * a:16 * b]),
-                K("ul") + IDK, K("WU"))
+            vop(lambda: g.vector.tensor_copy(W("WU", 0, V).indirect(T.ul[:, a:b]), W("ids", 16 * a, 16 * b)),
+                K("ul") + IDK, K("WU", 0))
 
         def prefill(j, c):
             D = "D%d" % (j % 2)
-            dma("y", T[D][0::16, 1024 * c:1024 * c + 1024], T.CN[j::16, :], "pre%d" % (3 * (j % 2) + c),
+            dma("y", T[D][KR::16, 1024 * c:1024 * c + 1024], T.CN[j::16, :], "pre%d" % (3 * (j % 2) + c),
                 K("CN", 0, 1, 2, 3), K(D, c))
 
         def accumulate(j, c):
             D, Kj = "D%d" % (j % 2), "K%d" % (j % 2)
-            dma("g", T[D][0::16, 1024 * c:1024 * c + 1024], T[Kj][0::16, 1024 * c:1024 * c + 1024],
+            dma("g", T[D][KR::16, 1024 * c:1024 * c + 1024], T[Kj][KR::16, 1024 * c:1024 * c + 1024],
                 "acc%d" % (3 * (j % 2) + c), K(Kj, c), K(D, c), accum_op=A.add)
 
-        def prefill_first():
-            claim("D0", "y")
-            for j in range(2):
-                for c in range(3):
-                    prefill(j, c)
+        def prefill_all(j):
+            for c in range(3):
+                prefill(j, c)
 
         if rnd == 0:
-            constants_doubling()
-            scatter_u(0, 72)
+            scatter_u(0, 112)
             conv("E45", [("WM", 0)], M, 1, 0, WMK)
             to16("uI", 0, M, 1, 0, K("uI"))
+            constants_doubling()
             arrive("landF", nxt, "ar_t0")
-            for r in range(2):
-                dma("y", row("WM", r), T.landF[:, r * M:(r + 1) * M], "upf", K("landF"), K("WM", "f%d" % r))
-            dma("y", row("K1", 0), T.tf[:], "upk" + R, K("tf"), K3("K1"))
-            prefill_first()
-            scatter_u(72, M)
-            for c, (a, b) in enumerate(CH):
-                gather("s", "OB", "WM", V, "uI", 0, a, b, WMK + K("uI"), K("OB", c))
-                conv("E01", [("OB", 16 * a)], 64, c, 0, K("OB", c))
+            for r, (at, key) in enumerate(((0, "f0"), (1, "f1"), (KR, "h"))):
+                dma("y", row("WM", at), T.landF[:, r * M:(r + 1) * M], "upf", K("landF"), K("WM", key))
+            scatter_u(112, M)
+
+            def f_of_u(q, a, b):
+                gather(q, "OB", "WM", V, "uI", 0, a, b, WMK + K("uI") + K("cf", 16), K("OB", a), bias=0.0, scale=cf(16))
+
+            def s_of(q, a, b):
+                gather(q, "OC", "WU", V, "fI", 0, a, b, K("WU", 0) + chunks("fI", a, b), K("OC", a))
+
             for c in range(2):
-                to16("fI", 64 * c, 64 * c + 64, c, 0, K("fI", c))
+                f_of_u("s", 64 * c, 64 * c + 64)
+                conv("E01", [("OB", 1024 * c)], 64, c, 0, K("OB", 64 * c))
+            f_of_u("s", 128, 144)
+            f_of_u("v", 144, M)
+            conv("E01", [("OB", 2048)], 64, 2, 0, K("OB", 128, 144))
+            dma("y", row("D1", KR), T.f2[:], "upk" + R, K("f2"), K3("D1"))
+            for r in range(2):
+                dma("y", row("ids", 2 + r), T.TP[:, r * M:(r + 1) * M], "upt", K("TP", r), K("ids", 2 + r))
+            for c in (2, 0, 1):
+                prefill(0, c)
+            to16("fI", 0, 64, 0, 0, K("fI", 0))
+            cp("wid16", "wid")
+            to16("fI", 64, 128, 1, 0, K("fI", 1))
             for c, (a, b) in enumerate(CH):
-                for q, a1 in (("v", a), ("s", a + 32)):
-                    gather(q, "OC", "WU", V, "fI", 0, a1, a1 + 32, K("WU") + K("fI", c), K("OC", a1))
+                s_of("v", a, a + 32)
+                s_of("s", a + 32, b)
                 if c == 0:
                     to16("fI", 128, M, 2, 0, K("fI", 2))
                 conv("E01", [("OC", 16 * a)], 64, 3 + c, 0, K("OC", a, a + 32))
-            keys, keyk, tabs, tabk = "K1", K3("K1"), "WM", WMK
+            keys, keyk, tabs, tabk = "D1", K3("D1"), "ids", IDK
+            marks, markk = "OB", [K("OB", 0), K("OB", 64), K("OB", 128, 144)]
         else:
-            arrive("landU", prv, "ar_h0")
-            dma("y", row("K1", 0), T.tf[:], "upk1", K("tf"), K("K1", "k"))
-            for r in range(2):
-                dma("y", row("K1", 2 + r), T.TF[:, r * M:(r + 1) * M], "upk1", K("TF", r), K("K1", "t%d" % r))
+            arrive("landK", prv, "ar_k")
+            arrive("landT", nxt, "ar_t1")
             claim("OC", "y")
             for r in range(2):
                 rows_up("y", "OC", 4 + r, "landU", r, "upu1")
-            prefill_first()
-            conv("E45", [("OC", 0)], M, 1, 0, whole("OC"))
-            arrive("landK", prv, "ar_k")
-            arrive("landT", nxt, "ar_t1")
+            for c, (a, b) in enumerate(CH):
+                conv("E45", [("OC", 16 * a)], 64, c, 0, whole("OC"))
             claim("OB", "vs")
             for q, a, b in (("v", 0, 96), ("s", 96, M)):
-                gather(q, "OB", "WU", V, "landT", 0, a, b, whole("WU") + K("landT"), K("OB", a))
-            for q, a, b in (("v", 0, 64), ("s", 88, M), ("v", 64, 88)):
-                gather(q, "QW", "K1", V, "landK", 0, a, b, whole("K1") + K("landK"), K("QW", a))
-                if a == 0:
-                    to16("uI", 0, M, 1, 0, K("uI"))
-            claim("P1", "vs")
+                gather(q, "OB", "P1", V, "landT", 0, a, b, whole("P1") + K("landT"), K("OB", a))
+            for q in "vs":
+                before(q, [], SLK)
+
+            def tables(q, a, b):
+                gather(q, "QW", "K1", V, "landK", 0, a, b, whole("K1") + K("landK") + K("cf", 17, 18), K("QW", a),
+                       bias=cf(18), scale=cf(17))
+
+            tables("v", 0, 40)
+            tables("s", 64, 144)
+            for c in range(3):
+                to16("uI", 64 * c, 64 * c + 64, c, 0, K("uI", c))
+            tables("v", 40, 64)
             for c, (a, b) in enumerate(CH):
                 for q, a1 in (("v", a), ("s", a + 32)):
-                    gather(q, "P1", "OB", V, "uI", 0, a1, a1 + 32, whole("OB") + K("uI"), K("P1", "y%d" % a1))
-                conv("E23", [("P1", 16 * a)], 64, 3 + c, 0, K("P1", "y%d" % a, "y%d" % (a + 32)))
+                    gather(q, "ids", "OB", V, "uI", 0, a1, a1 + 32, whole("OB") + K("uI", c), K("ids", "y%d" % a1))
+                conv("E23", [("ids", 16 * a)], 64, 3 + c, 0, K("ids", "y%d" % a, "y%d" % (a + 32)))
+            tables("v", 144, 168)
+            tables("s", 168, M)
             keys, keyk, tabs, tabk = "QW", whole("QW"), "QW", whole("QW")
+            marks, markk = "ids", [K("ids", "y%d" % a, "y%d" % (a + 32)) for a, b in CH]
+            claim("K0", "v")
+        sb = 3
         pend = []
 
         def flush():
@@ -475,19 +537,18 @@ def rank_program(g, core, T, topo):
                 to16("LL", M * j1 + 64 * c1, M * j1 + 64 * c1 + 64, c1, 0, K("LL", (j1, c1)))
 
         def first_keys(a, b, c, tag):
-            vop(lambda: g.vector.tensor_scalar(T.K0[:, 16 * a:16 * b], T[keys][:, 0:V].indirect(T.sI[:, a:b]),
-                                               4096.0, 1024.0, A.mult, A.add), keyk + K("sI", c), K("K0", tag))
+            vop(lambda: g.vector.tensor_tensor(T.K0[:, 16 * a:16 * b], T[keys][:, 0:V].indirect(T.sI[:, a:b]),
+                                               W(marks, 16 * a, 16 * b), A.add),
+                keyk + K("sI", c) + markk[c], K("K0", tag))
 
         claim("P0", "s")
         for c, (a, b) in enumerate(CH):
             if c == 0:
-                to16("sI", 0, 64, 3, 0, K("sI", 0))
-                if rnd == 0:
-                    cp("wid16", "wid")
+                to16("sI", 0, 64, sb, 0, K("sI", 0))
                 first_keys(0, 32, 0, "a")
-                to16("sI", 64, 128, 4, 0, K("sI", 1))
+                to16("sI", 64, 128, sb + 1, 0, K("sI", 1))
                 first_keys(32, 64, 0, 0)
-                to16("sI", 128, M, 5, 0, K("sI", 2))
+                to16("sI", 128, M, sb + 2, 0, K("sI", 2))
             else:
                 first_keys(a, b, c, c)
             gather("s", "P0", tabs, V, "sI", 0, a, b, tabk + K("sI", c), K("P0", c))
@@ -496,7 +557,7 @@ def rank_program(g, core, T, topo):
             flush()
             pend.append((0, c))
         if rnd == 0:
-            op("g", lambda: g.iota(T.vp[:, 0:M], [[16, M]], 0, 0, **fl), [], K("vp", 0))
+            prefill_all(1)
             op("g", lambda: g.iota(T.gg[:], [[1, 8], [0, 16]], 0, 0, **fl), [], K("gg"))
 
         side = []
@@ -504,14 +565,11 @@ def rank_program(g, core, T, topo):
             for r in range(2):
                 dma("y", row("WM", 10 + r), row("P0", 2 + r), "crow0", K3("P0"), K("WM", "c%d" % r))
             for r in range(2):
-                side.append((T.HP[:, r * M:(r + 1) * M], row("WU", 2 + r), "wdn", K("WU"), K("HP", r)))
-            for r in range(4):
                 side.append((T.sp[:, r * M:(r + 1) * M], row("OC", r), "sdn" + R, whole("OC"), K("sp", r)))
             for r in range(2):
                 side.append((row("WM", 6 + r), row("OC", r), "srow" + R, whole("OC"), K("WM", "s%d" % r)))
                 for x, at in (("uv", 4), ("wp", 8), ("vp", 12)):
                     side.append((row("WM", at + r), T[x][:, r * M:(r + 1) * M], "srow" + R, K(x, r), K("WM", x[0] + str(r))))
-            side += loads
         else:
             claim("K1", "v")
             claim("P1", "s")
@@ -534,90 +592,114 @@ def rank_program(g, core, T, topo):
                     accumulate(j + 1, c)
                 if j + 2 < STEPS:
                     prefill(j + 2, c)
-                if side:
+                if side and c < 2:
+                    before("y", K(Kb, c), [])
                     dma("y", *side.pop(0))
-                if (rnd, j, c) == (0, 2, 0):
-                    send("HP", "landW", nxt, "rs_w", "ar_w", K("HP", 0, 1))
-                if (rnd, j, c) == (0, STEPS - 1, 0):
-                    arrive("landW", prv, "ar_w")
-                    before("y", [], K("WU"))
-                    for r in range(2):
-                        rows_up("y", "WU", 2 + r, "landW", r, "wup")
-                if (j, c) == (STEPS - 2, 1):
-                    before("y", [], SLK)
+                if (j, c) == (STEPS - 1, 0):
+                    before("y", K(Kb, c), SLK)
+                    claim("ids", "y")
+                    claim("WU", "y")
                     for r in (12, 13, 14):
                         dma("y", row("SL", r), T.zb[:], "clr" + R, K("zb"), K("SL", r))
                 flush()
                 gather("s", Pb, Pa, V, "LL", M * j, a, b, K3(Pa) + lk, K(Pb, c))
                 conv("E23", [(Pb, 16 * a)], 64, c, 0, K(Pb, c))
                 pend.append((j + 1, c))
-        dma("y", T.KL[:], row("K0", 0), "kdn" + R, K3("K0"), K("KL"))
+                if rnd == 0 and j in (1, 3):
+                    conv("E%d" % (j // 2), [("WU", 16 * a)], 64, 6, a, K("WU", 0))
+                if rnd == 0 and j in (2, 4) and c == 1:
+                    act(T.HP[:, (j // 2 - 1) * M:j // 2 * M], ap(p(6, 0)), [p(6, 0)], K("HP", j // 2 - 1),
+                        scale=(1.0 / M, 16.0)[j // 2 - 1])
+        dma("y", T.KL[:], row("K1", KR), "kdn" + R, K3("K1"), K("KL"))
         for (dst, win, sem, lst, parts) in (
-                ("K1", "K0", "adn", "AL", [("v", 0, 64), ("s", 64, 128), ("v", 128, 160), ("s", 160, M)]),
-                ("D0", "K1", "bdn", "BL", [("v", 0, 96), ("s", 96, M)])):
+                ("K0", "K1", "adn", "AL", [("v", 0, 40), ("s", 64, 128), ("v", 40, 64), ("s", 128, 164), ("v", 164, M)]),
+                ("D0", "K0", "bdn", "BL", [("v", 0, 96), ("s", 96, M)])):
             claim(dst, "vs")
             for q, a, b in parts:
                 gather(q, dst, win, V, "LL", M * STEPS, a, b, whole(win) + chunks("LL", a, b, STEPS), K(dst, "at%d" % a),
-                       bias=1024.0)
+                       bias=float(HOP))
                 flush()
-            dma("y", T[lst][:], row(dst, 0), sem + R, whole(dst), K(lst))
+            dma("y", T[lst][:], row(dst, KR), sem + R, whole(dst), K(lst))
 
         if rnd == 0:
+            act(T.sp[:, 2 * M:3 * M], T.sp[:, M:2 * M], K("sp", 1), K("sp", 2), scale=16.0)
+            act(T.sp[:, 3 * M:4 * M], T.sp[:, 0:M], K("sp", 0), K("sp", 3), scale=1.0 / M)
             constants_leaders()
             constants_sums()
         sc = 2 if last else 0
+        own, base, fix, rest, lead = p(7, 0), p(7, 1), p(2, 0), p(5, 0), p(2, 1)
         lin(p(4, 1), pieces("Ib", "sp", 2))
         tt(p(6, 0), "KL", "AL", A.min)
+        lin(own, pieces("Ib", "wp", 0))
+        lin(base, pieces("I2k", "wp", 0) + term("Ib", "fgR"))
+        lin(fix, term("Ib", "tfx"))
         lin(p(4, 0), pieces("Ib", "uv", 0))
         sa("uf", p(4, 0), F.Copy)
         t_terms = term("Ip", "tf")
         if last:
-            sa("f2", "tf", F.Identity, scale=1.0 / M, bias=-95.5 / M)
-            cp("i2", "f2")
+            sa("f4", "tf", F.Identity, scale=1.0 / M, bias=-95.5 / M)
+            t_terms = term("I16", "tf") + term("Ip", "f4")
         else:
             claim("K1", "y")
             for r in range(2):
                 dma("y", row("K1", 6 + r), T.vf[:, r * M:(r + 1) * M], "vup", K("vf"), K("K1", "v%d" % r))
-        if rnd == 0:
-            constants_votes()
-        key, own = p(5, 1), p(5, 0)
-        off = T.ps3[:, 1:2]
-        tt(key, "BL", p(6, 0), A.min)
+        before("y", [], K3("P0"))
+
+        def record(r, src, x):
+            dma("y", row("P0", r), T[src][:, x * M:(x + 1) * M], "rec" + R, K(src) if src == "pb" else K(src, x),
+                K("P0", "r%d" % r))
+
         tt("i1", "BL", p(6, 0), A.min)
+
+        ts("i2", "i1", 11, A.arith_shift_right, 4095, A.bitwise_and)
+        ts("di", "i1", LAB - 1, A.bitwise_and)
+        ts("i3", "i1", 1, A.bitwise_and)
+        ts(p(6, 1), "i1", 0.0, A.is_lt)
+
+        tt("fg", "i2", own, A.not_equal)
+        dma("y", row("WM", 14), T.fg[:], "flg" + R, K("fg"), K("WM", "g"))
+        tt("hd", fix, "di", A.subtract)
+        tt("f2", "i1", base, A.is_lt)
+        tt(lead, "i2", own, A.is_equal)
+
+        tt(rest, "fg", "di", A.mult)
+        ts("mm", "i3", 1.0, A.add)
+        tt("f1", "hd", p(6, 1), A.subtract)
+
+        vop(lambda: g.vector.tensor_tensor_scan(T.Zb[:, 1:M + 1], T.di[:], ap(rest), 0.0, A.add, A.subtract),
+            [rest] + K("di"), K("Zb", 1))
+        matmuls([(T.ps3[:, 0:2], T.TR[:], T.Zb[:, M - 1:M + 1])], K("TR") + K("Zb", 1), [p(3, 0)])
+        high("r3", "f2", rest, A.mult)
+        record(12, "r3", 0)
+        tt(p(5, 1), "f2", rest, A.mult)
+        tt("i1", "f1", rest, A.subtract)
+        high("r2", "f1", rest, A.subtract)
+        record(10, "r2", 0)
+        tt("f3", "mm", lead, A.mult)
+
+        low("r3", p(5, 1))
+        record(13, "r3", 1)
+        vop(lambda: g.vector.tensor_scalar(ap(p(6, 0)), T.Zb[:, 0:M], T.ps3[:, 1:2], float(V), A.subtract, A.add),
+            K("Zb", 0, 1) + [p(3, 0)], [p(6, 0)])
+        ts("i3", "i1", 1, A.bitwise_and)
+        low("r2", "i1")
+        record(11, "r2", 1)
+
+        high("r1", p(6, 0), "f3", A.mult)
+        record(8, "r1", 0)
+        tt(p(5, 1), p(6, 0), "f3", A.mult)
+        ts("pb", "i3", 1.0, A.add)
+        record(14, "pb", 0)
+        cp("sI", "i2")
+
+        low("r1", p(5, 1))
+        record(9, "r1", 1)
+        ts("hd", "di", -float(HALF), A.add)
+        if last:
+            cp("i2", "f4")
+        cp("sv16", p(4, 1))
         if last:
             ts("f4", "i2", -float(V - 1), A.mult)
-            t_terms = term("I16", "tf") + term("Ip", "f4")
-        tt(own, "w4k", key, A.max)
-        ts("i3", "i1", 1, A.bitwise_and)
-        vop(lambda: g.vector.tensor_tensor_scan(T.Zb[:], ap(own), T.w4k[:], 0.0, A.add, A.subtract),
-            [own] + K("w4k"), K("Zb"))
-        matmuls([(T.ps3[:, 0:2], T.TR[:], T.Zb[:, M - 2:M])], K("TR") + K("Zb"), [p(3, 0)])
-        lin(p(1, 1), t_terms + pieces("Im", "sp", sc))
-        tt("f1", own, "w4k", A.subtract)
-        ts(p(7, 0), "i3", 5120.0, A.mult, float(V), A.add)
-        ts(p(6, 1), "i3", float(ODD + HALF), A.mult, -float(HALF), A.add)
-        tt(p(7, 1), p(7, 0), "f1", A.subtract)
-        tt("zo", "Zb", "f1", A.add)
-        ts("fg", p(7, 1), float(V), A.is_ge)
-        dma("y", row("WM", 14), T.fg[:], "flg" + R, K("fg"), K("WM", "g"))
-        tt("za", "Zb", p(6, 1), A.add)
-        high("r2", p(7, 0), "f1", A.subtract)
-        before("y", [], K3("P0"))
-        dma("y", row("P0", 10), T.r2[:, 0:M], "rec" + R, K("r2", 0), K("P0", "r2"))
-        ts(p(6, 0), "zo", off, A.add, rd=[p(3, 0)])
-        ts("f3", "za", off, A.add, 2.0, A.mult, rd=[p(3, 0)])
-        low("r2", p(7, 1))
-        dma("y", row("P0", 11), T.r2[:, M:2 * M], "rec" + R, K("r2", 1), K("P0", "r3"))
-        ts("i2", "i1", 12, A.arith_shift_right)
-        high("r1", "f3", p(6, 0), A.max)
-        dma("y", row("P0", 8), T.r1[:, 0:M], "rec" + R, K("r1", 0), K("P0", "r0"))
-        tt(p(6, 1), "f3", p(6, 0), A.max)
-        ts("di", "i1", 4095, A.bitwise_and)
-        cp("lab16", "i2")
-        low("r1", p(6, 1))
-        dma("y", row("P0", 9), T.r1[:, M:2 * M], "rec" + R, K("r1", 1), K("P0", "r1"))
-        ts("hd", "di", -1.0, A.mult, float(HALF), A.add)
-        cp("sv16", p(4, 1))
 
         def load_rows(a, b):
             gather("s", "P1", "WM", V, "wid16", 0, a, b, WMK + K("wid16"), K("P1", "r%d" % a))
@@ -626,56 +708,86 @@ def rank_program(g, core, T, topo):
         load_rows(0, 64)
         load_rows(64, 96)
 
-        rb, ra = p(6, 0), p(7, 0)
+        rb = p(6, 0)
+        TOP = ODD + HALF
 
-        def records(c, parts):
-            a, b = CH[c]
-            for q, a1, b1 in parts:
-                gather(q, "OB", "P0", V, "lab16", 0, a1, b1, whole("P0") + K("lab16"), K("OB", a1))
-            rd = K("OB", *[x[1] for x in parts])
-            conv("EBh", [("OB", 16 * a)], b - a, 6, a, rd)
-            conv("EA", [("OB", 16 * a)], b - a, 7, a, rd, plus=term("Ip", "hd"))
+        def look_up(q, a, b):
+            gather(q, "OB", "P0", V, "sI", 0, a, b, whole("P0") + K("sI"), K("OB", a))
 
-        def slot_calls(cols):
-            return [lambda: tt("f2", rb, "hd", A.is_le, cols), lambda: tt("up", rb, "f2", A.mult, cols),
-                    lambda: tt("f3", ra, "up", A.add, cols), lambda: ts("sl16", "f3", 0.25 - HALF, A.add, cols=cols)]
+        def slot_calls(qq, ra, cols):
+            return [lambda: tt("f2", qq, "hd", A.is_ge, cols), lambda: tt("up", qq, "f2", A.mult, cols),
+                    lambda: tt("f3", ra, "up", A.subtract, cols), lambda: ts("sl16", "f3", 0.25 - TOP, A.add, cols=cols)]
 
         def sort(a, b, rows):
             vop(lambda: g.vector.tensor_copy(T.SL[:, 0:SLW].indirect(T.sl16[:, a:b]), T.P1[:, 16 * a:16 * b]),
                 chunks("sl16", a, b) + K("P1", *["r%d" % x for x in rows]), SLK)
 
         claim("OB", "vs")
-        records(0, [("v", 0, 32), ("s", 32, 64)])
-        for call in slot_calls(CH[0]):
-            call()
-        records(1, [("s", 64, 128)])
-        records(2, [("s", 128, M)])
-        load_rows(96, 128)
-        sa("Bs", rb, F.Copy)
-        sa("sg", "Bs", F.Sign, bias=-2048.0)
-        sa("zz", "Bs", F.Relu, bias=-2560.0)
-        lin(p(0, 1), term("Ip", "Bs") + term("In", "hd") + term("It", "sg"))
+        parts = [[0, 32], [64, 104], [128, 152]]
+        for c, (a, b) in enumerate(CH):
+            look_up("v", a, parts[c][1])
+            look_up("s", parts[c][1], b)
+            conv("Eq", [("OB", 16 * a)], 64, 3 if c else 5, a, K("OB", *parts[c]))
+            for c1 in ([0], [], [1, 2])[c]:
+                conv("Era", [("OB", 1024 * c1)], 64, 4 if c1 else 7, 64 * c1, K("OB", *parts[c1]), plus=term("In", "hd"))
+        conv("Erb", [("OB", 0)], M, 6, 0, whole("OB"))
+        load_rows(96, M)
+        lead_calls, later = slot_calls(p(5, 0), p(7, 0), CH[0]), slot_calls(p(3, 0), p(4, 0), (64, M))
+        lead_calls[0]()
+        lead_calls[1]()
+        lead_calls[2]()
+        later[0]()
+        lead_calls[3]()
+        later[1]()
+        sort(0, 64, [0])
+        later[2]()
+        later[3]()
+        sort(64, M, [64, 96])
+        if rnd == 0:
+            before("y", K("sl16", 0), [])
+            for c in range(0, V, PIECE):
+                dma("y", T.xs[:, c:c + PIECE], T.x[:, c:c + PIECE], "ldx", [], K("xs", c))
+            before("g", K("sl16", 0), [])
+            send("HP", "landW", nxt, "rs_w", "ar_w", K("HP", 0, 1))
+        act(T.zo[:, 0:64], ap(p(5, 0), 0, 64), [p(5, 0)], K("zo", 0), func=F.Copy)
+        if rnd == 0:
+            constants_votes()
+        act(T.zo[:, 64:M], ap(p(3, 0), 64, M), [p(3, 0)], K("zo", 1, 2), func=F.Copy)
+        sa("sg", "zo", F.Sign, scale=-1.0, bias=-HALF - 0.25)
+        lin(p(0, 1), term("Ip", "zo") + term("In", "hd") + term("It", "sg"))
+        sa("pb", "sg", F.Identity, scale=float(LAB), bias=float(LAB))
+        lin(p(1, 1), t_terms + pieces("Im", "sp", sc) + 2 * term("Ib", "pb"))
+        sa("zz", rb, F.Relu, bias=-float(HALF))
         sa("od", "sg", F.Identity, scale=0.5, bias=0.5)
         sa("mh", "zz", F.Identity, scale=-1.0, bias=float(HALF))
-        sa("st", p(0, 1), F.Sign, bias=-1280.25)
-        sa("t0s", p(0, 1), F.Copy)
-        load_rows(128, M)
-        rest = slot_calls((64, M))
-        sort(0, 40, [0])
-        rest[0]()
-        sort(40, 64, [0])
-        rest[1]()
-        tt("tm", "od", p(1, 1), A.mult)
-        rest[2]()
-        tt("mm", "mh", "st", A.mult)
-        rest[3]()
-        lin(p(2, 0), term("Ip", "f3") + term("Ip", "mm") + term("Iq", "sg"))
-        tt("f1", "t0s", ra, A.add)
-        lin(p(7, 1), term("Ip", "tm") + pieces("Ib", "sp", sc))
-        sort(64, 128, [64, 96])
-        ts("hs16", p(2, 0), -float(HALF), A.add)
-        ts("es16", "f1", 0.25 - 1280 - HALF - 1, A.add, float(HALF), A.min)
-        sort(128, M, [128])
+        sa("fg", p(0, 1), F.Sign, scale=-1.0, bias=-768.25)
+        lin(p(2, 1), term("Ip", "mh") + term("I2k", "fg"))
+        sa("tm", p(1, 1), F.Relu, bias=-4096.0)
+        alike = term("Ip", "tm") + term("Im", "pb") + pieces("Ib", "sp", sc)
+        if not last:
+            lin(p(3, 1), alike + pieces("Im", "wp", 0))
+        sa("mm", p(2, 1), F.Relu, scale=2.0, bias=-4096.0)
+        lin(p(2, 0), term("Ip", "f3") + term("In", "mh") + term("Ip", "mm") + term("Iq", "sg"))
+        if not last:
+            sa("zz", p(3, 1), F.Abs)
+            sa("tfx", "zz", F.Sigmoid, scale=-STEEP, bias=0.5 * STEEP)
+            sa("fgR", "tfx", F.Identity, scale=-float(LVL))
+            send("fgR", "landG", prv, "rs_g", "ar_g", K("fgR"))
+            sa("f4", "tfx", F.Identity, scale=-2.0 * LVL / LAB)
+        lin(p(7, 1), alike)
+        lin(p(6, 1), term("Ip", "f3") + term("Ip", "up") + term("In", "zo") + term("Ip", "hd"))
+        ts("hs16", p(2, 0), -float(TOP), A.add)
+
+        if not last:
+            arrive("landW", prv, "ar_w")
+            arrive("landG", nxt, "ar_g")
+            claim("P1", "y")
+            for r in range(2):
+                rows_up("y", "P1", 2 + r, "landW", r, "wup")
+            dma("y", row("P1", KR), T.landG[:], "gup", K("landG"), K("P1", "g"))
+            claim("D0", "y")
+            prefill_all(0)
+            prefill_all(1)
 
         conv("Ev", [("SL", HALF)], 96, 1, 0, SLK)
         conv("Ev", [("SL", 0)], 96, 0, 0, SLK)
@@ -703,27 +815,29 @@ def rank_program(g, core, T, topo):
                                                     A.mult, A.max),
                 pk(3 + c) + K("xa", c) + (K("xm", c - 1) if c else []), K("xm", c))
 
-        def vote(c):
-            vop(lambda: g.vector.tensor_scalar(T.xd[:, cols(c)], T.xm[:, cols(c)], T.thf[:, 0:1], None, A.is_gt),
-                K("xm", c) + K("thf"), K("xd", c))
-            matmuls([(T["ps%d" % c][:], T.BO[:], T.xd[:, cols(c)])], K("BO") + K("xd", c), pk(c))
-
-        def verdict(c):
-            act(T.dec[:, cols(c)], T["ps%d" % c][:], pk(c) + K("cf", 5), K("dec", c), func=F.Sign, bias=5.5, scale=cf(5))
+        def against(q, a, b):
+            src, dst = T.xm[:].indirect(T.es16[:, a:b]), T.OB[:, 16 * a:16 * b]
+            rd = whole("xm") + K("es16") + K("thf") + K("cf", 5)
+            if q == "s":
+                act(dst, src, rd, K("OB", a), func=F.Sigmoid, scale=STEEP, bias=cf(5))
+            else:
+                vop(lambda: g.vector.tensor_scalar(dst, src, T.thf[:, 0:1], None, A.is_gt), rd, K("OB", a))
 
         own_u, own_s = pieces("Im", "uv", 0), pieces("Im", "sp", sc)
         claim("OC", "vs")
-        half("s", 0, 48)
-        half("v", 48, 80)
+        half("s", 0, 56)
+        half("v", 56, 84)
+        ts("es16", p(6, 1), 0.25 - TOP - 1, A.add, float(HALF), A.min)
         to16("row16", 96, M, 1, 0, K("row16", 1))
-        half("v", 80, 104)
+        half("v", 84, 108)
         for c in range(3):
             act(T.xa[:, cols(c)], T.xs[:, 0:V].indirect(T.row16[:, 96 + 32 * c:128 + 32 * c]), XK + K("row16", 1), K("xa", c),
                 func=F.Copy)
         to16("row16", 0, 96, 0, 0, K("row16", 0))
-        half("v", 104, 128)
-        early, late = (0, 128, [0, 48, 80, 104]), (128, M, [128, 138])
+        half("v", 108, 128)
+        early, late = (0, 128, [0, 56, 84, 108]), (128, M, [128, 144, 160])
         own_w = pieces("Im", "wp", 0)
+        tn, hout, tout = "AL", "BL", "za"
         half_list("E45", p(6, 0), own_u, *early)
         half_list("E67", p(6, 1), own_s, *early)
         if not last:
@@ -731,83 +845,98 @@ def rank_program(g, core, T, topo):
         gap(0)
         gap(1)
         gap(2)
+        half("s", 160, M)
         widest(0)
-        half("v", 128, 138)
-        widest(1)
-        vote(0)
-        widest(2)
-        vote(1)
-        vote(2)
-        half("v", 138, M)
-        for c in range(3):
-            verdict(c)
+        half("v", 128, 144)
         if not last:
-            half_list("Ecw", p(4, 0), [], *early)
+            half_list("Ecw", p(0, 0), [], *early)
+        widest(1)
+        half("v", 144, 160)
+        widest(2)
         half_list("E45", p(6, 0), own_u, *late)
+        half_list("E67", p(6, 1), own_s, *late)
         if not last:
             half_list("E89", p(7, 0), own_w, *late)
-            half_list("Ecw", p(4, 0), [], *late)
         claim("OB", "vs")
         for a, b in CH:
-            for q, a1 in (("v", a), ("s", a + 32)):
-                gather(q, "OB", "dec", HALF + 16, "es16", 0, a1, a1 + 32, K3("dec") + K("dec", "one") + K("es16"), K("OB", a1))
+            against("v", a, a + 32)
+            against("s", a + 32, b)
             conv("Eh", [("OB", 16 * a)], 64, 3, a, K("OB", a, a + 32))
-        if not last:
-            tt("mm", "od", p(4, 0), A.mult)
-        cp("du", p(6, 0))
-        half_list("E67", p(6, 1), own_s, *late)
         claim("P0", "vs")
+        for q in "v":
+            before(q, [], pk(4))
 
         def mirror(q, a, b):
             gather(q, "P0", "OB", V, "sv16", 0, a, b, whole("OB") + K("sv16"), K("P0", a))
 
-        def mirror_list(a, parts):
-            conv("Eh", [("P0", 16 * a)], 64, 2, a, K("P0", *parts))
+        def mirror_list(bk, a, parts):
+            conv("Eh", [("P0", 16 * a)], 64, bk, a, K("P0", *parts))
 
-        mirror("s", 0, 64)
+        def new_t(out, bk, cols):
+            b, x = p(4, 0, cols), p(4, 1, cols)
+            return [lambda: ts(b, p(bk, 0), LIMIT, A.is_le, -2.0, A.mult, cols=cols),
+                    lambda: tt(x, "f1", b, A.mult, cols), lambda: tt(out, "f3", x, A.add, cols)]
+
+        first, second = (0, 128), (128, M)
         if not last:
-            mirror("v", 64, 128)
-            mirror("s", 128, 164)
-            mirror("v", 164, M)
-            for a, parts in ((0, [0]), (64, [64]), (128, [128, 164])):
-                mirror_list(a, parts)
-            tt(p(5, 0), "du", p(3, 0), A.mult)
-            tt("mh", "mm", p(7, 0), A.add)
-            cp("tn", p(3, 0))
+            half_list("Ecw", p(0, 0), [], *late)
+        mirror("s", 0, 32)
+        mirror("v", 32, 64)
+        mirror_list(2, 0, [0, 32])
+        mirror("s", 64, 128)
+        mirror_list(2, 64, [64])
+        mirror("v", 128, 144)
+        ts(tn, p(3, 0), LIMIT, A.is_le)
+        ts("zz", p(3, 0), LIMIT, A.is_le, 0.5, A.subtract)
+        mirror("s", 160, M)
+        mirror("v", 144, 160)
+        mirror_list(1, 128, [128, 144, 160])
+        tt(p(5, 0), tn, p(6, 0), A.mult)
+        tt("f2", tn, p(6, 1), A.mult)
+        tt("f1", "zz", p(6, 1), A.mult)
+        if not last:
+            one, two = new_t("tf", 2, first), new_t("tf", 1, second)
+            tt("mm", "od", p(0, 0), A.mult)
             tt(p(5, 1), "uf", p(5, 0), A.add)
             high("HP", "uf", p(5, 0), A.add)
-            tt("zz", "mh", p(3, 0), A.mult)
-            tt("f1", "tn", p(2, 0), A.not_equal)
+            tt("f3", "f2", p(7, 1), A.add)
+            tt(p(0, 1), "mm", p(7, 0), A.add)
             low("HP", p(5, 1))
             send("HP", "landU", nxt, "rs_h" + R, "ar_h" + R, K("HP", 0, 1))
-            lin(p(1, 0), term("t128", "wid") + term("t128", "zz"))
-            tt("f2", "f1", p(6, 1), A.mult)
-            tt("tf", "f2", p(7, 1), A.add)
-            high("TP", "f2", p(7, 1), A.add)
+            one[0]()
+            tt("zz", tn, p(0, 1), A.mult)
+            two[0]()
+            lin(p(3, 1), pieces("Ib", "wp", 0) + term("t128", "zz"))
+            one[1]()
+            two[1]()
+            one[2]()
+            two[2]()
+            cp("fI", p(3, 1))
             cp("ul", "tf")
             send("ul", "landT", prv, "rs_t1", "ar_t1", K("ul"))
+            arrive("landU", prv, "ar_h0")
+            send("fI", "landK", nxt, "rs_k", "ar_k", K("fI") + K("landU"))
+            act(T.TP[:, 0:M], T.tf[:], K("tf"), K("TP", 0), func=F.Copy)
+            act(T.TF[:, 0:M], T.TP[:, 0:M], K("TP", 0), K("TF", 0), func=F.Copy)
+            tt("f2", "tf", "f4", A.add)
             vop(lambda: g.vector.tensor_tensor(T.TF[:, M:2 * M], T.tf[:], T.TP[:, 0:M], A.subtract),
                 K("tf") + K("TP", 0), K("TF", 1))
-            act(T.TF[:, 0:M], T.TP[:, 0:M], K("TP", 0), K("TF", 0), func=F.Copy)
-            cp("fI", p(1, 0))
-            send("fI", "landK", nxt, "rs_k", "ar_k", K("fI"))
+            dma("s", row("K1", KR), T.f2[:], "upk1", K("f2"), K("K1", "k"))
+            for r in range(2):
+                dma("s", row("K1", 2 + r), T.TF[:, r * M:(r + 1) * M], "upk1", K("TF", r), K("K1", "t%d" % r))
         else:
-            mirror("v", 64, 88)
-            mirror_list(0, [0])
-            tt(p(5, 0), "du", p(3, 0), A.mult)
-            mirror("s", 128, 176)
-            cp("tn", p(3, 0))
-            tt("hout", "uf", p(5, 0), A.add)
-            send("hout", "landY", nxt, "rs_h" + R, "ar_h" + R, K("hout"))
-            mirror("v", 88, 128)
-            mirror_list(64, [64, 88])
-            mirror("v", 176, M)
-            mirror_list(128, [128, 176])
-            tt("f1", "tn", p(2, 0), A.not_equal)
-            tt("f2", "f1", p(6, 1), A.mult)
-            tt("tout", "f2", p(7, 1), A.add)
+            one, two = new_t(tout, 2, first), new_t(tout, 1, second)
+            tt(hout, "uf", p(5, 0), A.add)
+            send(hout, "landY", nxt, "rs_h" + R, "ar_h" + R, K(hout))
+            tt("f3", "f2", p(7, 1), A.add)
+            one[0]()
+            two[0]()
+            one[1]()
+            two[1]()
+            one[2]()
+            two[2]()
             arrive("landY", prv, "ar_h" + R)
-            dma("s", T.yt[:], T.tout[:], "outt", K("tout"), K("yt", 0))
+            dma("s", T.yt[:], T[tout][:], "outt", K(tout), K("yt", 0))
             dma("y", T.yu[sh:128, :], T.landY[0:128 - sh, :], "outu", K("landY"), K("yu", 0))
             dma("y", T.yu[0:sh, :], T.landY[128 - sh:128, :], "outu", K("landY"), K("yu", 1))
 

from concourse.mybir import AluOpType as A, ActivationFunctionType as F, AxisListType as X

V = 3072
M = 192
RO = 2
GS = 3
HALF = V // 2
ODD = V
SLW = ODD + V
STEPS = 9
HOP = 1 << STEPS
KR = 15
LAB = 2048
LVL = 1 << 23
PIECE = 768
LIMIT = 16 - 11 + 0.5
STEEP = 64.0


def _sb(cols, dt):
    return ("sbuf", [128, cols], dt)


SCRATCH = {
    "xs": _sb(V, "bfloat16"), "WM": _sb(V, "bfloat16"),
    "P0": _sb(V, "bfloat16"), "P1": _sb(V, "bfloat16"), "OB": _sb(V, "bfloat16"), "OC": _sb(V, "bfloat16"),
    "K0": _sb(V, "float32"), "K1": _sb(V, "float32"), "D0": _sb(V, "float32"), "D1": _sb(V, "float32"),
    "SL": _sb(SLW, "bfloat16"),
    "xa": _sb(HALF, "bfloat16"), "xd": _sb(HALF, "bfloat16"), "xm": _sb(HALF + 16, "bfloat16"),
    "CN": _sb(1024, "float32"),
    "LL": _sb(M * (STEPS + 1), "uint16"),
    "tin": _sb(M, "int32"), "uin": _sb(M, "int32"), "thi": _sb(8, "int32"), "thf": _sb(8, "float32"),
    "TP": _sb(2 * M, "bfloat16"), "UP": _sb(2 * M, "bfloat16"), "HP": _sb(2 * M, "bfloat16"),
    "TV": _sb(3 * M, "bfloat16"), "landF": _sb(3 * M, "bfloat16"), "landU": _sb(2 * M, "bfloat16"), "landW": _sb(2 * M, "bfloat16"),
    "landY": _sb(M, "float32"), "wp": _sb(2 * M, "bfloat16"), "TF": _sb(2 * M, "float32"), "vf": _sb(2 * M, "float32"),
    "QW": _sb(V, "float32"), "t128": _sb(128, "float32"),
    "idp": _sb(2 * M, "bfloat16"), "vp": _sb(2 * M, "bfloat16"), "ia": _sb(M, "float32"), "wid": _sb(M, "float32"),
    "sp": _sb(4 * M, "bfloat16"), "uv": _sb(2 * M, "bfloat16"),
    "r1": _sb(2 * M, "bfloat16"), "r2": _sb(2 * M, "bfloat16"), "r3": _sb(2 * M, "bfloat16"),
    "Ip": _sb(128, "float32"), "In": _sb(128, "float32"), "I16": _sb(128, "float32"),
    "Zb": _sb(M + 8, "float32"), "zer": _sb(256, "float32"),
    "ci": _sb(8, "int32"), "cf": _sb(32, "float32"), "wt": _sb(8, "float32"), "i8": _sb(32, "float32"),
    "cc": _sb(144, "float32"), "EB": _sb(144, "float32"), "gg": _sb(128, "float32"),
    "FB": _sb(128, "bfloat16"), "TR": _sb(128, "float32"),
}
for _n in ("E0", "E1", "E01", "E23", "E45", "E67", "E89", "Ecw", "Era", "Erb", "Eq", "Ev", "Eh"):
    SCRATCH[_n] = _sb(144, "bfloat16")
for _n in ("Iq", "It", "Ib", "Im", "I2k"):
    SCRATCH[_n] = _sb(128, "bfloat16")
for _n in ("sg", "fg", "zb", "tfx", "fgR", "landG", "pb"):
    SCRATCH[_n] = _sb(M, "bfloat16")
for _n in ("ul", "uI", "fI", "sI", "sl16", "hs16", "es16", "row16", "wid16", "sv16", "landT", "landK"):
    SCRATCH[_n] = _sb(M, "uint16")
for _n in ("i1", "i2", "i3", "di"):
    SCRATCH[_n] = _sb(M, "int32")
for _n in ("tf", "uf", "mh", "KL", "AL", "BL", "f1", "f2", "f3", "f4", "za", "zo", "hd", "up",
           "zz", "st", "od", "mm", "tm"):
    SCRATCH[_n] = _sb(M, "float32")
for _b in range(8):
    SCRATCH["ps%d" % _b] = ("psum", [128, 512], "float32")

_PER_ROUND = ["clr", "upk", "upu", "sdn", "srow", "crow", "kdn", "adn", "bdn", "rec", "flg",
              "rs_t", "rs_h", "ar_t", "ar_h"]
SEMAPHORES = (["qv", "qs", "qt", "qg", "ldt", "ldu", "ldx", "ldth", "upid", "upt", "upf", "uvd", "vup", "wup",
               "rs_w", "ar_w", "rs_g", "ar_g", "gup", "rs_k", "ar_k", "outt", "outu"]
              + ["acc%d" % i for i in range(6)] + ["pre%d" % i for i in range(6)]
              + [n + str(r) for r in range(RO) for n in _PER_ROUND])


def rank_program(g, core, T, topo):
    rank = T.rank_of(core)
    if rank is None:
        return
    n_ranks = len(T.cores)
    nxt = T.cores[(rank + 1) % n_ranks]
    prv = T.cores[(rank - 1) % n_ranks]

    Q = {"v": g.vector, "s": g.scalar, "t": g.tensor, "y": g.sync, "g": g}
    total = {}
    seen = {q: {} for q in Q}
    writer = {}
    readers = {}
    bank = {}

    def need(q, tok):
        sem, val = tok
        if val is None:
            val = total[sem]
        if seen[q].get(sem, 0) < val:
            Q[q].wait_ge(T.sem[sem], val)
            seen[q][sem] = val

    def before(q, rd, wr):
        toks = []
        for k in rd:
            if k in writer:
                toks.append(writer[k])
        for k in wr:
            if k in writer:
                toks.append(writer[k])
            toks.extend(readers.get(k, []))
        for k in rd + wr:
            if k[0] == "ps" and k[1] in bank and bank[k[1]][0] != q:
                toks.append(bank[k[1]][1])
        top = {}
        for sem, val in toks:
            if q == "t" and sem == "qt":
                continue
            top[sem] = max(top.get(sem, 0), total[sem] if val is None else val)
        for sem in top:
            need(q, (sem, top[sem]))

    def after(q, tok, rd, wr):
        for k in rd:
            readers.setdefault(k, []).append(tok)
        for k in wr:
            writer[k] = tok
            readers[k] = []
        for k in rd + wr:
            if k[0] == "ps":
                bank[k[1]] = (q, tok)

    def op(q, fn, rd, wr):
        before(q, rd, wr)
        sem = "q" + q
        fn().then_inc(T.sem[sem], 1)
        total[sem] = total.get(sem, 0) + 1
        after(q, (sem, total[sem]), rd, wr)

    def dma(q, out, in_, sem, rd, wr, **kw):
        before(q, rd, wr)
        Q[q].dma_start(out, in_, **kw).then_inc(T.sem[sem], 16)
        total[sem] = total.get(sem, 0) + 16
        after(q, (sem, None), rd, wr)

    def send(src, dst, to, sem_l, sem_r, rd, cols=None):
        before("g", rd, [])
        rid, pid, _ = topo.addr(to)
        a, b = cols or (0, SCRATCH[src][1][1])
        g.remote_dma(T[dst][:, a:b], T[src][:, a:b], T.sem[sem_r], T.sem[sem_l], pid, rid, topo.mask(core, to))
        total[sem_l] = len(topo.engines(core, to))
        after("g", (sem_l, None), rd, [])

    def arrive(buf, frm, sem_r, *parts):
        total[sem_r] = len(topo.engines(frm, core))
        for k in K(buf, *parts):
            writer[k] = (sem_r, None)

    def K(name, *parts):
        if not parts and SCRATCH[name][1][1] == M:
            parts = (0, 1, 2)
        return [(name, x) for x in parts] if parts else [(name,)]

    def K3(name):
        return K(name, 0, 1, 2)

    def whole(name):
        return [k for k in writer if k[0] == name]

    def claim(name, queues):
        keys = whole(name)
        for q in queues:
            before(q, [], keys)
        for k in keys:
            del writer[k]
            readers.pop(k, None)

    def chunks(name, a, b, tag=None):
        return [(name, c if tag is None else (tag, c)) for c in range(a // 64, (b - 1) // 64 + 1)]

    def p(b, s, *part):
        return ("ps", b, s) + part

    def ap(x, a=0, b=M):
        if isinstance(x, tuple):
            return T["ps%d" % x[1]][:, 256 * x[2] + a:256 * x[2] + b]
        return T[x][:, a:b]

    def ky(x, cols=(0, M)):
        return [x] if isinstance(x, tuple) else chunks(x, *cols)

    def tt(out, a, b, o, cols=(0, M)):
        op("v", lambda: g.vector.tensor_tensor(ap(out, *cols), ap(a, *cols), ap(b, *cols), o),
           ky(a, cols) + ky(b, cols), ky(out, cols))

    def ts(out, a, s1, o1, s2=None, o2=None, cols=(0, M), rd=()):
        rd = ky(a, cols) + list(rd)
        if o2 is None:
            op("v", lambda: g.vector.tensor_scalar(ap(out, *cols), ap(a, *cols), s1, None, o1), rd, ky(out, cols))
        else:
            op("v", lambda: g.vector.tensor_scalar(ap(out, *cols), ap(a, *cols), s1, s2, o1, o2), rd, ky(out, cols))

    def cp(out, a):
        op("v", lambda: g.vector.tensor_copy(ap(out), ap(a)), ky(a), ky(out))

    def sa(out, a, func, scale=1.0, bias=0.0):
        op("s", lambda: g.scalar.activation(ap(out), ap(a), func, bias=bias, scale=scale), ky(a), ky(out))

    def vop(fn, rd, wr):
        op("v", fn, rd, wr)

    def matmuls(calls, rd, wr):
        before("t", rd, wr)
        ins = None
        for k, (out, lhsT, rhs) in enumerate(calls):
            ins = g.tensor.matmul(out, lhsT, rhs, k == 0, k == len(calls) - 1)
        ins.then_inc(T.sem.qt, 1)
        total["qt"] = total.get("qt", 0) + 1
        after("t", ("qt", total["qt"]), rd, wr)

    def pk(b):
        return [p(b, 0), p(b, 1)]

    PART = {"ids": ("SL", 0), "WU": ("SL", V)}

    def W(name, a, b, step=1, rows=slice(0, 128)):
        name, at = PART.get(name, (name, 0))
        return T[name][rows, at + a:at + b:step]

    def conv(E, srcs, n, b, col, rd, plus=()):
        out = T["ps%d" % b][:, col:col + n]
        a = col % 256
        matmuls([(out, T[I][:], T[x][:, c0 + a:c0 + a + n]) for (I, x, c0, _) in plus]
                + [(out, T[E][:, 15 - i:143 - i], W(s, c0 + i, c0 + 16 * n, 16)) for (s, c0) in srcs for i in range(16)],
                rd + K(E) + [k for x in plus for k in x[3]], [p(b, col // 256)])

    def term(I, x):
        return [(I, x, 0, K(I) + K(x))]

    def pieces(I, buf, c):
        return [(I, buf, x * M, K(I) + K(buf, x)) for x in (c, c + 1)]

    def lin(out, terms):
        matmuls([(ap(out), T[I][:], T[x][:, c0:c0 + M]) for (I, x, c0, _) in terms], [k for x in terms for k in x[3]], [out])

    def gather(q, out, win, wcols, lst, l0, a, b, rd, wr, bias=None, scale=1.0):
        src = W(win, 0, wcols).indirect(T[lst][:, l0 + a:l0 + b])
        dst = W(out, 16 * a, 16 * b)
        if q == "s":
            if bias is None:
                op("s", lambda: g.scalar.activation(dst, src, F.Copy), rd, wr)
            else:
                op("s", lambda: g.scalar.activation(dst, src, F.Identity, bias=bias, scale=scale), rd, wr)
        elif bias is None:
            op("v", lambda: g.vector.tensor_copy(dst, src), rd, wr)
        else:
            op("v", lambda: g.vector.tensor_scalar(dst, src, scale, bias, A.mult, A.add), rd, wr)

    def to16(lst, a, b, bk, col, wr):
        vop(lambda: g.vector.tensor_copy(T[lst][:, a:b], T["ps%d" % bk][:, col:col + b - a]), [p(bk, 0)], wr)

    def row(buf, r):
        return W(buf, 0, V, rows=slice(r, 128, 16))

    def col(out, src):
        vop(lambda: g.vector.tensor_copy(T.cf[:, out:out + 1], T.ci[:, src:src + 1]), K("ci", src), K("cf", out))

    def cf(i):
        return T.cf[:, i:i + 1]

    def wt(i):
        return T.wt[:, i:i + 1]

    def act(out, in_, rd, wr, func=F.Identity, **kw):
        op("s", lambda: g.scalar.activation(out, in_, func, **kw), rd, wr)

    def make_e(name, weights, key):
        act(T[name][:], T.EB[:], K("EB") + key, K(name), scale=weights)

    def pair_sum(out, buf, c, rd):
        vop(lambda: g.vector.tensor_tensor(T[out][:], T[buf][:, c * M:(c + 1) * M], T[buf][:, (c + 1) * M:(c + 2) * M], A.add),
            rd, K(out))

    WMK = K("WM", *[x + r for x in "ftuswcv" for r in "01"]) + K("WM", "g", "h")
    IDK = K("ids", 0, 1, 2, 3)
    sh = 16 * GS

    def cs(out, src, scale=1.0, bias=0.0, func=F.Identity):
        if isinstance(src, tuple):
            src, rd = wt(src[0]), K("wt")
        else:
            src, rd = cf(src), K("cf", src)
        if isinstance(bias, int):
            bias, rd = cf(bias), rd + K("cf", bias)
        act(cf(out), src, rd, K("cf", out), func=func, scale=scale, bias=bias)

    def fill(buf, a, b, keys):
        for c in range(a, b):
            act(T[buf][:, 256 * c:256 * c + 256], T.zer[:], K("zer"), K(buf, "z%d" % c), func=F.Copy)
        for k in keys:
            writer[k] = writer[(buf, "z%d" % (b - 1))]

    def pieces_in(pc, lo, hi, a, b):
        vop(lambda: g.vector.tensor_scalar(T[pc][:, 0:M], T[lo][:], a, None, A.mult), K(lo), K(pc, 0))
        vop(lambda: g.vector.tensor_scalar(T[pc][:, M:2 * M], T[hi][:], b, None, A.mult), K(hi), K(pc, 1))

    dma("y", T.tin[:], T.t0[:], "ldt", [], K("tin"))
    dma("y", T.uin[:], T.u0[:], "ldu", [], K("uin"))
    fl = {"allow_small_or_imprecise_dtypes": True}
    op("g", lambda: g.iota(T.ci[:, 0:1], [[0, 1]], 0, 1), [], K("ci", 0))
    op("g", lambda: g.iota(T.ia[:], [[1, 12], [0, 16]], 0, 0, **fl), [], K("ia"))
    op("g", lambda: g.iota(T.wid[:], [[1, M]], 0, 0, **fl), [], K("wid"))
    op("g", lambda: g.iota(T.idp[:, 0:M], [[0, 12], [M, 16]], 0, 0, **fl), [], K("idp", 0))
    op("g", lambda: g.iota(T.i8[:, 0:16], [[1, 16]], 0, 0, **fl), [], K("i8"))
    op("g", lambda: g.iota(T.cc[:], [[1, 144]], 0, -1, **fl), [], K("cc"))
    vop(lambda: g.vector.memset(T.zer[:], 0.0), [], K("zer"))
    vop(lambda: g.vector.memset(W("ids", 0, 1024), 1.0), [], K("ids", "a"))
    vop(lambda: g.vector.tensor_scalar(T.ci[:, 1:2], T.ci[:, 0:1], 15, None, A.bitwise_and), K("ci", 0), K("ci", 1))
    vop(lambda: g.vector.memset(W("ids", 1024, 2048), 1.0), [], K("ids", "b"))
    col(12, 1)
    vop(lambda: g.vector.tensor_scalar(cf(0), T.ci[:, 1:2], 12.0, None, A.mult), K("ci", 1), K("cf", 0))
    vop(lambda: g.vector.memset(W("ids", 2048, V), 1.0), [], IDK)
    vop(lambda: g.vector.tensor_scalar(T.idp[:, M:2 * M], T.ia[:], cf(0), None, A.add), K("ia") + K("cf", 0), K("idp", 1))
    fill("WM", 0, 4, [])
    act(T.f1[:], T.wid[:], K("wid") + K("cf", 12), K("f1"), bias=cf(12), scale=16.0)
    cs(1, 12, 1.0, -15.0)
    cs(2, 12, -1.0, 0.5)
    cs(6, 12, float(M))
    cs(15, 12, 1.0, -14.0, F.Relu)
    fill("WM", 4, 12, WMK)
    for r in (1, 0):
        dma("y", row("ids", r), T.idp[:, r * M:(r + 1) * M], "upid", K("idp", r), K("ids", r))

    ts("i1", "tin", 15, A.bitwise_and)
    ts("i2", "tin", 4, A.arith_shift_right)
    vop(lambda: g.vector.tensor_tensor(T.TV[:, 2 * M:3 * M], T.tin[:], T.f1[:], A.is_equal), K("tin") + K("f1"), K("TV", 2))
    pieces_in("TV", "i1", "i2", 1.0, 16.0)
    send("TV", "landF", prv, "rs_t0", "ar_t0", K("TV", 0, 1, 2))
    cp("ul", "uin")
    ts("i3", "uin", 15, A.bitwise_and)
    ts("di", "uin", 4, A.arith_shift_right)
    vop(lambda: g.vector.tensor_scalar(T.i8[:, 16:32], T.i8[:, 0:16], cf(12), 1.0, A.is_lt, A.add),
        K("i8") + K("cf", 12), K("i8", 1))
    vop(lambda: g.vector.memset(T.xm[:, HALF:HALF + 16], -1.0), [], K("xm", "turn"))
    vop(lambda: g.vector.memset(T.Zb[:, 0:8], 0.0), [], K("Zb", 0))
    pieces_in("UP", "i3", "di", float(M), 1.0)
    vop(lambda: g.vector.tensor_reduce(cf(14), T.i8[:, 16:32], X.X, A.mult, negate=True), K("i8", 1), K("cf", 14))
    for r in range(2):
        dma("y", row("WM", 4 + r), T.UP[:, r * M:(r + 1) * M], "upu0", K("UP", r), K("WM", "u%d" % r))
    act(T.EB[:], T.cc[:], K("cc") + K("cf", 1), K("EB"), func=F.Abs, bias=cf(1))
    act(T.wt[:], T.i8[:, 0:8], K("i8") + K("cf", 2), K("wt"), func=F.Abs, bias=cf(2), scale=2.0)
    act(T.In[:], T.cc[:, 0:128], K("cc"), K("In"), func=F.Abs)
    act(T.TP[:, 0:M], T.TV[:, 0:M], K("TV", 0), K("TP", 0), scale=float(M))
    act(T.EB[:], T.EB[:], K("EB"), K("EB"), func=F.Relu, bias=1.0, scale=-1.0)
    act(T.wt[:], T.wt[:], K("wt"), K("wt"), func=F.Relu, bias=1.5, scale=-1.0)
    act(T.Ip[:], T.In[:], K("In"), K("Ip"), func=F.Relu, scale=-1.0, bias=1.0)
    act(T.TP[:, M:2 * M], T.TV[:, M:2 * M], K("TV", 1), K("TP", 1), scale=1.0 / 16)
    act(T.fgR[:], T.TV[:, 2 * M:3 * M], K("TV", 2), K("fgR"), scale=-float(LVL))
    make_e("E45", wt(2), K("wt"))
    make_e("E01", wt(0), K("wt"))
    make_e("E23", wt(1), K("wt"))

    op("g", lambda: g.iota(T.D1[:], [[0, V]], 0, 0, **fl), [], K3("D1"))
    dma("g", T.thi[:, 0:1], T.th[:], "ldth", [], K("thi"), allow_slow_non_contiguous=True)
    for c in range(2):
        op("g", lambda: g.iota(T.D0[:, 1024 * c:1024 * c + 1024], [[0, 1024]], 0, 0, **fl), [], K("D0", c))
    SLK = K("SL", 12, 13, 14)
    XK = K("xs", *range(0, V, PIECE))

    def constants_doubling():
        for name, scale in (("Ib", 1.0), ("I2k", float(LAB)), ("Im", -1.0)):
            act(T[name][:], T.Ip[:], K("Ip"), K(name), scale=scale)
        lin(p(6, 0), pieces("I2k", "TP", 0) + 2 * term("Ib", "fgR"))
        lin(p(7, 0), pieces("Ib", "TP", 0))
        cs(16, 15, -float(LVL + 1), 1.0)
        cs(26, 12, -1.0, 1.0, F.Relu)
        cs(27, 12, 1.0, -1.0, F.Abs)
        for c in range(4):
            act(T.CN[:, 256 * c:256 * c + 256], T.zer[:], K("zer") + K("cf", 14), K("CN", c), bias=cf(14))
        act(T.tfx[:], T.TV[:, 2 * M:3 * M], K("TV", 2), K("tfx"), func=F.Copy)
        act(T.wp[:, M:2 * M], T.wid[:], K("wid"), K("wp", 1), func=F.Copy)
        act(T.wp[:, 0:M], T.zer[:, 0:M], K("zer") + K("cf", 6), K("wp", 0), bias=cf(6))
        act(T.vp[:, 0:M], T.wid[:], K("wid"), K("vp", 0), scale=16.0)
        act(T.vp[:, M:2 * M], T.zer[:, 0:M], K("zer") + K("cf", 12), K("vp", 1), bias=cf(12))
        act(T.zb[:], T.zer[:, 0:M], K("zer"), K("zb"))
        act(T.uv[:, 0:M], T.UP[:, M:2 * M], K("UP", 1), K("uv", 0), scale=16.0)
        act(T.uv[:, M:2 * M], T.UP[:, 0:M], K("UP", 0), K("uv", 1), scale=1.0 / M)
        act(T.wid[:], T.wid[:], K("wid") + K("cf", 6), K("wid"), bias=cf(6))
        cs(28, 27, -1.0, 1.0, F.Relu)
        make_e("E0", cf(26), K("cf", 26))
        sa("f2", p(6, 0), F.Identity, bias=float(LVL + HOP))
        sa("tf", p(7, 0), F.Copy)
        make_e("E1", cf(28), K("cf", 28))
        fill("D0", 8, 12, K("D0", 2))

    def constants_leaders():
        vop(lambda: g.vector.tensor_scalar(T.ci[:, 3:4], T.ci[:, 0:1], 4, None, A.arith_shift_right), K("ci", 0), K("ci", 3))
        vop(lambda: g.vector.tensor_copy(T.thf[:, 0:1], T.thi[:, 0:1]), K("thi"), K("thf"))
        col(3, 3)
        vop(lambda: g.vector.tensor_scalar(T.gg[:], T.gg[:], cf(3), None, A.is_equal), K("gg") + K("cf", 3), K("gg"))
        op("g", lambda: g.affine_select(T.TR[:], T.gg[:], [[-1, 128]], A.is_ge, 0.0, 0, 1), K("gg"), K("TR"))

        op("g", lambda: g.affine_select(T.t128[:], T.zer[:, 0:128], [[1, 128]], A.not_equal, 1.0, -sh, -1), K("zer"), K("t128"))
        op("g", lambda: g.affine_select(T.t128[:], T.t128[:], [[1, 128]], A.not_equal, 1.0, 128 - sh, -1), K("t128"), K("t128"))

    def constants_sums():
        act(T.vf[:], T.vp[:], K("vp", 0, 1), K("vf"), func=F.Copy)
        for name, scale in (("In", -1.0), ("It", 768.0), ("Iq", -0.25), ("I16", 16.0)):
            act(T[name][:], T.Ip[:], K("Ip"), K(name), scale=scale)
        cs(10, 12, 1.0, -14.0, F.Abs)
        cs(20, (6,), -1.0)
        cs(13, (5,), 0.5)
        cs(11, 10, -1.0, 1.0, F.Relu)
        cs(19, (5,), -1.0, 20)
        cs(22, (5,), -0.5, 20)
        cs(21, 11, float(HALF), 13)
        cs(8, (4,), 0.5, 19)
        cs(23, 11, -float(HALF), 22)
        make_e("Erb", cf(21), K("cf", 21))
        cs(24, 11, float(ODD), 8)
        make_e("Eq", cf(23), K("cf", 23))
        make_e("Era", cf(24), K("cf", 24))

    def constants_votes():
        act(cf(5), T.thf[:, 0:1], K("thf"), K("cf", 5), scale=-STEEP, bias=-0.5 * STEEP)
        cs(25, (4,), -1.0)
        make_e("Ev", wt(6), K("wt"))
        make_e("E67", wt(3), K("wt"))
        make_e("Eh", 1.0, [])
        cs(7, (5,), 1.0, 25)
        act(T.FB[:], T.gg[:], K("gg") + K("cf", 11), K("FB"), scale=cf(11))
        make_e("E89", wt(4), K("wt"))
        make_e("Ecw", cf(7), K("cf", 7))
        cs(17, 15, float(LAB - 1), 1.0)
        cs(18, 15, float(LVL + HOP))

    def high(dst, a, b, o):
        vop(lambda: g.vector.tensor_tensor(T[dst][:, 0:M], ap(a), ap(b), o), ky(a) + ky(b), K(dst, 0))

    def low(dst, src):
        vop(lambda: g.vector.tensor_tensor(T[dst][:, M:2 * M], ap(src), T[dst][:, 0:M], A.subtract),
            ky(src) + K(dst, 0), K(dst, 1))

    CH = [(0, 64), (64, 128), (128, 192)]

    for rnd in range(RO):
        R = str(rnd)
        last = rnd + 1 == RO
        def rows_up(q, buf, r, land, x, sem):
            dma(q, T[buf][sh + r::16, 0:V], T[land][0:128 - sh, x * M:(x + 1) * M], sem, K(land), K(buf, "a%d" % r))
            dma(q, T[buf][r:sh:16, 0:V], T[land][128 - sh:128, x * M:(x + 1) * M], sem, K(land), K(buf, "b%d" % r))

        def scatter_u(a, b):
            vop(lambda: g.vector.tensor_copy(W("WU", 0, V).indirect(T.ul[:, a:b]), W("ids", 16 * a, 16 * b)),
                K("ul") + IDK, K("WU", 0))

        def prefill(j, c):
            D = "D%d" % (j % 2)
            dma("y", T[D][KR::16, 1024 * c:1024 * c + 1024], T.CN[j::16, :], "pre%d" % (3 * (j % 2) + c),
                K("CN", 0, 1, 2, 3), K(D, c))

        def accumulate(j, c):
            D, Kj = "D%d" % (j % 2), "K%d" % (j % 2)
            dma("g", T[D][KR::16, 1024 * c:1024 * c + 1024], T[Kj][KR::16, 1024 * c:1024 * c + 1024],
                "acc%d" % (3 * (j % 2) + c), K(Kj, c), K(D, c), accum_op=A.add)

        def prefill_all(j):
            for c in range(3):
                prefill(j, c)

        if rnd == 0:
            scatter_u(0, 112)
            conv("E45", [("WM", 0)], M, 1, 0, WMK)
            to16("uI", 0, M, 1, 0, K("uI"))
            constants_doubling()
            arrive("landF", nxt, "ar_t0")
            for r, (at, key) in enumerate(((0, "f0"), (1, "f1"), (KR, "h"))):
                dma("y", row("WM", at), T.landF[:, r * M:(r + 1) * M], "upf", K("landF"), K("WM", key))
            scatter_u(112, M)

            def f_of_u(q, a, b):
                gather(q, "OB", "WM", V, "uI", 0, a, b, WMK + K("uI") + K("cf", 16), K("OB", a), bias=0.0, scale=cf(16))

            def s_of(q, a, b):
                gather(q, "OC", "WU", V, "fI", 0, a, b, K("WU", 0) + chunks("fI", a, b), K("OC", a))

            for c in range(2):
                f_of_u("s", 64 * c, 64 * c + 64)
                conv("E01", [("OB", 1024 * c)], 64, c, 0, K("OB", 64 * c))
            f_of_u("s", 128, 144)
            f_of_u("v", 144, M)
            conv("E01", [("OB", 2048)], 64, 2, 0, K("OB", 128, 144))
            dma("y", row("D1", KR), T.f2[:], "upk" + R, K("f2"), K3("D1"))
            for r in range(2):
                dma("y", row("ids", 2 + r), T.TP[:, r * M:(r + 1) * M], "upt", K("TP", r), K("ids", 2 + r))
            for c in (2, 0, 1):
                prefill(0, c)
            to16("fI", 0, 64, 0, 0, K("fI", 0))
            cp("wid16", "wid")
            to16("fI", 64, 128, 1, 0, K("fI", 1))
            for c, (a, b) in enumerate(CH):
                s_of("v", a, a + 32)
                s_of("s", a + 32, b)
                if c == 0:
                    to16("fI", 128, M, 2, 0, K("fI", 2))
                conv("E01", [("OC", 16 * a)], 64, 3 + c, 0, K("OC", a, a + 32))
            keys, keyk, tabs, tabk = "D1", K3("D1"), "ids", IDK
            marks, markk = "OB", [K("OB", 0), K("OB", 64), K("OB", 128, 144)]
        else:
            arrive("landK", prv, "ar_k")
            arrive("landT", nxt, "ar_t1")
            claim("OC", "y")
            for r in range(2):
                rows_up("y", "OC", 4 + r, "landU", r, "upu1")
            for c, (a, b) in enumerate(CH):
                conv("E45", [("OC", 16 * a)], 64, c, 0, whole("OC"))
            claim("OB", "vs")
            for q, a, b in (("v", 0, 96), ("s", 96, M)):
                gather(q, "OB", "P1", V, "landT", 0, a, b, whole("P1") + K("landT"), K("OB", a))
            for q in "vs":
                before(q, [], SLK)

            def tables(q, a, b):
                gather(q, "QW", "K1", V, "landK", 0, a, b, whole("K1") + K("landK") + K("cf", 17, 18), K("QW", a),
                       bias=cf(18), scale=cf(17))

            tables("v", 0, 40)
            tables("s", 64, 144)
            for c in range(3):
                to16("uI", 64 * c, 64 * c + 64, c, 0, K("uI", c))
            tables("v", 40, 64)
            for c, (a, b) in enumerate(CH):
                for q, a1 in (("v", a), ("s", a + 32)):
                    gather(q, "ids", "OB", V, "uI", 0, a1, a1 + 32, whole("OB") + K("uI", c), K("ids", "y%d" % a1))
                conv("E23", [("ids", 16 * a)], 64, 3 + c, 0, K("ids", "y%d" % a, "y%d" % (a + 32)))
            tables("v", 144, 168)
            tables("s", 168, M)
            keys, keyk, tabs, tabk = "QW", whole("QW"), "QW", whole("QW")
            marks, markk = "ids", [K("ids", "y%d" % a, "y%d" % (a + 32)) for a, b in CH]
            claim("K0", "v")
        sb = 3
        pend = []

        def flush():
            while pend:
                j1, c1 = pend.pop(0)
                to16("LL", M * j1 + 64 * c1, M * j1 + 64 * c1 + 64, c1, 0, K("LL", (j1, c1)))

        def first_keys(a, b, c, tag):
            vop(lambda: g.vector.tensor_tensor(T.K0[:, 16 * a:16 * b], T[keys][:, 0:V].indirect(T.sI[:, a:b]),
                                               W(marks, 16 * a, 16 * b), A.add),
                keyk + K("sI", c) + markk[c], K("K0", tag))

        claim("P0", "s")
        for c, (a, b) in enumerate(CH):
            if c == 0:
                to16("sI", 0, 64, sb, 0, K("sI", 0))
                first_keys(0, 32, 0, "a")
                to16("sI", 64, 128, sb + 1, 0, K("sI", 1))
                first_keys(32, 64, 0, 0)
                to16("sI", 128, M, sb + 2, 0, K("sI", 2))
            else:
                first_keys(a, b, c, c)
            gather("s", "P0", tabs, V, "sI", 0, a, b, tabk + K("sI", c), K("P0", c))
            conv("E23", [("P0", 16 * a)], 64, c, 0, K("P0", c))
            accumulate(0, c)
            flush()
            pend.append((0, c))
        if rnd == 0:
            prefill_all(1)
            op("g", lambda: g.iota(T.gg[:], [[1, 8], [0, 16]], 0, 0, **fl), [], K("gg"))

        side = []
        if rnd == 0:
            for r in range(2):
                dma("y", row("WM", 10 + r), row("P0", 2 + r), "crow0", K3("P0"), K("WM", "c%d" % r))
            for r in range(2):
                side.append((T.sp[:, r * M:(r + 1) * M], row("OC", r), "sdn" + R, whole("OC"), K("sp", r)))
            for r in range(2):
                side.append((row("WM", 6 + r), row("OC", r), "srow" + R, whole("OC"), K("WM", "s%d" % r)))
                for x, at in (("uv", 4), ("wp", 8), ("vp", 12)):
                    side.append((row("WM", at + r), T[x][:, r * M:(r + 1) * M], "srow" + R, K(x, r), K("WM", x[0] + str(r))))
        else:
            claim("K1", "v")
            claim("P1", "s")
            for r in range(2):
                dma("y", row("WM", 6 + r), row("P0", 6 + r), "crow1", K3("P0"), K("WM", "s%d" % r))
            for r in range(2):
                side.append((T.sp[:, (2 + r) * M:(3 + r) * M], row("WM", 6 + r), "sdn" + R, K("WM", "s%d" % r), K("sp", 2 + r)))
                side.append((row("WM", 4 + r), row("OC", 4 + r), "srow" + R, whole("OC"), K("WM", "u%d" % r)))
                side.append((T.uv[:, r * M:(r + 1) * M], row("OC", 4 + r), "uvd", whole("OC"), K("uv", r)))

        for j in range(STEPS):
            Pa, Pb = "P%d" % (j % 2), "P%d" % ((j + 1) % 2)
            Ka, Kb, D = "K%d" % (j % 2), "K%d" % ((j + 1) % 2), "D%d" % (j % 2)
            for c, (a, b) in enumerate(CH):
                lk = K("LL", (j, c))
                src = T[Ka][:, 0:V].indirect(T.LL[:, M * j + a:M * j + b])
                vop(lambda: g.vector.tensor_tensor(T[Kb][:, 16 * a:16 * b], src, T[D][:, 16 * a:16 * b], A.min),
                    K3(Ka) + lk + K(D, c), K(Kb, c))
                if j + 1 < STEPS:
                    accumulate(j + 1, c)
                if j + 2 < STEPS:
                    prefill(j + 2, c)
                if side and c < 2:
                    before("y", K(Kb, c), [])
                    dma("y", *side.pop(0))
                if (j, c) == (STEPS - 1, 0):
                    before("y", K(Kb, c), SLK)
                    claim("ids", "y")
                    claim("WU", "y")
                    for r in (12, 13, 14):
                        dma("y", row("SL", r), T.zb[:], "clr" + R, K("zb"), K("SL", r))
                flush()
                gather("s", Pb, Pa, V, "LL", M * j, a, b, K3(Pa) + lk, K(Pb, c))
                conv("E23", [(Pb, 16 * a)], 64, c, 0, K(Pb, c))
                pend.append((j + 1, c))
                if rnd == 0 and j in (1, 3):
                    conv("E%d" % (j // 2), [("WU", 16 * a)], 64, 6, a, K("WU", 0))
                if rnd == 0 and j in (2, 4) and c == 1:
                    act(T.HP[:, (j // 2 - 1) * M:j // 2 * M], ap(p(6, 0)), [p(6, 0)], K("HP", j // 2 - 1),
                        scale=(1.0 / M, 16.0)[j // 2 - 1])
        dma("y", T.KL[:], row("K1", KR), "kdn" + R, K3("K1"), K("KL"))
        for (dst, win, sem, lst, parts) in (
                ("K0", "K1", "adn", "AL", [("v", 0, 40), ("s", 64, 128), ("v", 40, 64), ("s", 128, 164), ("v", 164, M)]),
                ("D0", "K0", "bdn", "BL", [("v", 0, 96), ("s", 96, M)])):
            claim(dst, "vs")
            for q, a, b in parts:
                gather(q, dst, win, V, "LL", M * STEPS, a, b, whole(win) + chunks("LL", a, b, STEPS), K(dst, "at%d" % a),
                       bias=float(HOP))
                flush()
            dma("y", T[lst][:], row(dst, KR), sem + R, whole(dst), K(lst))

        if rnd == 0:
            act(T.sp[:, 2 * M:3 * M], T.sp[:, M:2 * M], K("sp", 1), K("sp", 2), scale=16.0)
            act(T.sp[:, 3 * M:4 * M], T.sp[:, 0:M], K("sp", 0), K("sp", 3), scale=1.0 / M)
            constants_leaders()
            constants_sums()
        sc = 2 if last else 0
        own, base, fix, rest, lead = p(7, 0), p(7, 1), p(2, 0), p(5, 0), p(2, 1)
        lin(p(4, 1), pieces("Ib", "sp", 2))
        tt(p(6, 0), "KL", "AL", A.min)
        lin(own, pieces("Ib", "wp", 0))
        lin(base, pieces("I2k", "wp", 0) + term("Ib", "fgR"))
        lin(fix, term("Ib", "tfx"))
        lin(p(4, 0), pieces("Ib", "uv", 0))
        sa("uf", p(4, 0), F.Copy)
        t_terms = term("Ip", "tf")
        if last:
            sa("f4", "tf", F.Identity, scale=1.0 / M, bias=-95.5 / M)
            t_terms = term("I16", "tf") + term("Ip", "f4")
        else:
            claim("K1", "y")
            for r in range(2):
                dma("y", row("K1", 6 + r), T.vf[:, r * M:(r + 1) * M], "vup", K("vf"), K("K1", "v%d" % r))
        before("y", [], K3("P0"))

        def record(r, src, x):
            dma("y", row("P0", r), T[src][:, x * M:(x + 1) * M], "rec" + R, K(src) if src == "pb" else K(src, x),
                K("P0", "r%d" % r))

        tt("i1", "BL", p(6, 0), A.min)

        ts("i2", "i1", 11, A.arith_shift_right, 4095, A.bitwise_and)
        ts("di", "i1", LAB - 1, A.bitwise_and)
        ts("i3", "i1", 1, A.bitwise_and)
        ts(p(6, 1), "i1", 0.0, A.is_lt)

        tt("fg", "i2", own, A.not_equal)
        dma("y", row("WM", 14), T.fg[:], "flg" + R, K("fg"), K("WM", "g"))
        tt("hd", fix, "di", A.subtract)
        tt("f2", "i1", base, A.is_lt)
        tt(lead, "i2", own, A.is_equal)

        tt(rest, "fg", "di", A.mult)
        ts("mm", "i3", 1.0, A.add)
        tt("f1", "hd", p(6, 1), A.subtract)

        vop(lambda: g.vector.tensor_tensor_scan(T.Zb[:, 1:M + 1], T.di[:], ap(rest), 0.0, A.add, A.subtract),
            [rest] + K("di"), K("Zb", 1))
        matmuls([(T.ps3[:, 0:2], T.TR[:], T.Zb[:, M - 1:M + 1])], K("TR") + K("Zb", 1), [p(3, 0)])
        high("r3", "f2", rest, A.mult)
        record(12, "r3", 0)
        tt(p(5, 1), "f2", rest, A.mult)
        tt("i1", "f1", rest, A.subtract)
        high("r2", "f1", rest, A.subtract)
        record(10, "r2", 0)
        tt("f3", "mm", lead, A.mult)

        low("r3", p(5, 1))
        record(13, "r3", 1)
        vop(lambda: g.vector.tensor_scalar(ap(p(6, 0)), T.Zb[:, 0:M], T.ps3[:, 1:2], float(V), A.subtract, A.add),
            K("Zb", 0, 1) + [p(3, 0)], [p(6, 0)])
        ts("i3", "i1", 1, A.bitwise_and)
        low("r2", "i1")
        record(11, "r2", 1)

        high("r1", p(6, 0), "f3", A.mult)
        record(8, "r1", 0)
        tt(p(5, 1), p(6, 0), "f3", A.mult)
        ts("pb", "i3", 1.0, A.add)
        record(14, "pb", 0)
        cp("sI", "i2")

        low("r1", p(5, 1))
        record(9, "r1", 1)
        ts("hd", "di", -float(HALF), A.add)
        if last:
            cp("i2", "f4")
        cp("sv16", p(4, 1))
        if last:
            ts("f4", "i2", -float(V - 1), A.mult)

        def load_rows(a, b):
            gather("s", "P1", "WM", V, "wid16", 0, a, b, WMK + K("wid16"), K("P1", "r%d" % a))

        claim("P1", "s")
        load_rows(0, 64)
        load_rows(64, 96)

        rb = p(6, 0)
        TOP = ODD + HALF

        def look_up(q, a, b):
            gather(q, "OB", "P0", V, "sI", 0, a, b, whole("P0") + K("sI"), K("OB", a))

        def slot_calls(qq, ra, cols):
            return [lambda: tt("f2", qq, "hd", A.is_ge, cols), lambda: tt("up", qq, "f2", A.mult, cols),
                    lambda: tt("f3", ra, "up", A.subtract, cols), lambda: ts("sl16", "f3", 0.25 - TOP, A.add, cols=cols)]

        def sort(a, b, rows):
            vop(lambda: g.vector.tensor_copy(T.SL[:, 0:SLW].indirect(T.sl16[:, a:b]), T.P1[:, 16 * a:16 * b]),
                chunks("sl16", a, b) + K("P1", *["r%d" % x for x in rows]), SLK)

        claim("OB", "vs")
        parts = [[0, 32], [64, 104], [128, 152]]
        for c, (a, b) in enumerate(CH):
            look_up("v", a, parts[c][1])
            look_up("s", parts[c][1], b)
            conv("Eq", [("OB", 16 * a)], 64, 3 if c else 5, a, K("OB", *parts[c]))
            for c1 in ([0], [], [1, 2])[c]:
                conv("Era", [("OB", 1024 * c1)], 64, 4 if c1 else 7, 64 * c1, K("OB", *parts[c1]), plus=term("In", "hd"))
        conv("Erb", [("OB", 0)], M, 6, 0, whole("OB"))
        load_rows(96, M)
        lead_calls, later = slot_calls(p(5, 0), p(7, 0), CH[0]), slot_calls(p(3, 0), p(4, 0), (64, M))
        lead_calls[0]()
        lead_calls[1]()
        lead_calls[2]()
        later[0]()
        lead_calls[3]()
        later[1]()
        sort(0, 64, [0])
        later[2]()
        later[3]()
        sort(64, M, [64, 96])
        if rnd == 0:
            before("y", K("sl16", 0), [])
            for c in range(0, V, PIECE):
                dma("y", T.xs[:, c:c + PIECE], T.x[:, c:c + PIECE], "ldx", [], K("xs", c))
            before("g", K("sl16", 0), [])
            send("HP", "landW", nxt, "rs_w", "ar_w", K("HP", 0, 1))
        act(T.zo[:, 0:64], ap(p(5, 0), 0, 64), [p(5, 0)], K("zo", 0), func=F.Copy)
        if rnd == 0:
            constants_votes()
        act(T.zo[:, 64:M], ap(p(3, 0), 64, M), [p(3, 0)], K("zo", 1, 2), func=F.Copy)
        sa("sg", "zo", F.Sign, scale=-1.0, bias=-HALF - 0.25)
        lin(p(0, 1), term("Ip", "zo") + term("In", "hd") + term("It", "sg"))
        sa("pb", "sg", F.Identity, scale=float(LAB), bias=float(LAB))
        lin(p(1, 1), t_terms + pieces("Im", "sp", sc) + 2 * term("Ib", "pb"))
        sa("zz", rb, F.Relu, bias=-float(HALF))
        sa("od", "sg", F.Identity, scale=0.5, bias=0.5)
        sa("mh", "zz", F.Identity, scale=-1.0, bias=float(HALF))
        sa("fg", p(0, 1), F.Sign, scale=-1.0, bias=-768.25)
        lin(p(2, 1), term("Ip", "mh") + term("I2k", "fg"))
        sa("tm", p(1, 1), F.Relu, bias=-4096.0)
        alike = term("Ip", "tm") + term("Im", "pb") + pieces("Ib", "sp", sc)
        if not last:
            lin(p(3, 1), alike + pieces("Im", "wp", 0))
        sa("mm", p(2, 1), F.Relu, scale=2.0, bias=-4096.0)
        lin(p(2, 0), term("Ip", "f3") + term("In", "mh") + term("Ip", "mm") + term("Iq", "sg"))
        if not last:
            sa("zz", p(3, 1), F.Abs)
            sa("tfx", "zz", F.Sigmoid, scale=-STEEP, bias=0.5 * STEEP)
            sa("fgR", "tfx", F.Identity, scale=-float(LVL))
            send("fgR", "landG", prv, "rs_g", "ar_g", K("fgR"))
            sa("f4", "tfx", F.Identity, scale=-2.0 * LVL / LAB)
        lin(p(7, 1), alike)
        lin(p(6, 1), term("Ip", "f3") + term("Ip", "up") + term("In", "zo") + term("Ip", "hd"))
        ts("hs16", p(2, 0), -float(TOP), A.add)

        if not last:
            arrive("landW", prv, "ar_w")
            arrive("landG", nxt, "ar_g")
            claim("P1", "y")
            for r in range(2):
                rows_up("y", "P1", 2 + r, "landW", r, "wup")
            dma("y", row("P1", KR), T.landG[:], "gup", K("landG"), K("P1", "g"))
            claim("D0", "y")
            prefill_all(0)
            prefill_all(1)

        conv("Ev", [("SL", HALF)], 96, 1, 0, SLK)
        conv("Ev", [("SL", 0)], 96, 0, 0, SLK)
        for c in range(3):
            matmuls([(T["ps%d" % (3 + c)][:], T.FB[:], T.SL[:, 512 * c:512 * c + 512])], K("FB") + SLK, pk(3 + c))

        def half(q, a, b):
            gather(q, "OC", "SL", SLW, "hs16", 0, a, b, SLK + K("hs16"), K("OC", "c%d" % a))

        def half_list(E, out, own, a, b, parts):
            conv(E, [("OC", 16 * a)], b - a, out[1], 256 * out[2] + a, K("OC", *["c%d" % x for x in parts]), plus=own)

        def cols(c):
            return slice(512 * c, 512 * c + 512)

        def gap(c):
            src = T.xs[:, 0:V].indirect(T.row16[:, 32 * c:32 * c + 32])
            vop(lambda: g.vector.tensor_tensor(T.xd[:, cols(c)], src, T.xa[:, cols(c)], A.subtract),
                XK + K("row16", 0) + K("xa", c), K("xd", c))
            act(T.xa[:, cols(c)], T.xd[:, cols(c)], K("xd", c), K("xa", c), func=F.Abs)

        def widest(c):
            init = 0.0 if c == 0 else T.xm[:, 512 * c - 1:512 * c]
            vop(lambda: g.vector.tensor_tensor_scan(T.xm[:, cols(c)], T["ps%d" % (3 + c)][:], T.xa[:, cols(c)], init,
                                                    A.mult, A.max),
                pk(3 + c) + K("xa", c) + (K("xm", c - 1) if c else []), K("xm", c))

        def against(q, a, b):
            src, dst = T.xm[:].indirect(T.es16[:, a:b]), T.OB[:, 16 * a:16 * b]
            rd = whole("xm") + K("es16") + K("thf") + K("cf", 5)
            if q == "s":
                act(dst, src, rd, K("OB", a), func=F.Sigmoid, scale=STEEP, bias=cf(5))
            else:
                vop(lambda: g.vector.tensor_scalar(dst, src, T.thf[:, 0:1], None, A.is_gt), rd, K("OB", a))

        own_u, own_s = pieces("Im", "uv", 0), pieces("Im", "sp", sc)
        claim("OC", "vs")
        half("s", 0, 56)
        half("v", 56, 84)
        ts("es16", p(6, 1), 0.25 - TOP - 1, A.add, float(HALF), A.min)
        to16("row16", 96, M, 1, 0, K("row16", 1))
        half("v", 84, 108)
        for c in range(3):
            act(T.xa[:, cols(c)], T.xs[:, 0:V].indirect(T.row16[:, 96 + 32 * c:128 + 32 * c]), XK + K("row16", 1), K("xa", c),
                func=F.Copy)
        to16("row16", 0, 96, 0, 0, K("row16", 0))
        half("v", 108, 128)
        early, late = (0, 128, [0, 56, 84, 108]), (128, M, [128, 144, 160])
        own_w = pieces("Im", "wp", 0)
        tn, hout, tout = "AL", "BL", "za"
        half_list("E45", p(6, 0), own_u, *early)
        half_list("E67", p(6, 1), own_s, *early)
        if not last:
            half_list("E89", p(7, 0), own_w, *early)
        gap(0)
        gap(1)
        gap(2)
        half("s", 160, M)
        widest(0)
        half("v", 128, 144)
        if not last:
            half_list("Ecw", p(0, 0), [], *early)
        widest(1)
        half("v", 144, 160)
        widest(2)
        half_list("E45", p(6, 0), own_u, *late)
        half_list("E67", p(6, 1), own_s, *late)
        if not last:
            half_list("E89", p(7, 0), own_w, *late)
        claim("OB", "vs")
        for a, b in CH:
            against("v", a, a + 32)
            against("s", a + 32, b)
            conv("Eh", [("OB", 16 * a)], 64, 3, a, K("OB", a, a + 32))
        claim("P0", "vs")
        for q in "v":
            before(q, [], pk(4))

        def mirror(q, a, b):
            gather(q, "P0", "OB", V, "sv16", 0, a, b, whole("OB") + K("sv16"), K("P0", a))

        def mirror_list(bk, a, parts):
            conv("Eh", [("P0", 16 * a)], 64, bk, a, K("P0", *parts))

        def new_t(out, bk, cols):
            b, x = p(4, 0, cols), p(4, 1, cols)
            return [lambda: ts(b, p(bk, 0), LIMIT, A.is_le, -2.0, A.mult, cols=cols),
                    lambda: tt(x, "f1", b, A.mult, cols), lambda: tt(out, "f3", x, A.add, cols)]

        first, second = (0, 128), (128, M)
        if not last:
            half_list("Ecw", p(0, 0), [], *late)
        mirror("s", 0, 32)
        mirror("v", 32, 64)
        mirror_list(2, 0, [0, 32])
        mirror("s", 64, 128)
        mirror_list(2, 64, [64])
        mirror("v", 128, 144)
        ts(tn, p(3, 0), LIMIT, A.is_le)
        ts("zz", p(3, 0), LIMIT, A.is_le, 0.5, A.subtract)
        mirror("s", 160, M)
        mirror("v", 144, 160)
        mirror_list(1, 128, [128, 144, 160])
        tt(p(5, 0), tn, p(6, 0), A.mult)
        tt("f2", tn, p(6, 1), A.mult)
        tt("f1", "zz", p(6, 1), A.mult)
        if not last:
            one, two = new_t("tf", 2, first), new_t("tf", 1, second)
            tt("mm", "od", p(0, 0), A.mult)
            tt(p(5, 1), "uf", p(5, 0), A.add)
            high("HP", "uf", p(5, 0), A.add)
            tt("f3", "f2", p(7, 1), A.add)
            tt(p(0, 1), "mm", p(7, 0), A.add)
            low("HP", p(5, 1))
            send("HP", "landU", nxt, "rs_h" + R, "ar_h" + R, K("HP", 0, 1))
            one[0]()
            tt("zz", tn, p(0, 1), A.mult)
            two[0]()
            lin(p(3, 1), pieces("Ib", "wp", 0) + term("t128", "zz"))
            one[1]()
            two[1]()
            one[2]()
            two[2]()
            cp("fI", p(3, 1))
            cp("ul", "tf")
            send("ul", "landT", prv, "rs_t1", "ar_t1", K("ul"))
            arrive("landU", prv, "ar_h0")
            send("fI", "landK", nxt, "rs_k", "ar_k", K("fI") + K("landU"))
            act(T.TP[:, 0:M], T.tf[:], K("tf"), K("TP", 0), func=F.Copy)
            act(T.TF[:, 0:M], T.TP[:, 0:M], K("TP", 0), K("TF", 0), func=F.Copy)
            tt("f2", "tf", "f4", A.add)
            vop(lambda: g.vector.tensor_tensor(T.TF[:, M:2 * M], T.tf[:], T.TP[:, 0:M], A.subtract),
                K("tf") + K("TP", 0), K("TF", 1))
            dma("s", row("K1", KR), T.f2[:], "upk1", K("f2"), K("K1", "k"))
            for r in range(2):
                dma("s", row("K1", 2 + r), T.TF[:, r * M:(r + 1) * M], "upk1", K("TF", r), K("K1", "t%d" % r))
        else:
            one, two = new_t(tout, 2, first), new_t(tout, 1, second)
            tt(hout, "uf", p(5, 0), A.add)
            send(hout, "landY", nxt, "rs_h" + R, "ar_h" + R, K(hout))
            tt("f3", "f2", p(7, 1), A.add)
            one[0]()
            two[0]()
            one[1]()
            two[1]()
            one[2]()
            two[2]()
            arrive("landY", prv, "ar_h" + R)
            dma("s", T.yt[:], T[tout][:], "outt", K(tout), K("yt", 0))
            dma("y", T.yu[sh:128, :], T.landY[0:128 - sh, :], "outu", K("landY"), K("yu", 0))
            dma("y", T.yu[0:sh, :], T.landY[128 - sh:128, :], "outu", K("landY"), K("yu", 1))

    for sem in total:
        need("g", (sem, None))
